import numpy as np
import ml_dtypes


def mxq(x, axis, fmt="e4m3"):
    dtype, down = {"e4m3": (ml_dtypes.float8_e4m3fn, 7), "e5m2": (ml_dtypes.float8_e5m2, 14)}[fmt]
    v = np.moveaxis(np.asarray(x, np.float32).astype(ml_dtypes.bfloat16).astype(np.float64), axis, -1)
    blocks = v.reshape(v.shape[:-1] + (-1, 32))
    amax = np.abs(blocks).max(-1, keepdims=True)
    byte = np.maximum(np.where(amax > 0, np.frexp(amax)[1] - 1 + 127, 0) - down, 1)
    scale = np.exp2(byte - 127.0)
    codes = (blocks / scale).astype(np.float32).astype(dtype).astype(np.float64)
    return np.moveaxis((codes * scale).reshape(v.shape), -1, axis)


WIDE = False


def mx_kscale(k):
    if not WIDE:
        return np.ones(k)
    levels = np.array([10, -10, 5, -5, 0])
    if k % 512:
        return np.exp2(np.random.permutation(np.resize(levels, k // 32))).repeat(32)
    a = np.empty((k // 512, 16))
    for p in range(k // 512):
        a[p, :8] = np.random.permutation(np.resize(levels, 8))
        for g in range(8):
            far = levels[np.abs(levels - a[p, g]) >= 10]
            a[p, g + 8] = far[np.random.randint(len(far))]
    return np.exp2(a.ravel()).repeat(32)


BF16 = ml_dtypes.bfloat16


def bf(x):
    return np.asarray(x, np.float32).astype(BF16)


def f64(x):
    return np.asarray(x).astype(np.float64)


E2M1 = np.array([0.0, 0.5, 1.0, 1.5, 2.0, 3.0, 4.0, 6.0, -0.0, -0.5, -1.0, -1.5, -2.0, -3.0, -4.0, -6.0])


def pack_weight(w, fmt):
    k, n = w.shape
    w = f64(bf(w)).reshape(k // 32, 32, n)
    amax = np.abs(w).max(1)
    if fmt == "e4m3":
        byte = np.frexp(amax)[1] - 1 + 127 - 7
    else:
        mant, ex = np.frexp(amax / 6.0)
        byte = np.where(mant > 0.5, ex, ex - 1) + 127
    byte = np.clip(np.where(amax > 0, byte, 1), 1, 254)
    scaled = (w * np.exp2(127.0 - byte)[:, None, :]).reshape(k, n).astype(np.float32)
    by_word = np.ascontiguousarray(scaled.reshape(k // 512, 128, 4, n).transpose(0, 1, 3, 2))
    if fmt == "e4m3":
        words = by_word.astype(ml_dtypes.float8_e4m3fn).view(np.uint8)
    else:
        c = by_word.astype(ml_dtypes.float4_e2m1fn).view(np.uint8) & 0xF
        words = c[..., 0::2] | (c[..., 1::2] << 4)
    return np.ascontiguousarray(words), np.ascontiguousarray(byte.astype(np.uint8).reshape(k // 512, 16, n))


def unpack_weight(words, scales, fmt):
    g, p, n, _ = words.shape
    if fmt == "e4m3":
        vals = np.ascontiguousarray(words).view(ml_dtypes.float8_e4m3fn).astype(np.float64)
    else:
        nib = np.empty((g, p, n, 4), np.uint8)
        nib[..., 0::2] = words & 0xF
        nib[..., 1::2] = words >> 4
        vals = E2M1[nib]
    vals = vals * np.repeat(np.exp2(scales.astype(np.float64) - 127.0), 8, axis=1)[..., None]
    return vals.transpose(0, 1, 3, 2).reshape(g * 512, n)
def pack4(w):
    words, scales = pack_weight(w, "e2m1")
    return words.reshape(words.shape[0], 128, -1), scales


def unpack4(words, scales):
    return unpack_weight(words.reshape(words.shape[0], 128, -1, 2), scales, "e2m1")


L, M, CD, CE, S, P = 4, 512, 512, 2048, 1024, 4096


def setup_inputs():
    s, u, t = mx_kscale(CD), mx_kscale(CE), mx_kscale(S)
    gd = np.random.standard_normal((M, CD)) + np.random.standard_normal((L, M, CD))
    ge = np.random.standard_normal((M, CE)) + np.random.standard_normal((L, M, CE))
    deep = np.random.standard_normal((CD, S)) / s[:, None] * t
    early = np.random.standard_normal((CE, S)) / u[:, None] * t
    up = np.random.standard_normal((S, P)) / np.sqrt(S) / t[:, None]
    early_words, early_scales = pack4(early)
    up_words, up_scales = pack4(up)
    return {"grad_deep": bf(gd / np.sqrt(CD) * s),
            "grad_early": bf(ge / np.sqrt(CE) * u),
            "deep": bf(deep),
            "early_words": early_words, "early_scales": early_scales,
            "up_words": up_words, "up_scales": up_scales}


def reference(grad_deep, grad_early, deep, early_words, early_scales, up_words, up_scales):
    a_deep = f64(grad_deep).mean(0)
    a_early = f64(grad_early).mean(0)
    z = ((mxq(a_deep, 1, "e4m3") @ mxq(f64(deep), 0, "e4m3"))
         + (mxq(a_early, 1, "e4m3") @ unpack4(early_words, early_scales)))
    cam = np.maximum(z, 0.0)
    return mxq(cam, 1, "e4m3") @ unpack4(up_words, up_scales)

@@ -1,0 +1,342 @@
+from contextlib import ExitStack
+
+import concourse.mybir as mybir
+from concourse.masks import make_identity
+
+F32 = mybir.dt.float32
+BF16 = mybir.dt.bfloat16
+I32 = mybir.dt.int32
+U32 = mybir.dt.uint32
+U8 = mybir.dt.uint8
+FP8X4 = mybir.dt.float8_e4m3fn_x4
+FP4X4 = mybir.dt.float4_e2m1fn_x4
+RELU = mybir.ActivationFunctionType.Relu
+COPY = mybir.ActivationFunctionType.Copy
+
+P = 128
+L, M, CD, CE, S, NPIX = 4, 512, 512, 2048, 1024, 4096
+K = 512
+JT = M // P
+GE = CE // K
+GS = S // K
+NT = NPIX // 512
+SCALAR_SUMS = ((0, 2), (0, 4), (1, 2), (1, 4))
+FLOPS = 2 * M * (CD + CE) * S + 2 * M * S * NPIX
+GROUPS = ((0,), (1, 2), (3, 4))
+
+
+def tile_two_layer_gradcam_s3_kernel(
+    tc, grad_deep, grad_early, deep, early_words, early_scales, up_words, up_scales, out
+):
+    nc = tc.nc
+    gd_view = grad_deep.rearrange("l (i j c) k -> c (l i) j k", j=4, c=JT)
+    ge_view = grad_early.rearrange("l (i j c) k -> c (l i) j k", j=4, c=JT)
+    out_view = out.rearrange("(q c) n -> c q n", c=JT)
+
+    with ExitStack() as ctx:
+        keep = ctx.enter_context(tc.tile_pool(name="keep", bufs=1))
+        grads = ctx.enter_context(tc.tile_pool(name="grads", bufs=3))
+        work = ctx.enter_context(tc.tile_pool(name="work", bufs=2))
+        outs = ctx.enter_context(tc.tile_pool(name="outs", bufs=4))
+        psum = ctx.enter_context(tc.psum_pool(name="psum", bufs=2))
+
+        ident = keep.tile([P, P], F32, align_bytes=64)
+        deep_raw = keep.tile([P, 4, S], BF16, align_bytes=64)
+        deep_grouped = keep.tile([P, S * 4], BF16, align_bytes=64)
+        deep_codes = keep.tile([P, S], U32, align_bytes=64)
+        deep_scales = keep.tile([P, S], U8, align_bytes=64)
+        ew = keep.tile([P, GE, 2 * S], U8, align_bytes=64)
+        es = keep.tile([P, GE, S], U8, align_bytes=64)
+        uw = [keep.tile([P, GS, NPIX], U8, name="uw%d" % h, align_bytes=64) for h in range(2)]
+        us = keep.tile([P, GS, NPIX], U8, align_bytes=64)
+        warm = keep.tile([P, 1], F32)
+        gd = [keep.tile([P, 4, CD], BF16, name="gd%d" % J, align_bytes=64) for J in range(JT)]
+        pick = keep.tile([P, 32], BF16, align_bytes=64)
+        ge = {}
+
+        ctx.enter_context(tc.manual_schedule())
+
+        def load_ge(J, half):
+            if half == 0:
+                ge[J] = [grads.tile([P, 4 * CE // 2], BF16, name="ge%d" % i, align_bytes=64) for i in range(2)]
+            t = ge[J][half]
+            dst = t[:].rearrange("p (j k) -> p j k", j=2)
+            nc.sync.dma_start(out=dst, in_=ge_view[J][:, 2 * half : 2 * half + 2, :])
+
+        def load_gd(J):
+            nc.sync.dma_start(out=gd[J][:], in_=gd_view[J])
+
+        def load_scales(plane, rows, groups):
+            for r in range(4):
+                nc.sync.dma_start(
+                    out=plane[r:P:32, :, :].bitcast(I32),
+                    in_=rows.rearrange("g (q r) n -> r q g n", r=4)[r].bitcast(I32),
+                )
+
+        nc.vector.memset(es[:].rearrange("p g n -> p (g n)").bitcast(I32), 0)
+        nc.vector.memset(us[:].rearrange("p g n -> p (g n)").bitcast(I32), 0)
+        nc.vector.memset(warm[:], 0.0)
+        nc.scalar.activation(out=warm[:], in_=warm[:], func=RELU)
+        make_identity(nc, ident[:])
+        for l in range(L):
+            nc.vector.tensor_copy(out=pick[32 * l : 32 * l + 32, :], in_=ident[32 * l : 32 * l + 32, 32 * l : 32 * l + 32])
+
+        def load_ew(h):
+            nc.sync.dma_start(
+                out=ew[:, 2 * h : 2 * h + 2, :].bitcast(I32),
+                in_=early_words[2 * h : 2 * h + 2].rearrange("g p n -> p g n").bitcast(I32),
+            )
+
+        def load_uw(h):
+            nc.sync.dma_start(
+                out=uw[h][:].bitcast(I32),
+                in_=up_words[:, :, h * NPIX : (h + 1) * NPIX].rearrange("g p n -> p g n").bitcast(I32),
+            )
+
+        half = S // 2
+
+        def deep_copies():
+            for h, eng in ((0, nc.vector.tensor_copy), (1, nc.scalar.copy)):
+                eng(
+                    out=deep_grouped[:, h * half * 4 : (h + 1) * half * 4].rearrange("p (w j) -> p w j", j=4),
+                    in_=deep_raw[:, :, h * half : (h + 1) * half].rearrange("p j w -> p w j"),
+                )
+
+        load_gd(0)
+        load_ge(0, 0)
+        nc.sync.dma_start(out=deep_raw[:], in_=deep.rearrange("(p j) w -> p j w", j=4))
+        load_ge(0, 1)
+        load_scales(es, early_scales, GE)
+        load_ew(0)
+        load_ew(1)
+        load_gd(1)
+        load_ge(1, 0)
+        load_ge(1, 1)
+        load_scales(us, up_scales, GS)
+        load_uw(0)
+        load_gd(2)
+        load_ge(2, 0)
+        load_uw(1)
+        load_ge(2, 1)
+        load_gd(3)
+
+        def quantize_deep(h):
+            nc.vector.quantize_mx(
+                out=deep_codes[:, h * half : (h + 1) * half].bitcast(FP8X4),
+                scales=deep_scales[:, h * half : (h + 1) * half],
+                in_=deep_grouped[:, h * half * 4 : (h + 1) * half * 4],
+            )
+
+        st = {}
+
+        def rows(J, jj, u, t):
+            if u == 0:
+                return gd[J][:, jj, t:CD:4]
+            base = (jj % 2) * CE + (u - 1) * K
+            return ge[J][jj // 2][:, base + t : base + K : 4]
+
+        def begin(J):
+            st[J] = {
+                "ag": work.tile([P, 5 * K], BF16, name="ag", align_bytes=64),
+                "ac": work.tile([P, 5 * P], U32, name="ac", align_bytes=64),
+                "as": work.tile([P, 5 * P], U8, name="a_s", align_bytes=64),
+                "n": 0,
+                "sum": {},
+            }
+
+        def sum_part(J, u, groups):
+            if u not in st[J]["sum"]:
+                st[J]["sum"][u] = psum.tile([P, K], F32, name="b", bufs=6)
+            acc = st[J]["sum"][u]
+            for t in range(4):
+                for jj in groups:
+                    nc.tensor.matmul(
+                        acc[:, t * P + 32 * jj : t * P + 32 * jj + 32], lhsT=rows(J, jj, u, t), rhs=pick[:], start=True, stop=True
+                    )
+
+        def empty_sum(J, u):
+            dst = st[J]["ag"][:, u * K : (u + 1) * K].rearrange("p (i j t) -> p i j t", j=4, t=4)
+            src = st[J]["sum"][u][:].rearrange("p (t j i) -> p i j t", t=4, j=4)
+            if (J, u) in SCALAR_SUMS:
+                nc.scalar.activation(out=dst, in_=src, func=COPY, scale=0.25)
+            else:
+                nc.vector.tensor_scalar(out=dst, in0=src, scalar1=0.25, scalar2=None, op0=mybir.AluOpType.mult)
+
+        def sum_cells(J, u):
+            sum_part(J, u, range(4))
+            empty_sum(J, u)
+
+        def quantize_a(J, g):
+            n = len(GROUPS[g])
+            u0 = GROUPS[g][0]
+            nc.vector.quantize_mx(
+                out=st[J]["ac"][:, u0 * P : (u0 + n) * P].bitcast(FP8X4),
+                scales=st[J]["as"][:, u0 * P : (u0 + n) * P],
+                in_=st[J]["ag"][:, u0 * K : (u0 + n) * K],
+            )
+
+        def stage1(J, units):
+            if units[0] == 0:
+                st[J]["z"] = [psum.tile([P, K], F32, name="z%d" % h, bufs=1) for h in range(2)]
+            for h in range(2):
+                for u in units:
+                    cols = slice(u * P, (u + 1) * P)
+                    if u == 0:
+                        rhs = deep_codes[:, h * K : (h + 1) * K].bitcast(FP8X4)
+                        rs = deep_scales[:, h * K : (h + 1) * K]
+                    else:
+                        rhs = ew[:, u - 1, h * 2 * K : (h + 1) * 2 * K].bitcast(FP4X4)
+                        rs = es[:, u - 1, h * K : (h + 1) * K]
+                    nc.tensor.matmul_mx(
+                        out=st[J]["z"][h][:],
+                        lhsT=st[J]["ac"][:, cols].bitcast(FP8X4),
+                        lhsT_scale=st[J]["as"][:, cols],
+                        rhs=rhs,
+                        rhs_scale=rs,
+                        start=(u == 0),
+                        stop=(u == 4),
+                    )
+
+        def relu(J):
+            st[J]["cam"] = work.tile([P, S], BF16, name="cam", align_bytes=64)
+            for h in range(2):
+                nc.scalar.activation(
+                    out=st[J]["cam"][:, h * K : (h + 1) * K].rearrange("m (u q e) -> m u q e", u=2, e=2),
+                    in_=st[J]["z"][h][:].rearrange("m (q u e) -> m u q e", u=2, e=2),
+                    func=RELU,
+                )
+
+        def cam_transposes(J):
+            tr = psum.tile([P, K], F32, name="b", bufs=6)
+            words = st[J]["cam"][:].bitcast(F32)
+            for i in range(4):
+                nc.tensor.transpose(tr[:, i * P : (i + 1) * P], words[:, i * P : (i + 1) * P], ident[:])
+            st[J]["ct"] = tr
+
+        def empty_cam(J):
+            st[J]["cg"] = work.tile([P, S], BF16, name="cg", align_bytes=64)
+            nc.scalar.copy(
+                out=st[J]["cg"][:].bitcast(F32).rearrange("p (c m v) -> p c m v", c=2, v=2),
+                in_=st[J]["ct"][:].rearrange("p (c v m) -> p c m v", c=2, v=2),
+            )
+
+        def quantize_cam(J):
+            st[J]["cc"] = work.tile([P, GS * P], U32, name="cc", align_bytes=64)
+            st[J]["cs"] = work.tile([P, GS * P], U8, name="cs", align_bytes=64)
+            nc.vector.quantize_mx(out=st[J]["cc"][:].bitcast(FP8X4), scales=st[J]["cs"][:], in_=st[J]["cg"][:])
+
+        def stage2(J, n):
+            o = psum.tile([P, 512], F32, name="b", bufs=6)
+            for g in range(GS):
+                nc.tensor.matmul_mx(
+                    out=o[:],
+                    lhsT=st[J]["cc"][:, g * P : (g + 1) * P].bitcast(FP8X4),
+                    lhsT_scale=st[J]["cs"][:, g * P : (g + 1) * P],
+                    rhs=uw[n // 4][:, g, (n % 4) * 1024 : (n % 4 + 1) * 1024].bitcast(FP4X4),
+                    rhs_scale=us[:, g, n * 512 : (n + 1) * 512],
+                    start=(g == 0),
+                    stop=(g == GS - 1),
+                )
+            if n % 4 == 0:
+                st[J]["o"] = outs.tile([P, 2048], F32, name="ot")
+            dst = st[J]["o"][:, (n % 4) * 512 : (n % 4 + 1) * 512]
+            if (J == JT - 1 or (J == JT - 2 and n > 4)) and n % 2 == 1:
+                nc.vector.tensor_copy(out=dst, in_=o[:])
+            else:
+                nc.scalar.copy(out=dst, in_=o[:])
+            w = 4 if J < 2 else 2 if J < 3 or n < 6 else 1
+            if n % w == w - 1:
+                lo = (n % 4 + 1 - w) * 512
+                nc.sync.dma_start(
+                    out=out_view[J][:, (n + 1 - w) * 512 : (n + 1) * 512], in_=st[J]["o"][:, lo : lo + w * 512]
+                )
+
+        def back(J, count):
+            for n in range(st[J]["n"], st[J]["n"] + count):
+                stage2(J, n)
+            st[J]["n"] += count
+
+        def halves(J, us_):
+            for u in us_:
+                sum_part(J, u, (0, 1))
+
+        def finish(J, us_):
+            for u in us_:
+                sum_part(J, u, (2, 3))
+                empty_sum(J, u)
+
+        begin(0)
+        sum_cells(0, 0)
+        deep_copies()
+        quantize_a(0, 0)
+        quantize_deep(0)
+        halves(0, (1, 2, 3, 4))
+        finish(0, (1, 2))
+        quantize_deep(1)
+        quantize_a(0, 1)
+        finish(0, (3, 4))
+        stage1(0, (0,))
+        quantize_a(0, 2)
+        stage1(0, (1, 2))
+        stage1(0, (3, 4))
+        relu(0)
+        load_ge(3, 0)
+        load_ge(3, 1)
+        begin(1)
+        sum_cells(1, 0)
+        quantize_a(1, 0)
+        cam_transposes(0)
+        empty_cam(0)
+        quantize_cam(0)
+        halves(1, (1, 2, 3, 4))
+        finish(1, (1, 2))
+        quantize_a(1, 1)
+        finish(1, (3, 4))
+        quantize_a(1, 2)
+        stage1(1, (0,))
+        stage1(1, (1, 2))
+        stage1(1, (3, 4))
+        relu(1)
+        back(0, 2)
+        begin(2)
+        sum_cells(2, 0)
+        quantize_a(2, 0)
+        cam_transposes(1)
+        empty_cam(1)
+        quantize_cam(1)
+        back(0, 2)
+        stage1(2, (0,))
+        back(1, 4)
+        back(0, 4)
+        for u in (1, 2, 3, 4):
+            sum_cells(2, u)
+            if u % 2 == 0:
+                quantize_a(2, u // 2)
+        begin(3)
+        sum_cells(3, 0)
+        quantize_a(3, 0)
+        back(1, 2)
+        stage1(2, (1, 2))
+        stage1(2, (3, 4))
+        relu(2)
+        sum_cells(3, 1)
+        sum_cells(3, 2)
+        back(1, 2)
+        cam_transposes(2)
+        empty_cam(2)
+        quantize_a(3, 1)
+        quantize_cam(2)
+        sum_cells(3, 3)
+        sum_cells(3, 4)
+        quantize_a(3, 2)
+        stage1(3, (0,))
+        stage1(3, (1, 2))
+        back(2, 2)
+        stage1(3, (3, 4))
+        relu(3)
+        back(2, 4)
+        cam_transposes(3)
+        empty_cam(3)
+        quantize_cam(3)
+        back(2, 2)
+        back(3, 8)

@@ -16,327 +16,275 @@ COPY = mybir.ActivationFunctionType.Copy
 P = 128
 L, M, CD, CE, S, NPIX = 4, 512, 512, 2048, 1024, 4096
 K = 512
-JT = M // P
+BANDS = M // P
 GE = CE // K
 GS = S // K
-NT = NPIX // 512
-SCALAR_SUMS = ((0, 2), (0, 4), (1, 2), (1, 4))
+STRIPS = NPIX // K
+UNITS = 1 + GE
+PIECES = (1, 2, 2, 2)
 FLOPS = 2 * M * (CD + CE) * S + 2 * M * S * NPIX
-GROUPS = ((0,), (1, 2), (3, 4))
 
 
 def tile_two_layer_gradcam_s3_kernel(
     tc, grad_deep, grad_early, deep, early_words, early_scales, up_words, up_scales, out
 ):
     nc = tc.nc
-    gd_view = grad_deep.rearrange("l (i j c) k -> c (l i) j k", j=4, c=JT)
-    ge_view = grad_early.rearrange("l (i j c) k -> c (l i) j k", j=4, c=JT)
-    out_view = out.rearrange("(q c) n -> c q n", c=JT)
+    gd_view = grad_deep.rearrange("l (i j c b) k -> c (l i) j (b k)", j=4, c=BANDS // 2, b=2)
+    ge_view = grad_early.rearrange("l (i j b) k -> b (l i) j k", j=4, b=BANDS)
+    out_view = out.rearrange("(q b) n -> b q n", b=BANDS)
 
     with ExitStack() as ctx:
         keep = ctx.enter_context(tc.tile_pool(name="keep", bufs=1))
-        grads = ctx.enter_context(tc.tile_pool(name="grads", bufs=3))
         work = ctx.enter_context(tc.tile_pool(name="work", bufs=2))
-        outs = ctx.enter_context(tc.tile_pool(name="outs", bufs=4))
-        psum = ctx.enter_context(tc.psum_pool(name="psum", bufs=2))
+        outs = ctx.enter_context(tc.tile_pool(name="outs", bufs=7))
+        psum = ctx.enter_context(tc.psum_pool(name="psum", bufs=1))
 
         ident = keep.tile([P, P], F32, align_bytes=64)
+        pick = keep.tile([P, 32], BF16, align_bytes=64)
         deep_raw = keep.tile([P, 4, S], BF16, align_bytes=64)
         deep_grouped = keep.tile([P, S * 4], BF16, align_bytes=64)
         deep_codes = keep.tile([P, S], U32, align_bytes=64)
         deep_scales = keep.tile([P, S], U8, align_bytes=64)
-        ew = keep.tile([P, GE, 2 * S], U8, align_bytes=64)
+        ew = [keep.tile([P, 2, 2 * S], U8, name="ew%d" % h, align_bytes=64) for h in range(2)]
         es = keep.tile([P, GE, S], U8, align_bytes=64)
-        uw = [keep.tile([P, GS, NPIX], U8, name="uw%d" % h, align_bytes=64) for h in range(2)]
-        us = keep.tile([P, GS, NPIX], U8, align_bytes=64)
-        warm = keep.tile([P, 1], F32)
-        gd = [keep.tile([P, 4, CD], BF16, name="gd%d" % J, align_bytes=64) for J in range(JT)]
-        pick = keep.tile([P, 32], BF16, align_bytes=64)
+        uw = [keep.tile([P, GS, NPIX // 2], U8, name="uw%d" % q, align_bytes=64) for q in range(4)]
+        us = [keep.tile([P, GS, NPIX // 2], U8, name="us%d" % h, align_bytes=64) for h in range(2)]
+        gd = [keep.tile([P, 4, 2 * CD], BF16, name="gd%d" % c, align_bytes=64) for c in range(BANDS // 2)]
         ge = {}
+        for b in range(BANDS):
+            for h in range(PIECES[b]):
+                ge[b, h] = keep.tile([P, 4, CE // PIECES[b]], BF16, name="ge%d_%d" % (b, h), align_bytes=64)
 
         ctx.enter_context(tc.manual_schedule())
 
-        def load_ge(J, half):
-            if half == 0:
-                ge[J] = [grads.tile([P, 4 * CE // 2], BF16, name="ge%d" % i, align_bytes=64) for i in range(2)]
-            t = ge[J][half]
-            dst = t[:].rearrange("p (j k) -> p j k", j=2)
-            nc.sync.dma_start(out=dst, in_=ge_view[J][:, 2 * half : 2 * half + 2, :])
+        def load_gd(c):
+            nc.sync.dma_start(out=gd[c][:], in_=gd_view[c])
 
-        def load_gd(J):
-            nc.sync.dma_start(out=gd[J][:], in_=gd_view[J])
+        def load_ge(b):
+            width = CE // PIECES[b]
+            for h in range(PIECES[b]):
+                nc.sync.dma_start(out=ge[b, h][:], in_=ge_view[b][:, :, h * width : (h + 1) * width])
 
-        def load_scales(plane, rows, groups):
+        def load_scales(plane, rows):
             for r in range(4):
                 nc.sync.dma_start(
                     out=plane[r:P:32, :, :].bitcast(I32),
                     in_=rows.rearrange("g (q r) n -> r q g n", r=4)[r].bitcast(I32),
                 )
 
-        nc.vector.memset(es[:].rearrange("p g n -> p (g n)").bitcast(I32), 0)
-        nc.vector.memset(us[:].rearrange("p g n -> p (g n)").bitcast(I32), 0)
-        nc.vector.memset(warm[:], 0.0)
-        nc.scalar.activation(out=warm[:], in_=warm[:], func=RELU)
-        make_identity(nc, ident[:])
-        for l in range(L):
-            nc.vector.tensor_copy(out=pick[32 * l : 32 * l + 32, :], in_=ident[32 * l : 32 * l + 32, 32 * l : 32 * l + 32])
-
         def load_ew(h):
             nc.sync.dma_start(
-                out=ew[:, 2 * h : 2 * h + 2, :].bitcast(I32),
+                out=ew[h][:].bitcast(I32),
                 in_=early_words[2 * h : 2 * h + 2].rearrange("g p n -> p g n").bitcast(I32),
             )
 
-        def load_uw(h):
+        def load_uw(q):
             nc.sync.dma_start(
-                out=uw[h][:].bitcast(I32),
-                in_=up_words[:, :, h * NPIX : (h + 1) * NPIX].rearrange("g p n -> p g n").bitcast(I32),
+                out=uw[q][:].bitcast(I32),
+                in_=up_words[:, :, q * NPIX // 2 : (q + 1) * NPIX // 2].rearrange("g p n -> p g n").bitcast(I32),
             )
 
-        half = S // 2
+        def load_us(h):
+            load_scales(us[h], up_scales[:, :, h * NPIX // 2 : (h + 1) * NPIX // 2])
 
-        def deep_copies():
-            for h, eng in ((0, nc.vector.tensor_copy), (1, nc.scalar.copy)):
-                eng(
-                    out=deep_grouped[:, h * half * 4 : (h + 1) * half * 4].rearrange("p (w j) -> p w j", j=4),
-                    in_=deep_raw[:, :, h * half : (h + 1) * half].rearrange("p j w -> p w j"),
-                )
+        def load_deep():
+            nc.sync.dma_start(out=deep_raw[:], in_=deep.rearrange("(p j) w -> p j w", j=4))
+
+        for plane in [es] + us:
+            nc.vector.memset(plane[:].rearrange("p g n -> p (g n)").bitcast(I32), 0)
+        make_identity(nc, ident[:])
+        for l in range(L):
+            rows = slice(32 * l, 32 * l + 32)
+            nc.scalar.activation(out=pick[rows, :], in_=ident[rows, rows], func=COPY, scale=1.0 / L)
 
         load_gd(0)
-        load_ge(0, 0)
-        nc.sync.dma_start(out=deep_raw[:], in_=deep.rearrange("(p j) w -> p j w", j=4))
-        load_ge(0, 1)
-        load_scales(es, early_scales, GE)
+        load_deep()
+        load_ge(0)
+        load_scales(es, early_scales)
         load_ew(0)
         load_ew(1)
+        load_ge(1)
+        for h in range(2):
+            load_us(h)
+            load_uw(2 * h)
+            load_uw(2 * h + 1)
         load_gd(1)
-        load_ge(1, 0)
-        load_ge(1, 1)
-        load_scales(us, up_scales, GS)
-        load_uw(0)
-        load_gd(2)
-        load_ge(2, 0)
-        load_uw(1)
-        load_ge(2, 1)
-        load_gd(3)
+        load_ge(2)
+        load_ge(3)
+
+        def group_deep(h, copy):
+            copy(
+                out=deep_grouped[:, h * K * 4 : (h + 1) * K * 4].rearrange("p (w j) -> p w j", j=4),
+                in_=deep_raw[:, :, h * K : (h + 1) * K].rearrange("p j w -> p w j"),
+            )
 
         def quantize_deep(h):
             nc.vector.quantize_mx(
-                out=deep_codes[:, h * half : (h + 1) * half].bitcast(FP8X4),
-                scales=deep_scales[:, h * half : (h + 1) * half],
-                in_=deep_grouped[:, h * half * 4 : (h + 1) * half * 4],
+                out=deep_codes[:, h * K : (h + 1) * K].bitcast(FP8X4),
+                scales=deep_scales[:, h * K : (h + 1) * K],
+                in_=deep_grouped[:, h * K * 4 : (h + 1) * K * 4],
             )
 
         st = {}
 
-        def rows(J, jj, u, t):
-            if u == 0:
-                return gd[J][:, jj, t:CD:4]
-            base = (jj % 2) * CE + (u - 1) * K
-            return ge[J][jj // 2][:, base + t : base + K : 4]
+        def bank():
+            return psum.tile([P, K], F32, name="bank", bufs=6)
 
-        def begin(J):
-            st[J] = {
-                "ag": work.tile([P, 5 * K], BF16, name="ag", align_bytes=64),
-                "ac": work.tile([P, 5 * P], U32, name="ac", align_bytes=64),
-                "as": work.tile([P, 5 * P], U8, name="a_s", align_bytes=64),
-                "n": 0,
-                "sum": {},
+        def begin(b):
+            st[b] = {
+                "means": work.tile([P, UNITS * K], BF16, name="means", align_bytes=64),
+                "codes": work.tile([P, UNITS * P], U32, name="codes", align_bytes=64),
+                "scales": work.tile([P, UNITS * P], U8, name="scales", align_bytes=64),
             }
 
-        def sum_part(J, u, groups):
-            if u not in st[J]["sum"]:
-                st[J]["sum"][u] = psum.tile([P, K], F32, name="b", bufs=6)
-            acc = st[J]["sum"][u]
+        def mean(b, u, on_scalar):
+            acc = bank()
             for t in range(4):
-                for jj in groups:
-                    nc.tensor.matmul(
-                        acc[:, t * P + 32 * jj : t * P + 32 * jj + 32], lhsT=rows(J, jj, u, t), rhs=pick[:], start=True, stop=True
-                    )
+                for j in range(4):
+                    if u == 0:
+                        cols = gd[b // 2][:, j, b % 2 * CD + t : (b % 2 + 1) * CD : 4]
+                    else:
+                        h, base = divmod((u - 1) * K, CE // PIECES[b])
+                        cols = ge[b, h][:, j, base + t : base + K : 4]
+                    nc.tensor.matmul(acc[:, t * P + 32 * j : t * P + 32 * j + 32], lhsT=cols, rhs=pick[:], start=True, stop=True)
+            dst = st[b]["means"][:, u * K : (u + 1) * K].rearrange("p (i j t) -> p i j t", j=4, t=4)
+            src = acc[:].rearrange("p (t j i) -> p i j t", t=4, j=4)
+            copy = nc.scalar.copy if on_scalar else nc.vector.tensor_copy
+            copy(out=dst, in_=src)
 
-        def empty_sum(J, u):
-            dst = st[J]["ag"][:, u * K : (u + 1) * K].rearrange("p (i j t) -> p i j t", j=4, t=4)
-            src = st[J]["sum"][u][:].rearrange("p (t j i) -> p i j t", t=4, j=4)
-            if (J, u) in SCALAR_SUMS:
-                nc.scalar.activation(out=dst, in_=src, func=COPY, scale=0.25)
-            else:
-                nc.vector.tensor_scalar(out=dst, in0=src, scalar1=0.25, scalar2=None, op0=mybir.AluOpType.mult)
-
-        def sum_cells(J, u):
-            sum_part(J, u, range(4))
-            empty_sum(J, u)
-
-        def quantize_a(J, g):
-            n = len(GROUPS[g])
-            u0 = GROUPS[g][0]
+        def quantize_means(b, u0, n):
             nc.vector.quantize_mx(
-                out=st[J]["ac"][:, u0 * P : (u0 + n) * P].bitcast(FP8X4),
-                scales=st[J]["as"][:, u0 * P : (u0 + n) * P],
-                in_=st[J]["ag"][:, u0 * K : (u0 + n) * K],
+                out=st[b]["codes"][:, u0 * P : (u0 + n) * P].bitcast(FP8X4),
+                scales=st[b]["scales"][:, u0 * P : (u0 + n) * P],
+                in_=st[b]["means"][:, u0 * K : (u0 + n) * K],
             )
 
-        def stage1(J, units):
-            if units[0] == 0:
-                st[J]["z"] = [psum.tile([P, K], F32, name="z%d" % h, bufs=1) for h in range(2)]
-            for h in range(2):
+        def stage1(b, units, first, last):
+            if first in units:
+                st[b]["z"] = [psum.tile([P, K], F32, name="z%d" % h) for h in range(GS)]
+            for h in range(GS):
                 for u in units:
                     cols = slice(u * P, (u + 1) * P)
                     if u == 0:
                         rhs = deep_codes[:, h * K : (h + 1) * K].bitcast(FP8X4)
-                        rs = deep_scales[:, h * K : (h + 1) * K]
+                        rhs_scale = deep_scales[:, h * K : (h + 1) * K]
                     else:
-                        rhs = ew[:, u - 1, h * 2 * K : (h + 1) * 2 * K].bitcast(FP4X4)
-                        rs = es[:, u - 1, h * K : (h + 1) * K]
+                        rhs = ew[(u - 1) // 2][:, (u - 1) % 2, h * 2 * K : (h + 1) * 2 * K].bitcast(FP4X4)
+                        rhs_scale = es[:, u - 1, h * K : (h + 1) * K]
                     nc.tensor.matmul_mx(
-                        out=st[J]["z"][h][:],
-                        lhsT=st[J]["ac"][:, cols].bitcast(FP8X4),
-                        lhsT_scale=st[J]["as"][:, cols],
+                        out=st[b]["z"][h][:],
+                        lhsT=st[b]["codes"][:, cols].bitcast(FP8X4),
+                        lhsT_scale=st[b]["scales"][:, cols],
                         rhs=rhs,
-                        rhs_scale=rs,
-                        start=(u == 0),
-                        stop=(u == 4),
+                        rhs_scale=rhs_scale,
+                        start=(u == first),
+                        stop=(u == last),
                     )
 
-        def relu(J):
-            st[J]["cam"] = work.tile([P, S], BF16, name="cam", align_bytes=64)
-            for h in range(2):
+        def relu(b):
+            st[b]["cam"] = work.tile([P, S], BF16, name="cam", align_bytes=64)
+            for h in range(GS):
                 nc.scalar.activation(
-                    out=st[J]["cam"][:, h * K : (h + 1) * K].rearrange("m (u q e) -> m u q e", u=2, e=2),
-                    in_=st[J]["z"][h][:].rearrange("m (q u e) -> m u q e", u=2, e=2),
+                    out=st[b]["cam"][:, h * K : (h + 1) * K].rearrange("m (u q e) -> m u q e", u=2, e=2),
+                    in_=st[b]["z"][h][:].rearrange("m (q u e) -> m u q e", u=2, e=2),
                     func=RELU,
                 )
 
-        def cam_transposes(J):
-            tr = psum.tile([P, K], F32, name="b", bufs=6)
-            words = st[J]["cam"][:].bitcast(F32)
+        def turn_cam(b, copy):
+            turned = bank()
+            words = st[b]["cam"][:].bitcast(F32)
             for i in range(4):
-                nc.tensor.transpose(tr[:, i * P : (i + 1) * P], words[:, i * P : (i + 1) * P], ident[:])
-            st[J]["ct"] = tr
-
-        def empty_cam(J):
-            st[J]["cg"] = work.tile([P, S], BF16, name="cg", align_bytes=64)
-            nc.scalar.copy(
-                out=st[J]["cg"][:].bitcast(F32).rearrange("p (c m v) -> p c m v", c=2, v=2),
-                in_=st[J]["ct"][:].rearrange("p (c v m) -> p c m v", c=2, v=2),
+                nc.tensor.transpose(turned[:, i * P : (i + 1) * P], words[:, i * P : (i + 1) * P], ident[:])
+            grouped = work.tile([P, S], BF16, name="grouped", align_bytes=64)
+            copy(
+                out=grouped[:].bitcast(F32).rearrange("p (g m v) -> p g m v", g=GS, v=2),
+                in_=turned[:].rearrange("p (g v m) -> p g m v", g=GS, v=2),
             )
+            st[b]["grouped"] = grouped
 
-        def quantize_cam(J):
-            st[J]["cc"] = work.tile([P, GS * P], U32, name="cc", align_bytes=64)
-            st[J]["cs"] = work.tile([P, GS * P], U8, name="cs", align_bytes=64)
-            nc.vector.quantize_mx(out=st[J]["cc"][:].bitcast(FP8X4), scales=st[J]["cs"][:], in_=st[J]["cg"][:])
+        def quantize_cam(b):
+            st[b]["cam_codes"] = work.tile([P, GS * P], U32, name="cam_codes", align_bytes=64)
+            st[b]["cam_scales"] = work.tile([P, GS * P], U8, name="cam_scales", align_bytes=64)
+            nc.vector.quantize_mx(out=st[b]["cam_codes"][:].bitcast(FP8X4), scales=st[b]["cam_scales"][:], in_=st[b]["grouped"][:])
 
-        def stage2(J, n):
-            o = psum.tile([P, 512], F32, name="b", bufs=6)
-            for g in range(GS):
-                nc.tensor.matmul_mx(
-                    out=o[:],
-                    lhsT=st[J]["cc"][:, g * P : (g + 1) * P].bitcast(FP8X4),
-                    lhsT_scale=st[J]["cs"][:, g * P : (g + 1) * P],
-                    rhs=uw[n // 4][:, g, (n % 4) * 1024 : (n % 4 + 1) * 1024].bitcast(FP4X4),
-                    rhs_scale=us[:, g, n * 512 : (n + 1) * 512],
-                    start=(g == 0),
-                    stop=(g == GS - 1),
-                )
-            if n % 4 == 0:
-                st[J]["o"] = outs.tile([P, 2048], F32, name="ot")
-            dst = st[J]["o"][:, (n % 4) * 512 : (n % 4 + 1) * 512]
-            if (J == JT - 1 or (J == JT - 2 and n > 4)) and n % 2 == 1:
-                nc.vector.tensor_copy(out=dst, in_=o[:])
-            else:
-                nc.scalar.copy(out=dst, in_=o[:])
-            w = 4 if J < 2 else 2 if J < 3 or n < 6 else 1
-            if n % w == w - 1:
-                lo = (n % 4 + 1 - w) * 512
-                nc.sync.dma_start(
-                    out=out_view[J][:, (n + 1 - w) * 512 : (n + 1) * 512], in_=st[J]["o"][:, lo : lo + w * 512]
-                )
+        def stage2(b, strips, shared=False, width=4):
+            for n in strips:
+                acc = bank()
+                for g in range(GS):
+                    nc.tensor.matmul_mx(
+                        out=acc[:],
+                        lhsT=st[b]["cam_codes"][:, g * P : (g + 1) * P].bitcast(FP8X4),
+                        lhsT_scale=st[b]["cam_scales"][:, g * P : (g + 1) * P],
+                        rhs=uw[n // 2][:, g, (n % 2) * 2 * K : (n % 2 + 1) * 2 * K].bitcast(FP4X4),
+                        rhs_scale=us[n // 4][:, g, (n % 4) * K : (n % 4 + 1) * K],
+                        start=(g == 0),
+                        stop=(g == GS - 1),
+                    )
+                if n % 4 == 0:
+                    st[b]["staged", n // 4] = outs.tile([P, 4 * K], F32, name="staged")
+                staged = st[b]["staged", n // 4]
+                copy = nc.vector.tensor_copy if shared and n % 2 == 1 else nc.scalar.copy
+                copy(out=staged[:, (n % 4) * K : (n % 4 + 1) * K], in_=acc[:])
+                if n % width == width - 1:
+                    lo = n + 1 - width
+                    nc.sync.dma_start(out=out_view[b][:, lo * K : (n + 1) * K], in_=staged[:, (lo % 4) * K : (n % 4 + 1) * K])
 
-        def back(J, count):
-            for n in range(st[J]["n"], st[J]["n"] + count):
-                stage2(J, n)
-            st[J]["n"] += count
-
-        def halves(J, us_):
-            for u in us_:
-                sum_part(J, u, (0, 1))
-
-        def finish(J, us_):
-            for u in us_:
-                sum_part(J, u, (2, 3))
-                empty_sum(J, u)
+        def means(b, units):
+            for u in units:
+                mean(b, u, u == units[-1])
+            quantize_means(b, units[0], len(units))
 
         begin(0)
-        sum_cells(0, 0)
-        deep_copies()
-        quantize_a(0, 0)
+        means(0, (0,))
+        group_deep(0, nc.vector.tensor_copy)
+        group_deep(1, nc.scalar.copy)
         quantize_deep(0)
-        halves(0, (1, 2, 3, 4))
-        finish(0, (1, 2))
         quantize_deep(1)
-        quantize_a(0, 1)
-        finish(0, (3, 4))
-        stage1(0, (0,))
-        quantize_a(0, 2)
-        stage1(0, (1, 2))
-        stage1(0, (3, 4))
-        relu(0)
-        load_ge(3, 0)
-        load_ge(3, 1)
         begin(1)
-        sum_cells(1, 0)
-        quantize_a(1, 0)
-        cam_transposes(0)
-        empty_cam(0)
+        means(1, (0,))
+        stage1(0, (0,), 0, 4)
+        means(0, (1, 2))
+        means(0, (3, 4))
+        stage1(0, (1, 2), 0, 4)
+        stage1(0, (3, 4), 0, 4)
+        relu(0)
+        turn_cam(0, nc.scalar.copy)
         quantize_cam(0)
-        halves(1, (1, 2, 3, 4))
-        finish(1, (1, 2))
-        quantize_a(1, 1)
-        finish(1, (3, 4))
-        quantize_a(1, 2)
-        stage1(1, (0,))
-        stage1(1, (1, 2))
-        stage1(1, (3, 4))
+        means(1, (1, 2))
+        stage1(1, (0,), 0, 4)
+        means(1, (3, 4))
+        stage1(1, (1, 2), 0, 4)
+        stage1(1, (3, 4), 0, 4)
         relu(1)
-        back(0, 2)
-        begin(2)
-        sum_cells(2, 0)
-        quantize_a(2, 0)
-        cam_transposes(1)
-        empty_cam(1)
+        stage2(0, (0, 1))
+        turn_cam(1, nc.vector.tensor_copy)
         quantize_cam(1)
-        back(0, 2)
-        stage1(2, (0,))
-        back(1, 4)
-        back(0, 4)
-        for u in (1, 2, 3, 4):
-            sum_cells(2, u)
-            if u % 2 == 0:
-                quantize_a(2, u // 2)
+        stage2(0, (2, 3))
+        stage2(1, (0, 1, 2, 3))
+        stage2(0, (4, 5, 6, 7))
+        begin(2)
+        means(2, (0,))
         begin(3)
-        sum_cells(3, 0)
-        quantize_a(3, 0)
-        back(1, 2)
-        stage1(2, (1, 2))
-        stage1(2, (3, 4))
+        means(3, (0,))
+        stage2(1, (4, 5))
+        means(2, (1, 2))
+        stage1(2, (0,), 0, 4)
+        stage2(1, (6,))
+        means(2, (3, 4))
+        stage1(2, (1, 2), 0, 4)
+        stage2(1, (7,))
+        stage1(2, (3, 4), 0, 4)
         relu(2)
-        sum_cells(3, 1)
-        sum_cells(3, 2)
-        back(1, 2)
-        cam_transposes(2)
-        empty_cam(2)
-        quantize_a(3, 1)
+        means(3, (1, 2))
+        turn_cam(2, nc.scalar.copy)
         quantize_cam(2)
-        sum_cells(3, 3)
-        sum_cells(3, 4)
-        quantize_a(3, 2)
-        stage1(3, (0,))
-        stage1(3, (1, 2))
-        back(2, 2)
-        stage1(3, (3, 4))
+        means(3, (3, 4))
+        stage2(2, (0, 1, 2, 3), width=2)
+        stage1(3, (0, 1, 2, 3, 4), 0, 4)
         relu(3)
-        back(2, 4)
-        cam_transposes(3)
-        empty_cam(3)
+        stage2(2, (4, 5), width=2)
+        turn_cam(3, nc.vector.tensor_copy)
         quantize_cam(3)
-        back(2, 2)
-        back(3, 8)
+        stage2(2, (6, 7), width=2)
+        stage2(3, range(6), shared=True, width=2)
+        stage2(3, range(6, 8), shared=True, width=1)

@@ -21,7 +21,8 @@ GE = CE // K
 GS = S // K
 STRIPS = NPIX // K
 UNITS = 1 + GE
-PIECES = (1, 2, 2, 2)
+PIECES = (((1, 4),), ((1, 2), (3, 2)), ((1, 2), (3, 2)), ((1, 2), (3, 2)))
+DEEP_PIECES = ((0, 2), (2, 2))
 FLOPS = 2 * M * (CD + CE) * S + 2 * M * S * NPIX
 
 
@@ -29,7 +30,7 @@ def tile_two_layer_gradcam_s3_kernel(
     tc, grad_deep, grad_early, deep, early_words, early_scales, up_words, up_scales, out
 ):
     nc = tc.nc
-    gd_view = grad_deep.rearrange("l (i j c b) k -> c (l i) j (b k)", j=4, c=BANDS // 2, b=2)
+    gd_view = grad_deep.rearrange("l (i j b) k -> (l i) j (b k)", j=4, b=BANDS)
     ge_view = grad_early.rearrange("l (i j b) k -> b (l i) j k", j=4, b=BANDS)
     out_view = out.rearrange("(q b) n -> b q n", b=BANDS)
 
@@ -49,21 +50,27 @@ def tile_two_layer_gradcam_s3_kernel(
         es = keep.tile([P, GE, S], U8, align_bytes=64)
         uw = [keep.tile([P, GS, NPIX // 2], U8, name="uw%d" % q, align_bytes=64) for q in range(4)]
         us = [keep.tile([P, GS, NPIX // 2], U8, name="us%d" % h, align_bytes=64) for h in range(2)]
-        gd = [keep.tile([P, 4, 2 * CD], BF16, name="gd%d" % c, align_bytes=64) for c in range(BANDS // 2)]
+        gd = {}
+        for b0, n in DEEP_PIECES:
+            piece = keep.tile([P, 4, n * CD], BF16, name="gd%d" % b0, align_bytes=64)
+            for b in range(b0, b0 + n):
+                gd[b] = piece[:, :, (b - b0) * CD : (b - b0 + 1) * CD]
+            gd[b0, n] = piece
         ge = {}
         for b in range(BANDS):
-            for h in range(PIECES[b]):
-                ge[b, h] = keep.tile([P, 4, CE // PIECES[b]], BF16, name="ge%d_%d" % (b, h), align_bytes=64)
+            for u0, n in PIECES[b]:
+                piece = keep.tile([P, 4, n * K], BF16, name="ge%d_%d" % (b, u0), align_bytes=64)
+                for u in range(u0, u0 + n):
+                    ge[b, u] = piece[:, :, (u - u0) * K : (u - u0 + 1) * K]
+                ge[b, u0, n] = piece
 
         ctx.enter_context(tc.manual_schedule())
 
-        def load_gd(c):
-            nc.sync.dma_start(out=gd[c][:], in_=gd_view[c])
+        def load_gd(b0, n):
+            nc.sync.dma_start(out=gd[b0, n][:], in_=gd_view[:, :, b0 * CD : (b0 + n) * CD])
 
-        def load_ge(b):
-            width = CE // PIECES[b]
-            for h in range(PIECES[b]):
-                nc.sync.dma_start(out=ge[b, h][:], in_=ge_view[b][:, :, h * width : (h + 1) * width])
+        def load_ge(b, u0, n):
+            nc.sync.dma_start(out=ge[b, u0, n][:], in_=ge_view[b][:, :, (u0 - 1) * K : (u0 - 1 + n) * K])
 
         def load_scales(plane, rows):
             for r in range(4):
@@ -97,20 +104,22 @@ def tile_two_layer_gradcam_s3_kernel(
             rows = slice(32 * l, 32 * l + 32)
             nc.scalar.activation(out=pick[rows, :], in_=ident[rows, rows], func=COPY, scale=1.0 / L)
 
-        load_gd(0)
+        load_gd(0, 2)
         load_deep()
-        load_ge(0)
+        load_ge(0, 1, 4)
         load_scales(es, early_scales)
         load_ew(0)
         load_ew(1)
-        load_ge(1)
+        load_ge(1, 1, 2)
+        load_ge(1, 3, 2)
         for h in range(2):
             load_us(h)
             load_uw(2 * h)
             load_uw(2 * h + 1)
-        load_gd(1)
-        load_ge(2)
-        load_ge(3)
+        load_gd(2, 2)
+        for b in (2, 3):
+            load_ge(b, 1, 2)
+            load_ge(b, 3, 2)
 
         def group_deep(h, copy):
             copy(
@@ -142,10 +151,9 @@ def tile_two_layer_gradcam_s3_kernel(
             for t in range(4):
                 for j in range(4):
                     if u == 0:
-                        cols = gd[b // 2][:, j, b % 2 * CD + t : (b % 2 + 1) * CD : 4]
+                        cols = gd[b][:, j, t:CD:4]
                     else:
-                        h, base = divmod((u - 1) * K, CE // PIECES[b])
-                        cols = ge[b, h][:, j, base + t : base + K : 4]
+                        cols = ge[b, u][:, j, t:K:4]
                     nc.tensor.matmul(acc[:, t * P + 32 * j : t * P + 32 * j + 32], lhsT=cols, rhs=pick[:], start=True, stop=True)
             dst = st[b]["means"][:, u * K : (u + 1) * K].rearrange("p (i j t) -> p i j t", j=4, t=4)
             src = acc[:].rearrange("p (t j i) -> p i j t", t=4, j=4)
@@ -159,8 +167,8 @@ def tile_two_layer_gradcam_s3_kernel(
                 in_=st[b]["means"][:, u0 * K : (u0 + n) * K],
             )
 
-        def stage1(b, units, first, last):
-            if first in units:
+        def stage1(b, units, first, last, fresh=True):
+            if fresh and first in units:
                 st[b]["z"] = [psum.tile([P, K], F32, name="z%d" % h) for h in range(GS)]
             for h in range(GS):
                 for u in units:
@@ -234,6 +242,9 @@ def tile_two_layer_gradcam_s3_kernel(
                 mean(b, u, u == units[-1])
             quantize_means(b, units[0], len(units))
 
+        def stage1_again(b):
+            stage1(b, (0, 1, 2, 3, 4), 0, 4, False)
+
         begin(0)
         means(0, (0,))
         group_deep(0, nc.vector.tensor_copy)
@@ -274,6 +285,7 @@ def tile_two_layer_gradcam_s3_kernel(
         stage1(2, (1, 2), 0, 4)
         stage2(1, (7,))
         stage1(2, (3, 4), 0, 4)
+        stage1_again(2)
         relu(2)
         means(3, (1, 2))
         turn_cam(2, nc.scalar.copy)

@@ -12,6 +12,9 @@ FP8X4 = mybir.dt.float8_e4m3fn_x4
 FP4X4 = mybir.dt.float4_e2m1fn_x4
 RELU = mybir.ActivationFunctionType.Relu
 COPY = mybir.ActivationFunctionType.Copy
+ADD = mybir.AluOpType.add
+MAX = mybir.AluOpType.max
+MULT = mybir.AluOpType.mult
 
 P = 128
 L, M, CD, CE, S, NPIX = 4, 512, 512, 2048, 1024, 4096
@@ -21,8 +24,9 @@ GE = CE // K
 GS = S // K
 STRIPS = NPIX // K
 UNITS = 1 + GE
-PIECES = (((1, 4),), ((1, 2), (3, 2)), ((1, 2), (3, 2)), ((1, 2), (3, 2)))
-DEEP_PIECES = ((0, 2), (2, 2))
+PIECES = (((1, 2), (3, 1), (4, 1)), ((1, 1), (2, 1), (3, 1), (4, 1)), ((1, 2), (3, 2)), ((1, 2), (3, 2)))
+DEEP_PIECES = ((0, 2), (2, 1), (3, 1))
+ON_VECTOR = {(3, 0), (3, 1), (3, 2)}
 FLOPS = 2 * M * (CD + CE) * S + 2 * M * S * NPIX
 
 
@@ -32,6 +36,8 @@ def tile_two_layer_gradcam_s3_kernel(
     nc = tc.nc
     gd_view = grad_deep.rearrange("l (i j b) k -> (l i) j (b k)", j=4, b=BANDS)
     ge_view = grad_early.rearrange("l (i j b) k -> b (l i) j k", j=4, b=BANDS)
+    gd_rows = grad_deep.rearrange("l (q b) k -> q l (b k)", b=BANDS)
+    ge_rows = grad_early.rearrange("l (q b) k -> b q l k", b=BANDS)
     out_view = out.rearrange("(q b) n -> b q n", b=BANDS)
 
     with ExitStack() as ctx:
@@ -67,10 +73,10 @@ def tile_two_layer_gradcam_s3_kernel(
         ctx.enter_context(tc.manual_schedule())
 
         def load_gd(b0, n):
-            nc.sync.dma_start(out=gd[b0, n][:], in_=gd_view[:, :, b0 * CD : (b0 + n) * CD])
+            nc.sync.dma_start(out=gd[b0, n][:], in_=(gd_rows if (b0, 0) in ON_VECTOR else gd_view)[:, :, b0 * CD : (b0 + n) * CD])
 
         def load_ge(b, u0, n):
-            nc.sync.dma_start(out=ge[b, u0, n][:], in_=ge_view[b][:, :, (u0 - 1) * K : (u0 - 1 + n) * K])
+            nc.sync.dma_start(out=ge[b, u0, n][:], in_=(ge_rows if (b, u0) in ON_VECTOR else ge_view)[b][:, :, (u0 - 1) * K : (u0 - 1 + n) * K])
 
         def load_scales(plane, rows):
             for r in range(4):
@@ -102,24 +108,30 @@ def tile_two_layer_gradcam_s3_kernel(
         make_identity(nc, ident[:])
         for l in range(L):
             rows = slice(32 * l, 32 * l + 32)
-            nc.scalar.activation(out=pick[rows, :], in_=ident[rows, rows], func=COPY, scale=1.0 / L)
+            nc.scalar.activation(out=pick[rows, :], in_=ident[rows, rows], func=COPY)
 
         load_gd(0, 2)
         load_deep()
-        load_ge(0, 1, 4)
+        load_ge(0, 1, 2)
         load_scales(es, early_scales)
         load_ew(0)
+        load_ge(0, 3, 1)
+        load_ge(0, 4, 1)
         load_ew(1)
-        load_ge(1, 1, 2)
-        load_ge(1, 3, 2)
-        for h in range(2):
-            load_us(h)
-            load_uw(2 * h)
-            load_uw(2 * h + 1)
-        load_gd(2, 2)
-        for b in (2, 3):
-            load_ge(b, 1, 2)
-            load_ge(b, 3, 2)
+        for u in range(1, UNITS):
+            load_ge(1, u, 1)
+        load_us(0)
+        load_uw(0)
+        load_uw(1)
+        load_gd(2, 1)
+        load_ge(2, 1, 2)
+        load_ge(2, 3, 2)
+        load_us(1)
+        load_uw(2)
+        load_uw(3)
+        load_gd(3, 1)
+        load_ge(3, 1, 2)
+        load_ge(3, 3, 2)
 
         def group_deep(h, copy):
             copy(
@@ -135,9 +147,19 @@ def tile_two_layer_gradcam_s3_kernel(
             )
 
         st = {}
+        pairs = {}
+        summed = {}
 
-        def bank():
-            return psum.tile([P, K], F32, name="bank", bufs=6)
+        free = list(range(8))
+        held = {}
+
+        def bank(owner):
+            held[owner] = free[0]
+            free.remove(held[owner])
+            return psum.tile([P, K], F32, name="bank%d" % held[owner])
+
+        def release(owner):
+            free.append(held[owner])
 
         def begin(b):
             st[b] = {
@@ -147,7 +169,7 @@ def tile_two_layer_gradcam_s3_kernel(
             }
 
         def mean(b, u, on_scalar):
-            acc = bank()
+            acc = bank("mean")
             for t in range(4):
                 for j in range(4):
                     if u == 0:
@@ -159,6 +181,38 @@ def tile_two_layer_gradcam_s3_kernel(
             src = acc[:].rearrange("p (t j i) -> p i j t", t=4, j=4)
             copy = nc.scalar.copy if on_scalar else nc.vector.tensor_copy
             copy(out=dst, in_=src)
+            release("mean")
+
+        def add_pairs(b, u):
+            source = gd[b] if u == 0 else ge[b, u]
+            pairs[b, u] = work.tile([P, 2, K], F32, name="pairs", align_bytes=64)
+            nc.vector.tensor_tensor(out=pairs[b, u][:], in0=source[:, 0:2, :], in1=source[:, 2:4, :], op=ADD)
+
+        def add_halves(b, u):
+            summed[b, u] = work.tile([P, K], BF16, name="summed", bufs=4, align_bytes=64)
+            halves = [pairs[b, u][:, h, :].rearrange("q (p v e) -> q v p e", v=2, e=2) for h in range(2)]
+            nc.vector.tensor_tensor(
+                out=summed[b, u][:].rearrange("q (v p e) -> q v p e", v=2, e=2), in0=halves[0], in1=halves[1], op=ADD
+            )
+
+        def add_cells(*units):
+            for b, u in units:
+                add_pairs(b, u)
+            for b, u in units:
+                add_halves(b, u)
+
+        def turn_sums(*units):
+            turned = bank("sums")
+            for n, (b, u) in enumerate(units):
+                words = summed[b, u][:].bitcast(F32)
+                for v in range(2):
+                    nc.tensor.transpose(turned[:, (2 * n + v) * P : (2 * n + v + 1) * P], words[:, v * P : (v + 1) * P], ident[:])
+            for n, (b, u) in enumerate(units):
+                nc.scalar.copy(
+                    out=st[b]["means"][:, u * K : (u + 1) * K].bitcast(F32).rearrange("p (m v) -> p m v", v=2),
+                    in_=turned[:, 2 * n * P : 2 * (n + 1) * P].rearrange("p (v m) -> p m v", v=2),
+                )
+            release("sums")
 
         def quantize_means(b, u0, n):
             nc.vector.quantize_mx(
@@ -167,9 +221,9 @@ def tile_two_layer_gradcam_s3_kernel(
                 in_=st[b]["means"][:, u0 * K : (u0 + n) * K],
             )
 
-        def stage1(b, units, first, last, fresh=True):
-            if fresh and first in units:
-                st[b]["z"] = [psum.tile([P, K], F32, name="z%d" % h) for h in range(GS)]
+        def stage1(b, units, first, last):
+            if first in units:
+                st[b]["z"] = [bank((b, h)) for h in range(GS)]
             for h in range(GS):
                 for u in units:
                     cols = slice(u * P, (u + 1) * P)
@@ -192,14 +246,16 @@ def tile_two_layer_gradcam_s3_kernel(
         def relu(b):
             st[b]["cam"] = work.tile([P, S], BF16, name="cam", align_bytes=64)
             for h in range(GS):
-                nc.scalar.activation(
-                    out=st[b]["cam"][:, h * K : (h + 1) * K].rearrange("m (u q e) -> m u q e", u=2, e=2),
-                    in_=st[b]["z"][h][:].rearrange("m (q u e) -> m u q e", u=2, e=2),
-                    func=RELU,
-                )
+                dst = st[b]["cam"][:, h * K : (h + 1) * K].rearrange("m (v q e) -> m v q e", v=2, e=2)
+                src = st[b]["z"][h][:].rearrange("m (q v e) -> m v q e", v=2, e=2)
+                if h == 0 or False:
+                    nc.scalar.activation(out=dst, in_=src, func=RELU, scale=1.0 / L)
+                else:
+                    nc.vector.tensor_scalar(out=dst, in0=src, scalar1=0.0, scalar2=1.0 / L, op0=MAX, op1=MULT)
+                release((b, h))
 
         def turn_cam(b, copy):
-            turned = bank()
+            turned = bank("cam")
             words = st[b]["cam"][:].bitcast(F32)
             for i in range(4):
                 nc.tensor.transpose(turned[:, i * P : (i + 1) * P], words[:, i * P : (i + 1) * P], ident[:])
@@ -208,6 +264,7 @@ def tile_two_layer_gradcam_s3_kernel(
                 out=grouped[:].bitcast(F32).rearrange("p (g m v) -> p g m v", g=GS, v=2),
                 in_=turned[:].rearrange("p (g v m) -> p g m v", g=GS, v=2),
             )
+            release("cam")
             st[b]["grouped"] = grouped
 
         def quantize_cam(b):
@@ -215,9 +272,9 @@ def tile_two_layer_gradcam_s3_kernel(
             st[b]["cam_scales"] = work.tile([P, GS * P], U8, name="cam_scales", align_bytes=64)
             nc.vector.quantize_mx(out=st[b]["cam_codes"][:].bitcast(FP8X4), scales=st[b]["cam_scales"][:], in_=st[b]["grouped"][:])
 
-        def stage2(b, strips, shared=False, width=4):
-            for n in strips:
-                acc = bank()
+        def stage2(b, strips, on="S", width=4):
+            for n, engine in zip(strips, on * len(strips)):
+                acc = bank("strip")
                 for g in range(GS):
                     nc.tensor.matmul_mx(
                         out=acc[:],
@@ -231,72 +288,92 @@ def tile_two_layer_gradcam_s3_kernel(
                 if n % 4 == 0:
                     st[b]["staged", n // 4] = outs.tile([P, 4 * K], F32, name="staged")
                 staged = st[b]["staged", n // 4]
-                copy = nc.vector.tensor_copy if shared and n % 2 == 1 else nc.scalar.copy
+                copy = nc.vector.tensor_copy if engine == "V" else nc.scalar.copy
                 copy(out=staged[:, (n % 4) * K : (n % 4 + 1) * K], in_=acc[:])
+                release("strip")
                 if n % width == width - 1:
                     lo = n + 1 - width
                     nc.sync.dma_start(out=out_view[b][:, lo * K : (n + 1) * K], in_=staged[:, (lo % 4) * K : (n % 4 + 1) * K])
 
-        def means(b, units):
-            for u in units:
-                mean(b, u, u == units[-1])
-            quantize_means(b, units[0], len(units))
-
-        def stage1_again(b):
-            stage1(b, (0, 1, 2, 3, 4), 0, 4, False)
-
         begin(0)
-        means(0, (0,))
-        group_deep(0, nc.vector.tensor_copy)
+        begin(1)
+        mean(0, 0, False)
+        mean(1, 0, False)
         group_deep(1, nc.scalar.copy)
+        quantize_means(0, 0, 1)
+        quantize_means(1, 0, 1)
+        group_deep(0, nc.vector.tensor_copy)
         quantize_deep(0)
         quantize_deep(1)
-        begin(1)
-        means(1, (0,))
+        mean(0, 1, True)
+        mean(0, 2, False)
+        quantize_means(0, 1, 2)
         stage1(0, (0,), 0, 4)
-        means(0, (1, 2))
-        means(0, (3, 4))
-        stage1(0, (1, 2), 0, 4)
-        stage1(0, (3, 4), 0, 4)
-        relu(0)
-        turn_cam(0, nc.scalar.copy)
-        quantize_cam(0)
-        means(1, (1, 2))
         stage1(1, (0,), 0, 4)
-        means(1, (3, 4))
-        stage1(1, (1, 2), 0, 4)
-        stage1(1, (3, 4), 0, 4)
+        stage1(0, (1, 2), 0, 4)
+        mean(0, 3, True)
+        quantize_means(0, 3, 1)
+        mean(0, 4, True)
+        quantize_means(0, 4, 1)
+        stage1(0, (3,), 0, 4)
+        stage1(0, (4,), 0, 4)
+        relu(0)
+        mean(1, 1, True)
+        quantize_means(1, 1, 1)
+        mean(1, 2, True)
+        quantize_means(1, 2, 1)
+        turn_cam(0, nc.vector.tensor_copy)
+        mean(1, 3, True)
+        quantize_cam(0)
+        quantize_means(1, 3, 1)
+        stage1(1, (1,), 0, 4)
+        mean(1, 4, True)
+        quantize_means(1, 4, 1)
+        stage1(1, (2,), 0, 4)
+        stage1(1, (3,), 0, 4)
+        stage1(1, (4,), 0, 4)
         relu(1)
-        stage2(0, (0, 1))
-        turn_cam(1, nc.vector.tensor_copy)
+        stage2(0, (0, 1), "SV")
+        turn_cam(1, nc.scalar.copy)
         quantize_cam(1)
-        stage2(0, (2, 3))
-        stage2(1, (0, 1, 2, 3))
-        stage2(0, (4, 5, 6, 7))
+        stage2(0, (2, 3), "VS")
         begin(2)
-        means(2, (0,))
-        begin(3)
-        means(3, (0,))
-        stage2(1, (4, 5))
-        means(2, (1, 2))
-        stage1(2, (0,), 0, 4)
-        stage2(1, (6,))
-        means(2, (3, 4))
-        stage1(2, (1, 2), 0, 4)
-        stage2(1, (7,))
+        mean(2, 0, True)
+        quantize_means(2, 0, 1)
+        stage2(1, (0, 1, 2, 3), "VS")
+        mean(2, 1, False)
+        mean(2, 2, True)
+        quantize_means(2, 1, 2)
+        mean(2, 3, False)
+        mean(2, 4, True)
+        quantize_means(2, 3, 2)
+        stage1(2, (0, 1, 2), 0, 4)
         stage1(2, (3, 4), 0, 4)
-        stage1_again(2)
         relu(2)
-        means(3, (1, 2))
+        begin(3)
+        add_cells((3, 0))
+        stage2(0, (4, 5), "SS")
         turn_cam(2, nc.scalar.copy)
         quantize_cam(2)
-        means(3, (3, 4))
-        stage2(2, (0, 1, 2, 3), width=2)
-        stage1(3, (0, 1, 2, 3, 4), 0, 4)
+        stage2(1, (4, 5))
+        stage2(0, (6, 7))
+        add_cells((3, 1), (3, 2))
+        stage2(1, (6, 7))
+        stage2(2, (0, 1), width=2)
+        mean(3, 3, True)
+        mean(3, 4, True)
+        turn_sums((3, 0))
+        turn_sums((3, 1), (3, 2))
+        quantize_means(3, 3, 2)
+        quantize_means(3, 0, 1)
+        quantize_means(3, 1, 2)
+        stage2(2, (2,), "V", width=2)
+        stage1(3, (3, 4), 3, 2)
+        stage1(3, (0, 1, 2), 3, 2)
         relu(3)
-        stage2(2, (4, 5), width=2)
-        turn_cam(3, nc.vector.tensor_copy)
+        stage2(2, (3, 4), "SV", width=2)
+        turn_cam(3, nc.scalar.copy)
         quantize_cam(3)
-        stage2(2, (6, 7), width=2)
-        stage2(3, range(6), shared=True, width=2)
-        stage2(3, range(6, 8), shared=True, width=1)
+        stage2(2, (5, 6, 7), "SVS", width=2)
+        stage2(3, range(6), "VS", width=2)
+        stage2(3, range(6, 8), "VS", width=1)

@@ -78,9 +78,9 @@ def tile_two_layer_gradcam_s3_kernel(
         def load_ge(b, u0, n):
             nc.sync.dma_start(out=ge[b, u0, n][:], in_=(ge_rows if (b, u0) in ON_VECTOR else ge_view)[b][:, :, (u0 - 1) * K : (u0 - 1 + n) * K])
 
-        def load_scales(plane, rows):
+        def load_scales(plane, rows, queue=nc.sync):
             for r in range(4):
-                nc.sync.dma_start(
+                queue.dma_start(
                     out=plane[r:P:32, :, :].bitcast(I32),
                     in_=rows.rearrange("g (q r) n -> r q g n", r=4)[r].bitcast(I32),
                 )
@@ -105,15 +105,15 @@ def tile_two_layer_gradcam_s3_kernel(
 
         for plane in [es] + us:
             nc.vector.memset(plane[:].rearrange("p g n -> p (g n)").bitcast(I32), 0)
+        load_gd(0, 2)
+        load_deep()
+        load_ge(0, 1, 2)
+        load_scales(es, early_scales, nc.scalar)
         make_identity(nc, ident[:])
         for l in range(L):
             rows = slice(32 * l, 32 * l + 32)
             nc.scalar.activation(out=pick[rows, :], in_=ident[rows, rows], func=COPY)
 
-        load_gd(0, 2)
-        load_deep()
-        load_ge(0, 1, 2)
-        load_scales(es, early_scales)
         load_ew(0)
         load_ge(0, 3, 1)
         load_ge(0, 4, 1)

@@ -25,7 +25,6 @@ GS = S // K
 STRIPS = NPIX // K
 UNITS = 1 + GE
 PIECES = (((1, 2), (3, 1), (4, 1)), ((1, 1), (2, 1), (3, 1), (4, 1)), ((1, 2), (3, 2)), ((1, 2), (3, 2)))
-DEEP_PIECES = ((0, 2), (2, 1), (3, 1))
 ON_VECTOR = {(3, 0), (3, 1), (3, 2)}
 FLOPS = 2 * M * (CD + CE) * S + 2 * M * S * NPIX
 
@@ -54,14 +53,9 @@ def tile_two_layer_gradcam_s3_kernel(
         deep_scales = keep.tile([P, S], U8, align_bytes=64)
         ew = [keep.tile([P, 2, 2 * S], U8, name="ew%d" % h, align_bytes=64) for h in range(2)]
         es = keep.tile([P, GE, S], U8, align_bytes=64)
-        uw = [keep.tile([P, GS, NPIX // 2], U8, name="uw%d" % q, align_bytes=64) for q in range(4)]
+        uw = {}
         us = [keep.tile([P, GS, NPIX // 2], U8, name="us%d" % h, align_bytes=64) for h in range(2)]
         gd = {}
-        for b0, n in DEEP_PIECES:
-            piece = keep.tile([P, 4, n * CD], BF16, name="gd%d" % b0, align_bytes=64)
-            for b in range(b0, b0 + n):
-                gd[b] = piece[:, :, (b - b0) * CD : (b - b0 + 1) * CD]
-            gd[b0, n] = piece
         ge = {}
         for b in range(BANDS):
             for u0, n in PIECES[b]:
@@ -72,13 +66,16 @@ def tile_two_layer_gradcam_s3_kernel(
 
         ctx.enter_context(tc.manual_schedule())
 
-        def load_gd(b0, n):
-            nc.sync.dma_start(out=gd[b0, n][:], in_=(gd_rows if (b0, 0) in ON_VECTOR else gd_view)[:, :, b0 * CD : (b0 + n) * CD])
+        def load_gd(b0, n, slot):
+            piece = keep.tile([P, 4, n * CD], BF16, name=slot, align_bytes=64)
+            for b in range(b0, b0 + n):
+                gd[b] = piece[:, :, (b - b0) * CD : (b - b0 + 1) * CD]
+            nc.sync.dma_start(out=piece[:], in_=(gd_rows if (b0, 0) in ON_VECTOR else gd_view)[:, :, b0 * CD : (b0 + n) * CD])
 
         def load_ge(b, u0, n):
             nc.sync.dma_start(out=ge[b, u0, n][:], in_=(ge_rows if (b, u0) in ON_VECTOR else ge_view)[b][:, :, (u0 - 1) * K : (u0 - 1 + n) * K])
 
-        def load_scales(plane, rows, queue=nc.sync):
+        def load_scales(plane, rows, queue):
             for r in range(4):
                 queue.dma_start(
                     out=plane[r:P:32, :, :].bitcast(I32),
@@ -91,21 +88,24 @@ def tile_two_layer_gradcam_s3_kernel(
                 in_=early_words[2 * h : 2 * h + 2].rearrange("g p n -> p g n").bitcast(I32),
             )
 
-        def load_uw(q):
+        def load_uw(n0, count, slot):
+            piece = keep.tile([P, GS, count * 2 * K], U8, name=slot, align_bytes=64)
+            for n in range(n0, n0 + count):
+                uw[n] = piece[:, :, (n - n0) * 2 * K : (n - n0 + 1) * 2 * K]
             nc.sync.dma_start(
-                out=uw[q][:].bitcast(I32),
-                in_=up_words[:, :, q * NPIX // 2 : (q + 1) * NPIX // 2].rearrange("g p n -> p g n").bitcast(I32),
+                out=piece[:].bitcast(I32),
+                in_=up_words[:, :, n0 * 2 * K : (n0 + count) * 2 * K].rearrange("g p n -> p g n").bitcast(I32),
             )
 
-        def load_us(h):
-            load_scales(us[h], up_scales[:, :, h * NPIX // 2 : (h + 1) * NPIX // 2])
+        def load_us(h, queue):
+            load_scales(us[h], up_scales[:, :, h * NPIX // 2 : (h + 1) * NPIX // 2], queue)
 
         def load_deep():
             nc.sync.dma_start(out=deep_raw[:], in_=deep.rearrange("(p j) w -> p j w", j=4))
 
         for plane in [es] + us:
             nc.vector.memset(plane[:].rearrange("p g n -> p (g n)").bitcast(I32), 0)
-        load_gd(0, 2)
+        load_gd(0, 2, "gd01")
         load_deep()
         load_ge(0, 1, 2)
         load_scales(es, early_scales, nc.scalar)
@@ -120,18 +120,6 @@ def tile_two_layer_gradcam_s3_kernel(
         load_ew(1)
         for u in range(1, UNITS):
             load_ge(1, u, 1)
-        load_us(0)
-        load_uw(0)
-        load_uw(1)
-        load_gd(2, 1)
-        load_ge(2, 1, 2)
-        load_ge(2, 3, 2)
-        load_us(1)
-        load_uw(2)
-        load_uw(3)
-        load_gd(3, 1)
-        load_ge(3, 1, 2)
-        load_ge(3, 3, 2)
 
         def group_deep(h, copy):
             copy(
@@ -147,6 +135,7 @@ def tile_two_layer_gradcam_s3_kernel(
             )
 
         st = {}
+        ready = []
         pairs = {}
         summed = {}
 
@@ -272,7 +261,12 @@ def tile_two_layer_gradcam_s3_kernel(
             st[b]["cam_scales"] = work.tile([P, GS * P], U8, name="cam_scales", align_bytes=64)
             nc.vector.quantize_mx(out=st[b]["cam_codes"][:].bitcast(FP8X4), scales=st[b]["cam_scales"][:], in_=st[b]["grouped"][:])
 
-        def stage2(b, strips, on="S", width=4):
+        def store_ready():
+            for rows, source in ready:
+                nc.sync.dma_start(out=rows, in_=source)
+            ready.clear()
+
+        def stage2(b, strips, on="S", width=4, loads_first=False):
             for n, engine in zip(strips, on * len(strips)):
                 acc = bank("strip")
                 for g in range(GS):
@@ -280,7 +274,7 @@ def tile_two_layer_gradcam_s3_kernel(
                         out=acc[:],
                         lhsT=st[b]["cam_codes"][:, g * P : (g + 1) * P].bitcast(FP8X4),
                         lhsT_scale=st[b]["cam_scales"][:, g * P : (g + 1) * P],
-                        rhs=uw[n // 2][:, g, (n % 2) * 2 * K : (n % 2 + 1) * 2 * K].bitcast(FP4X4),
+                        rhs=uw[n][:, g, :].bitcast(FP4X4),
                         rhs_scale=us[n // 4][:, g, (n % 4) * K : (n % 4 + 1) * K],
                         start=(g == 0),
                         stop=(g == GS - 1),
@@ -293,25 +287,33 @@ def tile_two_layer_gradcam_s3_kernel(
                 release("strip")
                 if n % width == width - 1:
                     lo = n + 1 - width
-                    nc.sync.dma_start(out=out_view[b][:, lo * K : (n + 1) * K], in_=staged[:, (lo % 4) * K : (n % 4 + 1) * K])
+                    ready.append((out_view[b][:, lo * K : (n + 1) * K], staged[:, (lo % 4) * K : (n % 4 + 1) * K]))
+                    if not loads_first:
+                        store_ready()
 
         begin(0)
         begin(1)
         mean(0, 0, False)
         mean(1, 0, False)
         group_deep(1, nc.scalar.copy)
+        load_us(0, nc.scalar)
         quantize_means(0, 0, 1)
         quantize_means(1, 0, 1)
         group_deep(0, nc.vector.tensor_copy)
         quantize_deep(0)
         quantize_deep(1)
-        mean(0, 1, True)
+        mean(0, 1, False)
         mean(0, 2, False)
         quantize_means(0, 1, 2)
         stage1(0, (0,), 0, 4)
         stage1(1, (0,), 0, 4)
         stage1(0, (1, 2), 0, 4)
-        mean(0, 3, True)
+        mean(0, 3, False)
+        load_uw(0, 2, "ge0_3")
+        load_uw(2, 2, "uw2")
+        load_gd(2, 1, "gd2")
+        load_ge(2, 1, 2)
+        load_ge(2, 3, 2)
         quantize_means(0, 3, 1)
         mean(0, 4, True)
         quantize_means(0, 4, 1)
@@ -333,12 +335,19 @@ def tile_two_layer_gradcam_s3_kernel(
         stage1(1, (3,), 0, 4)
         stage1(1, (4,), 0, 4)
         relu(1)
+        load_us(1, nc.scalar)
         stage2(0, (0, 1), "SV")
         turn_cam(1, nc.scalar.copy)
         quantize_cam(1)
-        stage2(0, (2, 3), "VS")
+        stage2(0, (2, 3), "VS", loads_first=True)
         begin(2)
         mean(2, 0, True)
+        load_uw(4, 2, "gd2")
+        load_uw(6, 2, "uw6")
+        load_gd(3, 1, "gd3")
+        load_ge(3, 1, 2)
+        load_ge(3, 3, 2)
+        store_ready()
         quantize_means(2, 0, 1)
         stage2(1, (0, 1, 2, 3), "VS")
         mean(2, 1, False)

@@ -237,7 +237,7 @@ def tile_two_layer_gradcam_s3_kernel(
             for h in range(GS):
                 dst = st[b]["cam"][:, h * K : (h + 1) * K].rearrange("m (v q e) -> m v q e", v=2, e=2)
                 src = st[b]["z"][h][:].rearrange("m (q v e) -> m v q e", v=2, e=2)
-                if h == 0 or False:
+                if h == 0 or b == 2:
                     nc.scalar.activation(out=dst, in_=src, func=RELU, scale=1.0 / L)
                 else:
                     nc.vector.tensor_scalar(out=dst, in0=src, scalar1=0.0, scalar2=1.0 / L, op0=MAX, op1=MULT)
@@ -306,8 +306,6 @@ def tile_two_layer_gradcam_s3_kernel(
         mean(0, 2, False)
         quantize_means(0, 1, 2)
         stage1(0, (0,), 0, 4)
-        stage1(1, (0,), 0, 4)
-        stage1(0, (1, 2), 0, 4)
         mean(0, 3, False)
         load_uw(0, 2, "ge0_3")
         load_uw(2, 2, "uw2")
@@ -315,8 +313,10 @@ def tile_two_layer_gradcam_s3_kernel(
         load_ge(2, 1, 2)
         load_ge(2, 3, 2)
         quantize_means(0, 3, 1)
-        mean(0, 4, True)
+        stage1(0, (1, 2), 0, 4)
+        mean(0, 4, False)
         quantize_means(0, 4, 1)
+        stage1(1, (0,), 0, 4)
         stage1(0, (3,), 0, 4)
         stage1(0, (4,), 0, 4)
         relu(0)
@@ -342,10 +342,10 @@ def tile_two_layer_gradcam_s3_kernel(
         stage2(0, (2, 3), "VS", loads_first=True)
         begin(2)
         mean(2, 0, True)
-        load_uw(4, 2, "gd2")
-        load_uw(6, 2, "uw6")
-        load_gd(3, 1, "gd3")
+        load_gd(3, 1, "gd2")
+        load_uw(4, 2, "uw4")
         load_ge(3, 1, 2)
+        load_uw(6, 2, "uw6")
         load_ge(3, 3, 2)
         store_ready()
         quantize_means(2, 0, 1)
@@ -356,29 +356,33 @@ def tile_two_layer_gradcam_s3_kernel(
         mean(2, 3, False)
         mean(2, 4, True)
         quantize_means(2, 3, 2)
-        stage1(2, (0, 1, 2), 0, 4)
-        stage1(2, (3, 4), 0, 4)
-        relu(2)
+        stage1(2, (0,), 0, 4)
+        stage1(2, (1, 2), 0, 4)
         begin(3)
         add_cells((3, 0))
+        stage1(2, (3, 4), 0, 4)
+        relu(2)
+        add_pairs(3, 1)
         stage2(0, (4, 5), "SS")
         turn_cam(2, nc.scalar.copy)
+        turn_sums((3, 0))
+        add_pairs(3, 2)
         quantize_cam(2)
+        quantize_means(3, 0, 1)
+        add_halves(3, 1)
+        add_halves(3, 2)
         stage2(1, (4, 5))
         stage2(0, (6, 7))
-        add_cells((3, 1), (3, 2))
-        stage2(1, (6, 7))
-        stage2(2, (0, 1), width=2)
+        stage2(1, (6, 7), "SV")
         mean(3, 3, True)
-        mean(3, 4, True)
-        turn_sums((3, 0))
+        mean(3, 4, False)
         turn_sums((3, 1), (3, 2))
         quantize_means(3, 3, 2)
-        quantize_means(3, 0, 1)
         quantize_means(3, 1, 2)
+        stage2(2, (0, 1), "VS", width=2)
+        stage1(3, (0, 3, 4), 0, 2)
         stage2(2, (2,), "V", width=2)
-        stage1(3, (3, 4), 3, 2)
-        stage1(3, (0, 1, 2), 3, 2)
+        stage1(3, (1, 2), 0, 2)
         relu(3)
         stage2(2, (3, 4), "SV", width=2)
         turn_cam(3, nc.scalar.copy)

@@ -24,8 +24,8 @@ GE = CE // K
 GS = S // K
 STRIPS = NPIX // K
 UNITS = 1 + GE
-PIECES = (((1, 2), (3, 1), (4, 1)), ((1, 1), (2, 1), (3, 1), (4, 1)), ((1, 2), (3, 2)), ((1, 2), (3, 2)))
-ON_VECTOR = {(3, 0), (3, 1), (3, 2)}
+US_CUTS = (0, 2, 8)
+ON_VECTOR = {(3, 1), (3, 2), (3, 3), (3, 4)}
 FLOPS = 2 * M * (CD + CE) * S + 2 * M * S * NPIX
 
 
@@ -42,27 +42,20 @@ def tile_two_layer_gradcam_s3_kernel(
     with ExitStack() as ctx:
         keep = ctx.enter_context(tc.tile_pool(name="keep", bufs=1))
         work = ctx.enter_context(tc.tile_pool(name="work", bufs=2))
-        outs = ctx.enter_context(tc.tile_pool(name="outs", bufs=7))
         psum = ctx.enter_context(tc.psum_pool(name="psum", bufs=1))
 
         ident = keep.tile([P, P], F32, align_bytes=64)
         pick = keep.tile([P, 32], BF16, align_bytes=64)
-        deep_raw = keep.tile([P, 4, S], BF16, align_bytes=64)
+        deep_raw = keep.tile([P, 4, S], BF16, name="deep_raw", align_bytes=64)
         deep_grouped = keep.tile([P, S * 4], BF16, align_bytes=64)
         deep_codes = keep.tile([P, S], U32, align_bytes=64)
         deep_scales = keep.tile([P, S], U8, align_bytes=64)
-        ew = [keep.tile([P, 2, 2 * S], U8, name="ew%d" % h, align_bytes=64) for h in range(2)]
+        ew = {}
         es = keep.tile([P, GE, S], U8, align_bytes=64)
         uw = {}
-        us = [keep.tile([P, GS, NPIX // 2], U8, name="us%d" % h, align_bytes=64) for h in range(2)]
+        us = [keep.tile([P, GS, (US_CUTS[h + 1] - US_CUTS[h]) * K], U8, name="us%d" % h, align_bytes=64) for h in range(len(US_CUTS) - 1)]
         gd = {}
         ge = {}
-        for b in range(BANDS):
-            for u0, n in PIECES[b]:
-                piece = keep.tile([P, 4, n * K], BF16, name="ge%d_%d" % (b, u0), align_bytes=64)
-                for u in range(u0, u0 + n):
-                    ge[b, u] = piece[:, :, (u - u0) * K : (u - u0 + 1) * K]
-                ge[b, u0, n] = piece
 
         ctx.enter_context(tc.manual_schedule())
 
@@ -72,8 +65,11 @@ def tile_two_layer_gradcam_s3_kernel(
                 gd[b] = piece[:, :, (b - b0) * CD : (b - b0 + 1) * CD]
             nc.sync.dma_start(out=piece[:], in_=(gd_rows if (b0, 0) in ON_VECTOR else gd_view)[:, :, b0 * CD : (b0 + n) * CD])
 
-        def load_ge(b, u0, n):
-            nc.sync.dma_start(out=ge[b, u0, n][:], in_=(ge_rows if (b, u0) in ON_VECTOR else ge_view)[b][:, :, (u0 - 1) * K : (u0 - 1 + n) * K])
+        def load_ge(b, u0, n, slot=None):
+            piece = keep.tile([P, 4, n * K], BF16, name=slot or "ge%d_%d" % (b, u0), align_bytes=64)
+            for u in range(u0, u0 + n):
+                ge[b, u] = piece[:, :, (u - u0) * K : (u - u0 + 1) * K]
+            nc.sync.dma_start(out=piece[:], in_=(ge_rows if (b, u0) in ON_VECTOR else ge_view)[b][:, :, (u0 - 1) * K : (u0 - 1 + n) * K])
 
         def load_scales(plane, rows, queue):
             for r in range(4):
@@ -82,11 +78,11 @@ def tile_two_layer_gradcam_s3_kernel(
                     in_=rows.rearrange("g (q r) n -> r q g n", r=4)[r].bitcast(I32),
                 )
 
-        def load_ew(h):
-            nc.sync.dma_start(
-                out=ew[h][:].bitcast(I32),
-                in_=early_words[2 * h : 2 * h + 2].rearrange("g p n -> p g n").bitcast(I32),
-            )
+        def load_ew(g0, count, slot=None):
+            piece = keep.tile([P, count, 2 * S], U8, name=slot or "ew%d" % g0, align_bytes=64)
+            for g in range(g0, g0 + count):
+                ew[g] = piece[:, g - g0, :]
+            nc.sync.dma_start(out=piece[:].bitcast(I32), in_=early_words[g0 : g0 + count].rearrange("g p n -> p g n").bitcast(I32))
 
         def load_uw(n0, count, slot):
             piece = keep.tile([P, GS, count * 2 * K], U8, name=slot, align_bytes=64)
@@ -98,31 +94,13 @@ def tile_two_layer_gradcam_s3_kernel(
             )
 
         def load_us(h, queue):
-            load_scales(us[h], up_scales[:, :, h * NPIX // 2 : (h + 1) * NPIX // 2], queue)
+            load_scales(us[h], up_scales[:, :, US_CUTS[h] * K : US_CUTS[h + 1] * K], queue)
 
         def load_deep():
             nc.sync.dma_start(out=deep_raw[:], in_=deep.rearrange("(p j) w -> p j w", j=4))
 
-        for plane in [es] + us:
-            nc.vector.memset(plane[:].rearrange("p g n -> p (g n)").bitcast(I32), 0)
-        load_gd(0, 2, "gd01")
-        load_deep()
-        load_ge(0, 1, 2)
-        load_scales(es, early_scales, nc.scalar)
-        make_identity(nc, ident[:])
-        for l in range(L):
-            rows = slice(32 * l, 32 * l + 32)
-            nc.scalar.activation(out=pick[rows, :], in_=ident[rows, rows], func=COPY)
-
-        load_ew(0)
-        load_ge(0, 3, 1)
-        load_ge(0, 4, 1)
-        load_ew(1)
-        for u in range(1, UNITS):
-            load_ge(1, u, 1)
-
-        def group_deep(h, copy):
-            copy(
+        def group_deep(h, on):
+            engine_copy(on)(
                 out=deep_grouped[:, h * K * 4 : (h + 1) * K * 4].rearrange("p (w j) -> p w j", j=4),
                 in_=deep_raw[:, :, h * K : (h + 1) * K].rearrange("p j w -> p w j"),
             )
@@ -136,6 +114,7 @@ def tile_two_layer_gradcam_s3_kernel(
 
         st = {}
         ready = []
+        spent = ["deep_raw", "gd01", "ge0_1", "ge0_3", "ge1_1", "ge1_3", "gd23", "ge2_1"]
         pairs = {}
         summed = {}
 
@@ -150,14 +129,29 @@ def tile_two_layer_gradcam_s3_kernel(
         def release(owner):
             free.append(held[owner])
 
+        def copy_by_activation(out, in_):
+            nc.scalar.activation(out=out, in_=in_, func=COPY)
+
+        def engine_copy(on):
+            return {"V": nc.vector.tensor_copy, "S": nc.scalar.copy, "A": copy_by_activation}[on]
+
+        def zero(plane):
+            nc.vector.memset(plane[:].rearrange("p g n -> p (g n)").bitcast(I32), 0)
+
+        def constants():
+            make_identity(nc, ident[:])
+            for l in range(L):
+                rows = slice(32 * l, 32 * l + 32)
+                nc.vector.tensor_copy(out=pick[rows, :], in_=ident[rows, rows])
+
         def begin(b):
             st[b] = {
                 "means": work.tile([P, UNITS * K], BF16, name="means", align_bytes=64),
-                "codes": work.tile([P, UNITS * P], U32, name="codes", align_bytes=64),
-                "scales": work.tile([P, UNITS * P], U8, name="scales", align_bytes=64),
+                "codes": work.tile([P, UNITS * P], U32, name="codes", bufs=4, align_bytes=64),
+                "scales": work.tile([P, UNITS * P], U8, name="scales", bufs=4, align_bytes=64),
             }
 
-        def mean(b, u, on_scalar):
+        def mean(b, u, on):
             acc = bank("mean")
             for t in range(4):
                 for j in range(4):
@@ -168,8 +162,7 @@ def tile_two_layer_gradcam_s3_kernel(
                     nc.tensor.matmul(acc[:, t * P + 32 * j : t * P + 32 * j + 32], lhsT=cols, rhs=pick[:], start=True, stop=True)
             dst = st[b]["means"][:, u * K : (u + 1) * K].rearrange("p (i j t) -> p i j t", j=4, t=4)
             src = acc[:].rearrange("p (t j i) -> p i j t", t=4, j=4)
-            copy = nc.scalar.copy if on_scalar else nc.vector.tensor_copy
-            copy(out=dst, in_=src)
+            engine_copy(on)(out=dst, in_=src)
             release("mean")
 
         def add_pairs(b, u):
@@ -190,14 +183,14 @@ def tile_two_layer_gradcam_s3_kernel(
             for b, u in units:
                 add_halves(b, u)
 
-        def turn_sums(*units):
+        def turn_sums(on, *units):
             turned = bank("sums")
             for n, (b, u) in enumerate(units):
                 words = summed[b, u][:].bitcast(F32)
                 for v in range(2):
                     nc.tensor.transpose(turned[:, (2 * n + v) * P : (2 * n + v + 1) * P], words[:, v * P : (v + 1) * P], ident[:])
             for n, (b, u) in enumerate(units):
-                nc.scalar.copy(
+                engine_copy(on)(
                     out=st[b]["means"][:, u * K : (u + 1) * K].bitcast(F32).rearrange("p (m v) -> p m v", v=2),
                     in_=turned[:, 2 * n * P : 2 * (n + 1) * P].rearrange("p (v m) -> p m v", v=2),
                 )
@@ -210,7 +203,7 @@ def tile_two_layer_gradcam_s3_kernel(
                 in_=st[b]["means"][:, u0 * K : (u0 + n) * K],
             )
 
-        def stage1(b, units, first, last):
+        def stage1(b, units, first=0, last=4):
             if first in units:
                 st[b]["z"] = [bank((b, h)) for h in range(GS)]
             for h in range(GS):
@@ -220,7 +213,7 @@ def tile_two_layer_gradcam_s3_kernel(
                         rhs = deep_codes[:, h * K : (h + 1) * K].bitcast(FP8X4)
                         rhs_scale = deep_scales[:, h * K : (h + 1) * K]
                     else:
-                        rhs = ew[(u - 1) // 2][:, (u - 1) % 2, h * 2 * K : (h + 1) * 2 * K].bitcast(FP4X4)
+                        rhs = ew[u - 1][:, h * 2 * K : (h + 1) * 2 * K].bitcast(FP4X4)
                         rhs_scale = es[:, u - 1, h * K : (h + 1) * K]
                     nc.tensor.matmul_mx(
                         out=st[b]["z"][h][:],
@@ -232,24 +225,24 @@ def tile_two_layer_gradcam_s3_kernel(
                         stop=(u == last),
                     )
 
-        def relu(b):
+        def relu(b, on):
             st[b]["cam"] = work.tile([P, S], BF16, name="cam", align_bytes=64)
             for h in range(GS):
                 dst = st[b]["cam"][:, h * K : (h + 1) * K].rearrange("m (v q e) -> m v q e", v=2, e=2)
                 src = st[b]["z"][h][:].rearrange("m (q v e) -> m v q e", v=2, e=2)
-                if h == 0 or b == 2:
+                if on[h] == "S":
                     nc.scalar.activation(out=dst, in_=src, func=RELU, scale=1.0 / L)
                 else:
                     nc.vector.tensor_scalar(out=dst, in0=src, scalar1=0.0, scalar2=1.0 / L, op0=MAX, op1=MULT)
                 release((b, h))
 
-        def turn_cam(b, copy):
+        def turn_cam(b, on):
             turned = bank("cam")
             words = st[b]["cam"][:].bitcast(F32)
             for i in range(4):
                 nc.tensor.transpose(turned[:, i * P : (i + 1) * P], words[:, i * P : (i + 1) * P], ident[:])
             grouped = work.tile([P, S], BF16, name="grouped", align_bytes=64)
-            copy(
+            engine_copy(on)(
                 out=grouped[:].bitcast(F32).rearrange("p (g m v) -> p g m v", g=GS, v=2),
                 in_=turned[:].rearrange("p (g v m) -> p g m v", g=GS, v=2),
             )
@@ -257,136 +250,144 @@ def tile_two_layer_gradcam_s3_kernel(
             st[b]["grouped"] = grouped
 
         def quantize_cam(b):
-            st[b]["cam_codes"] = work.tile([P, GS * P], U32, name="cam_codes", align_bytes=64)
-            st[b]["cam_scales"] = work.tile([P, GS * P], U8, name="cam_scales", align_bytes=64)
+            st[b]["cam_codes"] = work.tile([P, GS * P], U32, name="cam_codes", bufs=4, align_bytes=64)
+            st[b]["cam_scales"] = work.tile([P, GS * P], U8, name="cam_scales", bufs=4, align_bytes=64)
             nc.vector.quantize_mx(out=st[b]["cam_codes"][:].bitcast(FP8X4), scales=st[b]["cam_scales"][:], in_=st[b]["grouped"][:])
 
-        def store_ready():
+        def store_ready(queue):
             for rows, source in ready:
-                nc.sync.dma_start(out=rows, in_=source)
+                queue.dma_start(out=rows, in_=source)
             ready.clear()
 
-        def stage2(b, strips, on="S", width=4, loads_first=False):
+        def stage2(b, strips, on="S", width=4, queues="Y"):
+            stores = 0
             for n, engine in zip(strips, on * len(strips)):
                 acc = bank("strip")
+                run = max(h for h in range(len(us)) if US_CUTS[h] <= n)
                 for g in range(GS):
                     nc.tensor.matmul_mx(
                         out=acc[:],
                         lhsT=st[b]["cam_codes"][:, g * P : (g + 1) * P].bitcast(FP8X4),
                         lhsT_scale=st[b]["cam_scales"][:, g * P : (g + 1) * P],
                         rhs=uw[n][:, g, :].bitcast(FP4X4),
-                        rhs_scale=us[n // 4][:, g, (n % 4) * K : (n % 4 + 1) * K],
+                        rhs_scale=us[run][:, g, (n - US_CUTS[run]) * K : (n - US_CUTS[run] + 1) * K],
                         start=(g == 0),
                         stop=(g == GS - 1),
                     )
                 if n % 4 == 0:
-                    st[b]["staged", n // 4] = outs.tile([P, 4 * K], F32, name="staged")
+                    st[b]["staged", n // 4] = keep.tile([P, 4 * K], F32, name=spent.pop(0), align_bytes=64)
                 staged = st[b]["staged", n // 4]
-                copy = nc.vector.tensor_copy if engine == "V" else nc.scalar.copy
-                copy(out=staged[:, (n % 4) * K : (n % 4 + 1) * K], in_=acc[:])
+                engine_copy(engine)(out=staged[:, (n % 4) * K : (n % 4 + 1) * K], in_=acc[:])
                 release("strip")
                 if n % width == width - 1:
                     lo = n + 1 - width
                     ready.append((out_view[b][:, lo * K : (n + 1) * K], staged[:, (lo % 4) * K : (n % 4 + 1) * K]))
-                    if not loads_first:
-                        store_ready()
+                    store_ready(nc.sync if queues[stores % len(queues)] == "Y" else nc.scalar)
+                    stores = stores + 1
 
-        begin(0)
-        begin(1)
-        mean(0, 0, False)
-        mean(1, 0, False)
-        group_deep(1, nc.scalar.copy)
+        zero(es)
+        zero(us[0])
+        load_deep()
+        load_gd(0, 2, "gd01")
+        load_ge(0, 1, 2)
+        load_scales(es, early_scales, nc.scalar)
         load_us(0, nc.scalar)
-        quantize_means(0, 0, 1)
-        quantize_means(1, 0, 1)
-        group_deep(0, nc.vector.tensor_copy)
-        quantize_deep(0)
-        quantize_deep(1)
-        mean(0, 1, False)
-        mean(0, 2, False)
-        quantize_means(0, 1, 2)
-        stage1(0, (0,), 0, 4)
-        mean(0, 3, False)
-        load_uw(0, 2, "ge0_3")
-        load_uw(2, 2, "uw2")
-        load_gd(2, 1, "gd2")
+        constants()
+        zero(us[1])
+        load_ge(0, 3, 2)
+        load_ew(0, 4)
+        load_ge(1, 1, 2)
+        load_ge(1, 3, 2)
+        load_gd(2, 2, "gd23")
         load_ge(2, 1, 2)
         load_ge(2, 3, 2)
-        quantize_means(0, 3, 1)
-        stage1(0, (1, 2), 0, 4)
-        mean(0, 4, False)
-        quantize_means(0, 4, 1)
-        stage1(1, (0,), 0, 4)
-        stage1(0, (3,), 0, 4)
-        stage1(0, (4,), 0, 4)
-        relu(0)
-        mean(1, 1, True)
-        quantize_means(1, 1, 1)
-        mean(1, 2, True)
-        quantize_means(1, 2, 1)
-        turn_cam(0, nc.vector.tensor_copy)
-        mean(1, 3, True)
-        quantize_cam(0)
-        quantize_means(1, 3, 1)
-        stage1(1, (1,), 0, 4)
-        mean(1, 4, True)
-        quantize_means(1, 4, 1)
-        stage1(1, (2,), 0, 4)
-        stage1(1, (3,), 0, 4)
-        stage1(1, (4,), 0, 4)
-        relu(1)
-        load_us(1, nc.scalar)
-        stage2(0, (0, 1), "SV")
-        turn_cam(1, nc.scalar.copy)
-        quantize_cam(1)
-        stage2(0, (2, 3), "VS", loads_first=True)
-        begin(2)
-        mean(2, 0, True)
-        load_gd(3, 1, "gd2")
-        load_uw(4, 2, "uw4")
         load_ge(3, 1, 2)
-        load_uw(6, 2, "uw6")
+        load_uw(0, 2, "uw0")
         load_ge(3, 3, 2)
-        store_ready()
-        quantize_means(2, 0, 1)
-        stage2(1, (0, 1, 2, 3), "VS")
-        mean(2, 1, False)
-        mean(2, 2, True)
-        quantize_means(2, 1, 2)
-        mean(2, 3, False)
-        mean(2, 4, True)
-        quantize_means(2, 3, 2)
-        stage1(2, (0,), 0, 4)
-        stage1(2, (1, 2), 0, 4)
+        load_uw(2, 2, "uw2")
+        load_uw(4, 4, "uw4")
+        begin(0)
+        begin(1)
+        group_deep(0, "V")
+        group_deep(1, "V")
+        quantize_deep(0)
+        quantize_deep(1)
+        mean(0, 0, "V")
+        mean(1, 0, "V")
+        quantize_means(0, 0, 1)
+        quantize_means(1, 0, 1)
+        mean(0, 1, "A")
+        mean(0, 2, "S")
+        stage1(0, (0,))
+        quantize_means(0, 1, 2)
+        mean(0, 3, "V")
+        mean(0, 4, "S")
+        quantize_means(0, 3, 2)
+        stage1(0, (1, 2))
+        stage1(0, (3, 4))
+        relu(0, "SV")
+        mean(1, 1, "S")
+        mean(1, 2, "V")
+        turn_cam(0, "S")
+        quantize_means(1, 1, 2)
+        quantize_cam(0)
+        stage1(1, (0,))
+        mean(1, 3, "V")
+        mean(1, 4, "S")
+        quantize_means(1, 3, 1)
+        quantize_means(1, 4, 1)
+        stage1(1, (1, 2))
+        stage1(1, (3,))
+        stage1(1, (4,))
+        relu(1, "SV")
+        begin(2)
         begin(3)
-        add_cells((3, 0))
-        stage1(2, (3, 4), 0, 4)
-        relu(2)
-        add_pairs(3, 1)
-        stage2(0, (4, 5), "SS")
-        turn_cam(2, nc.scalar.copy)
-        turn_sums((3, 0))
-        add_pairs(3, 2)
-        quantize_cam(2)
+        mean(2, 0, "S")
+        mean(3, 0, "V")
+        quantize_means(2, 0, 1)
         quantize_means(3, 0, 1)
-        add_halves(3, 1)
-        add_halves(3, 2)
-        stage2(1, (4, 5))
-        stage2(0, (6, 7))
-        stage2(1, (6, 7), "SV")
-        mean(3, 3, True)
-        mean(3, 4, False)
-        turn_sums((3, 1), (3, 2))
-        quantize_means(3, 3, 2)
+        mean(2, 1, "S")
+        mean(2, 2, "V")
+        turn_cam(1, "S")
+        quantize_means(2, 1, 2)
+        quantize_cam(1)
+        stage1(2, (0,))
+        mean(2, 3, "V")
+        mean(2, 4, "S")
+        load_us(1, nc.scalar)
+        quantize_means(2, 3, 1)
+        quantize_means(2, 4, 1)
+        stage1(2, (1, 2))
+        add_cells((3, 1), (3, 2))
+        stage1(2, (3,))
+        stage1(2, (4,))
+        relu(2, "SS")
+        stage1(3, (0,))
+        stage2(0, (0, 1), "SS")
+        turn_cam(2, "V")
+        turn_sums("S", (3, 1), (3, 2))
+        quantize_cam(2)
+        stage2(1, (0, 1), "VS", width=2)
         quantize_means(3, 1, 2)
         stage2(2, (0, 1), "VS", width=2)
-        stage1(3, (0, 3, 4), 0, 2)
-        stage2(2, (2,), "V", width=2)
-        stage1(3, (1, 2), 0, 2)
-        relu(3)
-        stage2(2, (3, 4), "SV", width=2)
-        turn_cam(3, nc.scalar.copy)
+        add_pairs(3, 3)
+        stage1(3, (1, 2))
+        add_pairs(3, 4)
+        stage2(0, (2, 3), "SS")
+        add_halves(3, 3)
+        add_halves(3, 4)
+        stage2(1, (2, 3), "SS", width=2)
+        stage2(2, (2, 3), "VS", width=2)
+        turn_sums("V", (3, 3), (3, 4))
+        stage2(0, (4, 5), "SS")
+        quantize_means(3, 3, 2)
+        stage2(0, (6, 7), "VS")
+        stage1(3, (3, 4))
+        relu(3, "SV")
+        stage2(1, (4, 5), "SV", width=2)
+        turn_cam(3, "S")
+        stage2(1, (6, 7), "VS", width=2)
         quantize_cam(3)
-        stage2(2, (5, 6, 7), "SVS", width=2)
+        stage2(2, range(4, 8), "VS", width=2)
         stage2(3, range(6), "VS", width=2)
-        stage2(3, range(6, 8), "VS", width=1)
+        stage2(3, (6, 7), "VS", width=1)

@@ -203,10 +203,10 @@ def tile_two_layer_gradcam_s3_kernel(
                 in_=st[b]["means"][:, u0 * K : (u0 + n) * K],
             )
 
-        def stage1(b, units, first=0, last=4):
-            if first in units:
-                st[b]["z"] = [bank((b, h)) for h in range(GS)]
-            for h in range(GS):
+        def stage1(b, units, first=0, last=4, halves=range(GS)):
+            for h in halves:
+                if first in units:
+                    st[b]["z", h] = bank((b, h))
                 for u in units:
                     cols = slice(u * P, (u + 1) * P)
                     if u == 0:
@@ -216,7 +216,7 @@ def tile_two_layer_gradcam_s3_kernel(
                         rhs = ew[u - 1][:, h * 2 * K : (h + 1) * 2 * K].bitcast(FP4X4)
                         rhs_scale = es[:, u - 1, h * K : (h + 1) * K]
                     nc.tensor.matmul_mx(
-                        out=st[b]["z"][h][:],
+                        out=st[b]["z", h][:],
                         lhsT=st[b]["codes"][:, cols].bitcast(FP8X4),
                         lhsT_scale=st[b]["scales"][:, cols],
                         rhs=rhs,
@@ -229,7 +229,7 @@ def tile_two_layer_gradcam_s3_kernel(
             st[b]["cam"] = work.tile([P, S], BF16, name="cam", align_bytes=64)
             for h in range(GS):
                 dst = st[b]["cam"][:, h * K : (h + 1) * K].rearrange("m (v q e) -> m v q e", v=2, e=2)
-                src = st[b]["z"][h][:].rearrange("m (q v e) -> m v q e", v=2, e=2)
+                src = st[b]["z", h][:].rearrange("m (q v e) -> m v q e", v=2, e=2)
                 if on[h] == "S":
                     nc.scalar.activation(out=dst, in_=src, func=RELU, scale=1.0 / L)
                 else:
@@ -303,8 +303,8 @@ def tile_two_layer_gradcam_s3_kernel(
         load_ge(2, 3, 2)
         load_ge(3, 1, 2)
         load_uw(0, 2, "uw0")
-        load_ge(3, 3, 2)
         load_uw(2, 2, "uw2")
+        load_ge(3, 3, 2)
         load_uw(4, 4, "uw4")
         begin(0)
         begin(1)
@@ -323,6 +323,7 @@ def tile_two_layer_gradcam_s3_kernel(
         mean(0, 3, "V")
         mean(0, 4, "S")
         quantize_means(0, 3, 2)
+        stage1(1, (0,), halves=(0,))
         stage1(0, (1, 2))
         stage1(0, (3, 4))
         relu(0, "SV")
@@ -331,7 +332,7 @@ def tile_two_layer_gradcam_s3_kernel(
         turn_cam(0, "S")
         quantize_means(1, 1, 2)
         quantize_cam(0)
-        stage1(1, (0,))
+        stage1(1, (0,), halves=(1,))
         mean(1, 3, "V")
         mean(1, 4, "S")
         quantize_means(1, 3, 1)
@@ -358,36 +359,39 @@ def tile_two_layer_gradcam_s3_kernel(
         quantize_means(2, 3, 1)
         quantize_means(2, 4, 1)
         stage1(2, (1, 2))
-        add_cells((3, 1), (3, 2))
+        add_pairs(3, 1)
+        add_pairs(3, 2)
         stage1(2, (3,))
         stage1(2, (4,))
         relu(2, "SS")
-        stage1(3, (0,))
         stage2(0, (0, 1), "SS")
-        turn_cam(2, "V")
-        turn_sums("S", (3, 1), (3, 2))
+        turn_cam(2, "S")
+        add_halves(3, 1)
+        add_halves(3, 2)
         quantize_cam(2)
-        stage2(1, (0, 1), "VS", width=2)
+        stage2(1, (0, 1), "SS", width=2)
+        turn_sums("V", (3, 1), (3, 2))
+        stage2(2, (0, 1), "SS", width=2)
         quantize_means(3, 1, 2)
-        stage2(2, (0, 1), "VS", width=2)
+        stage1(3, (0,))
+        stage2(0, (2, 3), "SS")
         add_pairs(3, 3)
         stage1(3, (1, 2))
         add_pairs(3, 4)
-        stage2(0, (2, 3), "SS")
+        stage2(1, (2, 3), "SS", width=2)
         add_halves(3, 3)
         add_halves(3, 4)
-        stage2(1, (2, 3), "SS", width=2)
-        stage2(2, (2, 3), "VS", width=2)
-        turn_sums("V", (3, 3), (3, 4))
-        stage2(0, (4, 5), "SS")
-        quantize_means(3, 3, 2)
+        stage2(2, (2, 3), "SS", width=2)
+        stage2(0, (4, 5), "SV")
+        turn_sums("S", (3, 3), (3, 4))
         stage2(0, (6, 7), "VS")
+        quantize_means(3, 3, 2)
+        stage2(1, (4, 5), "VS", width=2)
         stage1(3, (3, 4))
         relu(3, "SV")
-        stage2(1, (4, 5), "SV", width=2)
+        stage2(1, (6, 7), "SV", width=2)
         turn_cam(3, "S")
-        stage2(1, (6, 7), "VS", width=2)
+        stage2(2, (4, 5), "VS", width=2)
         quantize_cam(3)
-        stage2(2, range(4, 8), "VS", width=2)
-        stage2(3, range(6), "VS", width=2)
-        stage2(3, (6, 7), "VS", width=1)
+        stage2(2, (6, 7), "VS", width=2)
+        stage2(3, range(8), "VS", width=2)

@@ -26,6 +26,7 @@ STRIPS = NPIX // K
 UNITS = 1 + GE
 US_CUTS = (0, 2, 8)
 ON_VECTOR = {(3, 1), (3, 2), (3, 3), (3, 4)}
+MOVING, MOVING_SCALE, STILL, STILL_SCALE = 0, 128, 64, 192
 FLOPS = 2 * M * (CD + CE) * S + 2 * M * S * NPIX
 
 
@@ -44,16 +45,21 @@ def tile_two_layer_gradcam_s3_kernel(
         work = ctx.enter_context(tc.tile_pool(name="work", bufs=2))
         psum = ctx.enter_context(tc.psum_pool(name="psum", bufs=1))
 
+        def placed(pool, shape, dtype, size, at, **kw):
+            count = shape[1] if len(shape) == 2 else shape[1] * shape[2]
+            flat = pool.tile([P, at // size + count], dtype, align_bytes=256, **kw)[:, at // size :]
+            return flat if len(shape) == 2 else flat.rearrange("p (g n) -> p g n", g=shape[1])
+
         ident = keep.tile([P, P], F32, align_bytes=64)
         pick = keep.tile([P, 32], BF16, align_bytes=64)
         deep_raw = keep.tile([P, 4, S], BF16, name="deep_raw", align_bytes=64)
         deep_grouped = keep.tile([P, S * 4], BF16, align_bytes=64)
-        deep_codes = keep.tile([P, S], U32, align_bytes=64)
-        deep_scales = keep.tile([P, S], U8, align_bytes=64)
+        deep_codes = placed(keep, [P, S], U32, 4, MOVING, name="deep_codes")
+        deep_scales = placed(keep, [P, S], U8, 1, MOVING_SCALE, name="deep_scales")
         ew = {}
-        es = keep.tile([P, GE, S], U8, align_bytes=64)
+        es = placed(keep, [P, GE, S], U8, 1, MOVING_SCALE, name="es")
         uw = {}
-        us = [keep.tile([P, GS, (US_CUTS[h + 1] - US_CUTS[h]) * K], U8, name="us%d" % h, align_bytes=64) for h in range(len(US_CUTS) - 1)]
+        us = [placed(keep, [P, GS, (US_CUTS[h + 1] - US_CUTS[h]) * K], U8, 1, MOVING_SCALE, name="us%d" % h) for h in range(len(US_CUTS) - 1)]
         gd = {}
         ge = {}
 
@@ -79,13 +85,13 @@ def tile_two_layer_gradcam_s3_kernel(
                 )
 
         def load_ew(g0, count, slot=None):
-            piece = keep.tile([P, count, 2 * S], U8, name=slot or "ew%d" % g0, align_bytes=64)
+            piece = placed(keep, [P, count, 2 * S], U8, 1, MOVING, name=slot or "ew%d" % g0)
             for g in range(g0, g0 + count):
                 ew[g] = piece[:, g - g0, :]
             nc.sync.dma_start(out=piece[:].bitcast(I32), in_=early_words[g0 : g0 + count].rearrange("g p n -> p g n").bitcast(I32))
 
         def load_uw(n0, count, slot):
-            piece = keep.tile([P, GS, count * 2 * K], U8, name=slot, align_bytes=64)
+            piece = placed(keep, [P, GS, count * 2 * K], U8, 1, MOVING, name=slot)
             for n in range(n0, n0 + count):
                 uw[n] = piece[:, :, (n - n0) * 2 * K : (n - n0 + 1) * 2 * K]
             nc.sync.dma_start(
@@ -147,8 +153,8 @@ def tile_two_layer_gradcam_s3_kernel(
         def begin(b):
             st[b] = {
                 "means": work.tile([P, UNITS * K], BF16, name="means", align_bytes=64),
-                "codes": work.tile([P, UNITS * P], U32, name="codes", bufs=4, align_bytes=64),
-                "scales": work.tile([P, UNITS * P], U8, name="scales", bufs=4, align_bytes=64),
+                "codes": placed(work, [P, UNITS * P], U32, 4, STILL, name="codes", bufs=4),
+                "scales": placed(work, [P, UNITS * P], U8, 1, STILL_SCALE, name="scales", bufs=4),
             }
 
         def mean(b, u, on):
@@ -250,8 +256,8 @@ def tile_two_layer_gradcam_s3_kernel(
             st[b]["grouped"] = grouped
 
         def quantize_cam(b):
-            st[b]["cam_codes"] = work.tile([P, GS * P], U32, name="cam_codes", bufs=4, align_bytes=64)
-            st[b]["cam_scales"] = work.tile([P, GS * P], U8, name="cam_scales", bufs=4, align_bytes=64)
+            st[b]["cam_codes"] = placed(work, [P, GS * P], U32, 4, STILL, name="cam_codes", bufs=4)
+            st[b]["cam_scales"] = placed(work, [P, GS * P], U8, 1, STILL_SCALE, name="cam_scales", bufs=4)
             nc.vector.quantize_mx(out=st[b]["cam_codes"][:].bitcast(FP8X4), scales=st[b]["cam_scales"][:], in_=st[b]["grouped"][:])
 
         def store_ready(queue):

@@ -50,10 +50,10 @@ def tile_two_layer_gradcam_s3_kernel(
             flat = pool.tile([P, at // size + count], dtype, align_bytes=256, **kw)[:, at // size :]
             return flat if len(shape) == 2 else flat.rearrange("p (g n) -> p g n", g=shape[1])
 
-        ident = keep.tile([P, P], F32, align_bytes=64)
-        pick = keep.tile([P, 32], BF16, align_bytes=64)
-        deep_raw = keep.tile([P, 4, S], BF16, name="deep_raw", align_bytes=64)
-        deep_grouped = keep.tile([P, S * 4], BF16, align_bytes=64)
+        ident = keep.tile([P, P], F32, align_bytes=256)
+        pick = keep.tile([P, 32], BF16, align_bytes=256)
+        deep_raw = keep.tile([P, 4, S], BF16, name="deep_raw", align_bytes=256)
+        deep_grouped = keep.tile([P, S * 4], BF16, align_bytes=256)
         deep_codes = placed(keep, [P, S], U32, 4, MOVING, name="deep_codes")
         deep_scales = placed(keep, [P, S], U8, 1, MOVING_SCALE, name="deep_scales")
         ew = {}
@@ -66,13 +66,13 @@ def tile_two_layer_gradcam_s3_kernel(
         ctx.enter_context(tc.manual_schedule())
 
         def load_gd(b0, n, slot):
-            piece = keep.tile([P, 4, n * CD], BF16, name=slot, align_bytes=64)
+            piece = keep.tile([P, 4, n * CD], BF16, name=slot, align_bytes=256)
             for b in range(b0, b0 + n):
                 gd[b] = piece[:, :, (b - b0) * CD : (b - b0 + 1) * CD]
             nc.sync.dma_start(out=piece[:], in_=(gd_rows if (b0, 0) in ON_VECTOR else gd_view)[:, :, b0 * CD : (b0 + n) * CD])
 
         def load_ge(b, u0, n, slot=None):
-            piece = keep.tile([P, 4, n * K], BF16, name=slot or "ge%d_%d" % (b, u0), align_bytes=64)
+            piece = keep.tile([P, 4, n * K], BF16, name=slot or "ge%d_%d" % (b, u0), align_bytes=256)
             for u in range(u0, u0 + n):
                 ge[b, u] = piece[:, :, (u - u0) * K : (u - u0 + 1) * K]
             nc.sync.dma_start(out=piece[:], in_=(ge_rows if (b, u0) in ON_VECTOR else ge_view)[b][:, :, (u0 - 1) * K : (u0 - 1 + n) * K])
@@ -152,7 +152,7 @@ def tile_two_layer_gradcam_s3_kernel(
 
         def begin(b):
             st[b] = {
-                "means": work.tile([P, UNITS * K], BF16, name="means", align_bytes=64),
+                "means": work.tile([P, UNITS * K], BF16, name="means", align_bytes=256),
                 "codes": placed(work, [P, UNITS * P], U32, 4, STILL, name="codes", bufs=4),
                 "scales": placed(work, [P, UNITS * P], U8, 1, STILL_SCALE, name="scales", bufs=4),
             }
@@ -173,11 +173,11 @@ def tile_two_layer_gradcam_s3_kernel(
 
         def add_pairs(b, u):
             source = gd[b] if u == 0 else ge[b, u]
-            pairs[b, u] = work.tile([P, 2, K], F32, name="pairs", align_bytes=64)
+            pairs[b, u] = work.tile([P, 2, K], F32, name="pairs", align_bytes=256)
             nc.vector.tensor_tensor(out=pairs[b, u][:], in0=source[:, 0:2, :], in1=source[:, 2:4, :], op=ADD)
 
         def add_halves(b, u):
-            summed[b, u] = work.tile([P, K], BF16, name="summed", bufs=4, align_bytes=64)
+            summed[b, u] = work.tile([P, K], BF16, name="summed", bufs=4, align_bytes=256)
             halves = [pairs[b, u][:, h, :].rearrange("q (p v e) -> q v p e", v=2, e=2) for h in range(2)]
             nc.vector.tensor_tensor(
                 out=summed[b, u][:].rearrange("q (v p e) -> q v p e", v=2, e=2), in0=halves[0], in1=halves[1], op=ADD
@@ -232,7 +232,7 @@ def tile_two_layer_gradcam_s3_kernel(
                     )
 
         def relu(b, on):
-            st[b]["cam"] = work.tile([P, S], BF16, name="cam", align_bytes=64)
+            st[b]["cam"] = work.tile([P, S], BF16, name="cam", align_bytes=256)
             for h in range(GS):
                 dst = st[b]["cam"][:, h * K : (h + 1) * K].rearrange("m (v q e) -> m v q e", v=2, e=2)
                 src = st[b]["z", h][:].rearrange("m (q v e) -> m v q e", v=2, e=2)
@@ -247,7 +247,7 @@ def tile_two_layer_gradcam_s3_kernel(
             words = st[b]["cam"][:].bitcast(F32)
             for i in range(4):
                 nc.tensor.transpose(turned[:, i * P : (i + 1) * P], words[:, i * P : (i + 1) * P], ident[:])
-            grouped = work.tile([P, S], BF16, name="grouped", align_bytes=64)
+            grouped = work.tile([P, S], BF16, name="grouped", align_bytes=256)
             engine_copy(on)(
                 out=grouped[:].bitcast(F32).rearrange("p (g m v) -> p g m v", g=GS, v=2),
                 in_=turned[:].rearrange("p (g v m) -> p g m v", g=GS, v=2),
@@ -281,7 +281,7 @@ def tile_two_layer_gradcam_s3_kernel(
                         stop=(g == GS - 1),
                     )
                 if n % 4 == 0:
-                    st[b]["staged", n // 4] = keep.tile([P, 4 * K], F32, name=spent.pop(0), align_bytes=64)
+                    st[b]["staged", n // 4] = keep.tile([P, 4 * K], F32, name=spent.pop(0), align_bytes=256)
                 staged = st[b]["staged", n // 4]
                 engine_copy(engine)(out=staged[:, (n % 4) * K : (n % 4 + 1) * K], in_=acc[:])
                 release("strip")

@@ -22,22 +22,20 @@ K = 512
 BANDS = M // P
 GE = CE // K
 GS = S // K
-STRIPS = NPIX // K
 UNITS = 1 + GE
-US_CUTS = (0, 2, 8)
-ON_VECTOR = {(3, 1), (3, 2), (3, 3), (3, 4)}
 MOVING, MOVING_SCALE, STILL, STILL_SCALE = 0, 128, 64, 192
 FLOPS = 2 * M * (CD + CE) * S + 2 * M * S * NPIX
+ON_VECTOR = {(3, 1), (3, 2), (3, 3), (3, 4)}
 
 
 def tile_two_layer_gradcam_s3_kernel(
     tc, grad_deep, grad_early, deep, early_words, early_scales, up_words, up_scales, out
 ):
     nc = tc.nc
-    gd_view = grad_deep.rearrange("l (i j b) k -> (l i) j (b k)", j=4, b=BANDS)
-    ge_view = grad_early.rearrange("l (i j b) k -> b (l i) j k", j=4, b=BANDS)
-    gd_rows = grad_deep.rearrange("l (q b) k -> q l (b k)", b=BANDS)
-    ge_rows = grad_early.rearrange("l (q b) k -> b q l k", b=BANDS)
+    gd_stacked = grad_deep.rearrange("l (i j b) k -> (l i) j (b k)", j=4, b=BANDS)
+    ge_stacked = grad_early.rearrange("l (i j b) k -> b (l i) j k", j=4, b=BANDS)
+    gd_by_target = grad_deep.rearrange("l (q b) k -> q l (b k)", b=BANDS)
+    ge_by_target = grad_early.rearrange("l (q b) k -> b q l k", b=BANDS)
     out_view = out.rearrange("(q b) n -> b q n", b=BANDS)
 
     with ExitStack() as ctx:
@@ -53,45 +51,43 @@ def tile_two_layer_gradcam_s3_kernel(
         ident = keep.tile([P, P], F32, align_bytes=256)
         pick = keep.tile([P, 32], BF16, align_bytes=256)
         deep_raw = keep.tile([P, 4, S], BF16, name="deep_raw", align_bytes=256)
-        deep_grouped = keep.tile([P, S * 4], BF16, align_bytes=256)
+        deep_grouped = keep.tile([P, S * 4], BF16, name="deep_grouped", align_bytes=256)
         deep_codes = placed(keep, [P, S], U32, 4, MOVING, name="deep_codes")
         deep_scales = placed(keep, [P, S], U8, 1, MOVING_SCALE, name="deep_scales")
-        ew = {}
         es = placed(keep, [P, GE, S], U8, 1, MOVING_SCALE, name="es")
-        uw = {}
-        us = [placed(keep, [P, GS, (US_CUTS[h + 1] - US_CUTS[h]) * K], U8, 1, MOVING_SCALE, name="us%d" % h) for h in range(len(US_CUTS) - 1)]
-        gd = {}
-        ge = {}
+        ew, uw, us, grad = {}, {}, {}, {}
 
         ctx.enter_context(tc.manual_schedule())
 
         def load_gd(b0, n, slot):
             piece = keep.tile([P, 4, n * CD], BF16, name=slot, align_bytes=256)
             for b in range(b0, b0 + n):
-                gd[b] = piece[:, :, (b - b0) * CD : (b - b0 + 1) * CD]
-            nc.sync.dma_start(out=piece[:], in_=(gd_rows if (b0, 0) in ON_VECTOR else gd_view)[:, :, b0 * CD : (b0 + n) * CD])
+                grad[b, 0] = piece[:, :, (b - b0) * CD : (b - b0 + 1) * CD]
+            view = gd_by_target if (b0, 0) in ON_VECTOR else gd_stacked
+            nc.sync.dma_start(out=piece[:], in_=view[:, :, b0 * CD : (b0 + n) * CD])
 
-        def load_ge(b, u0, n, slot=None):
-            piece = keep.tile([P, 4, n * K], BF16, name=slot or "ge%d_%d" % (b, u0), align_bytes=256)
+        def load_ge(b, u0, n, slot):
+            piece = keep.tile([P, 4, n * K], BF16, name=slot, align_bytes=256)
             for u in range(u0, u0 + n):
-                ge[b, u] = piece[:, :, (u - u0) * K : (u - u0 + 1) * K]
-            nc.sync.dma_start(out=piece[:], in_=(ge_rows if (b, u0) in ON_VECTOR else ge_view)[b][:, :, (u0 - 1) * K : (u0 - 1 + n) * K])
+                grad[b, u] = piece[:, :, (u - u0) * K : (u - u0 + 1) * K]
+            view = ge_by_target if (b, u0) in ON_VECTOR else ge_stacked
+            nc.sync.dma_start(out=piece[:], in_=view[b][:, :, (u0 - 1) * K : (u0 - 1 + n) * K])
 
-        def load_scales(plane, rows, queue):
+        def load_scales(plane, rows):
             for r in range(4):
-                queue.dma_start(
+                nc.scalar.dma_start(
                     out=plane[r:P:32, :, :].bitcast(I32),
                     in_=rows.rearrange("g (q r) n -> r q g n", r=4)[r].bitcast(I32),
                 )
 
-        def load_ew(g0, count, slot=None):
-            piece = placed(keep, [P, count, 2 * S], U8, 1, MOVING, name=slot or "ew%d" % g0)
+        def load_ew(g0, count):
+            piece = placed(keep, [P, count, 2 * S], U8, 1, MOVING, name="ew%d" % g0)
             for g in range(g0, g0 + count):
                 ew[g] = piece[:, g - g0, :]
             nc.sync.dma_start(out=piece[:].bitcast(I32), in_=early_words[g0 : g0 + count].rearrange("g p n -> p g n").bitcast(I32))
 
-        def load_uw(n0, count, slot):
-            piece = placed(keep, [P, GS, count * 2 * K], U8, 1, MOVING, name=slot)
+        def load_uw(n0, count, slot=None):
+            piece = placed(keep, [P, GS, count * 2 * K], U8, 1, MOVING, name=slot or "uw%d" % n0)
             for n in range(n0, n0 + count):
                 uw[n] = piece[:, :, (n - n0) * 2 * K : (n - n0 + 1) * 2 * K]
             nc.sync.dma_start(
@@ -99,11 +95,20 @@ def tile_two_layer_gradcam_s3_kernel(
                 in_=up_words[:, :, n0 * 2 * K : (n0 + count) * 2 * K].rearrange("g p n -> p g n").bitcast(I32),
             )
 
-        def load_us(h, queue):
-            load_scales(us[h], up_scales[:, :, US_CUTS[h] * K : US_CUTS[h + 1] * K], queue)
+        def load_us(n0, count):
+            plane = placed(keep, [P, GS, count * K], U8, 1, MOVING_SCALE, name="us%d" % n0)
+            for n in range(n0, n0 + count):
+                us[n] = plane[:, :, (n - n0) * K : (n - n0 + 1) * K]
+            load_scales(plane, up_scales[:, :, n0 * K : (n0 + count) * K])
 
         def load_deep():
             nc.sync.dma_start(out=deep_raw[:], in_=deep.rearrange("(p j) w -> p j w", j=4))
+
+        def copy_by_activation(out, in_):
+            nc.scalar.activation(out=out, in_=in_, func=COPY)
+
+        def engine_copy(on):
+            return {"V": nc.vector.tensor_copy, "S": nc.scalar.copy, "A": copy_by_activation}[on]
 
         def group_deep(h, on):
             engine_copy(on)(
@@ -118,11 +123,7 @@ def tile_two_layer_gradcam_s3_kernel(
                 in_=deep_grouped[:, h * K * 4 : (h + 1) * K * 4],
             )
 
-        st = {}
-        ready = []
-        spent = ["deep_raw", "gd01", "ge0_1", "ge0_3", "ge1_1", "ge1_3", "gd23", "ge2_1"]
-        pairs = {}
-        summed = {}
+        st, pairs, summed, staged = {}, {}, {}, {}
 
         free = list(range(8))
         held = {}
@@ -135,24 +136,15 @@ def tile_two_layer_gradcam_s3_kernel(
         def release(owner):
             free.append(held[owner])
 
-        def copy_by_activation(out, in_):
-            nc.scalar.activation(out=out, in_=in_, func=COPY)
-
-        def engine_copy(on):
-            return {"V": nc.vector.tensor_copy, "S": nc.scalar.copy, "A": copy_by_activation}[on]
-
-        def zero(plane):
-            nc.vector.memset(plane[:].rearrange("p g n -> p (g n)").bitcast(I32), 0)
-
         def constants():
             make_identity(nc, ident[:])
             for l in range(L):
                 rows = slice(32 * l, 32 * l + 32)
                 nc.vector.tensor_copy(out=pick[rows, :], in_=ident[rows, rows])
 
-        def begin(b):
+        def begin(b, slot):
             st[b] = {
-                "means": work.tile([P, UNITS * K], BF16, name="means", align_bytes=256),
+                "means": keep.tile([P, UNITS * K], BF16, name=slot, align_bytes=256),
                 "codes": placed(work, [P, UNITS * P], U32, 4, STILL, name="codes", bufs=4),
                 "scales": placed(work, [P, UNITS * P], U8, 1, STILL_SCALE, name="scales", bufs=4),
             }
@@ -161,20 +153,17 @@ def tile_two_layer_gradcam_s3_kernel(
             acc = bank("mean")
             for t in range(4):
                 for j in range(4):
-                    if u == 0:
-                        cols = gd[b][:, j, t:CD:4]
-                    else:
-                        cols = ge[b, u][:, j, t:K:4]
-                    nc.tensor.matmul(acc[:, t * P + 32 * j : t * P + 32 * j + 32], lhsT=cols, rhs=pick[:], start=True, stop=True)
+                    nc.tensor.matmul(
+                        acc[:, t * P + 32 * j : t * P + 32 * j + 32], lhsT=grad[b, u][:, j, t:K:4], rhs=pick[:], start=True, stop=True
+                    )
             dst = st[b]["means"][:, u * K : (u + 1) * K].rearrange("p (i j t) -> p i j t", j=4, t=4)
             src = acc[:].rearrange("p (t j i) -> p i j t", t=4, j=4)
             engine_copy(on)(out=dst, in_=src)
             release("mean")
 
         def add_pairs(b, u):
-            source = gd[b] if u == 0 else ge[b, u]
             pairs[b, u] = work.tile([P, 2, K], F32, name="pairs", align_bytes=256)
-            nc.vector.tensor_tensor(out=pairs[b, u][:], in0=source[:, 0:2, :], in1=source[:, 2:4, :], op=ADD)
+            nc.vector.tensor_tensor(out=pairs[b, u][:], in0=grad[b, u][:, 0:2, :], in1=grad[b, u][:, 2:4, :], op=ADD)
 
         def add_halves(b, u):
             summed[b, u] = work.tile([P, K], BF16, name="summed", bufs=4, align_bytes=256)
@@ -182,12 +171,6 @@ def tile_two_layer_gradcam_s3_kernel(
             nc.vector.tensor_tensor(
                 out=summed[b, u][:].rearrange("q (v p e) -> q v p e", v=2, e=2), in0=halves[0], in1=halves[1], op=ADD
             )
-
-        def add_cells(*units):
-            for b, u in units:
-                add_pairs(b, u)
-            for b, u in units:
-                add_halves(b, u)
 
         def turn_sums(on, *units):
             turned = bank("sums")
@@ -202,16 +185,17 @@ def tile_two_layer_gradcam_s3_kernel(
                 )
             release("sums")
 
-        def quantize_means(b, u0, n):
+        def quantize_means(b, u0, n=1):
             nc.vector.quantize_mx(
                 out=st[b]["codes"][:, u0 * P : (u0 + n) * P].bitcast(FP8X4),
                 scales=st[b]["scales"][:, u0 * P : (u0 + n) * P],
                 in_=st[b]["means"][:, u0 * K : (u0 + n) * K],
             )
 
-        def stage1(b, units, first=0, last=4, halves=range(GS)):
+        def stage1(b, *units, halves=range(GS)):
             for h in halves:
-                if first in units:
+                done = st[b].setdefault(("done", h), [])
+                if not done:
                     st[b]["z", h] = bank((b, h))
                 for u in units:
                     cols = slice(u * P, (u + 1) * P)
@@ -227,12 +211,16 @@ def tile_two_layer_gradcam_s3_kernel(
                         lhsT_scale=st[b]["scales"][:, cols],
                         rhs=rhs,
                         rhs_scale=rhs_scale,
-                        start=(u == first),
-                        stop=(u == last),
+                        start=(len(done) == 0),
+                        stop=(len(done) == UNITS - 1),
                     )
+                    done.append(u)
 
-        def relu(b, on):
-            st[b]["cam"] = work.tile([P, S], BF16, name="cam", align_bytes=256)
+        def relu(b, on, slot=None):
+            if slot:
+                st[b]["cam"] = keep.tile([P, S], BF16, name=slot, align_bytes=256)
+            else:
+                st[b]["cam"] = work.tile([P, S], BF16, name="cam", align_bytes=256)
             for h in range(GS):
                 dst = st[b]["cam"][:, h * K : (h + 1) * K].rearrange("m (v q e) -> m v q e", v=2, e=2)
                 src = st[b]["z", h][:].rearrange("m (q v e) -> m v q e", v=2, e=2)
@@ -242,12 +230,15 @@ def tile_two_layer_gradcam_s3_kernel(
                     nc.vector.tensor_scalar(out=dst, in0=src, scalar1=0.0, scalar2=1.0 / L, op0=MAX, op1=MULT)
                 release((b, h))
 
-        def turn_cam(b, on):
+        def turn_cam(b, on, slot=None):
             turned = bank("cam")
             words = st[b]["cam"][:].bitcast(F32)
             for i in range(4):
                 nc.tensor.transpose(turned[:, i * P : (i + 1) * P], words[:, i * P : (i + 1) * P], ident[:])
-            grouped = work.tile([P, S], BF16, name="grouped", align_bytes=256)
+            if slot:
+                grouped = keep.tile([P, S], BF16, name=slot, align_bytes=256)
+            else:
+                grouped = work.tile([P, S], BF16, name="grouped", align_bytes=256)
             engine_copy(on)(
                 out=grouped[:].bitcast(F32).rearrange("p (g m v) -> p g m v", g=GS, v=2),
                 in_=turned[:].rearrange("p (g v m) -> p g m v", g=GS, v=2),
@@ -260,144 +251,164 @@ def tile_two_layer_gradcam_s3_kernel(
             st[b]["cam_scales"] = placed(work, [P, GS * P], U8, 1, STILL_SCALE, name="cam_scales", bufs=4)
             nc.vector.quantize_mx(out=st[b]["cam_codes"][:].bitcast(FP8X4), scales=st[b]["cam_scales"][:], in_=st[b]["grouped"][:])
 
-        def store_ready(queue):
-            for rows, source in ready:
-                queue.dma_start(out=rows, in_=source)
-            ready.clear()
-
-        def stage2(b, strips, on="S", width=4, queues="Y"):
-            stores = 0
-            for n, engine in zip(strips, on * len(strips)):
+        def stage2(b, strips, on):
+            for n, engine in zip(strips, on):
                 acc = bank("strip")
-                run = max(h for h in range(len(us)) if US_CUTS[h] <= n)
                 for g in range(GS):
                     nc.tensor.matmul_mx(
                         out=acc[:],
                         lhsT=st[b]["cam_codes"][:, g * P : (g + 1) * P].bitcast(FP8X4),
                         lhsT_scale=st[b]["cam_scales"][:, g * P : (g + 1) * P],
                         rhs=uw[n][:, g, :].bitcast(FP4X4),
-                        rhs_scale=us[run][:, g, (n - US_CUTS[run]) * K : (n - US_CUTS[run] + 1) * K],
+                        rhs_scale=us[n][:, g, :],
                         start=(g == 0),
                         stop=(g == GS - 1),
                     )
                 if n % 4 == 0:
-                    st[b]["staged", n // 4] = keep.tile([P, 4 * K], F32, name=spent.pop(0), align_bytes=256)
-                staged = st[b]["staged", n // 4]
-                engine_copy(engine)(out=staged[:, (n % 4) * K : (n % 4 + 1) * K], in_=acc[:])
+                    staged[b, n // 4] = keep.tile([P, 4 * K], F32, name=spent.pop(0), align_bytes=256)
+                engine_copy(engine)(out=staged[b, n // 4][:, (n % 4) * K : (n % 4 + 1) * K], in_=acc[:])
                 release("strip")
-                if n % width == width - 1:
-                    lo = n + 1 - width
-                    ready.append((out_view[b][:, lo * K : (n + 1) * K], staged[:, (lo % 4) * K : (n % 4 + 1) * K]))
-                    store_ready(nc.sync if queues[stores % len(queues)] == "Y" else nc.scalar)
-                    stores = stores + 1
 
-        zero(es)
-        zero(us[0])
+        def store(b, n0, count):
+            nc.sync.dma_start(
+                out=out_view[b][:, n0 * K : (n0 + count) * K], in_=staged[b, n0 // 4][:, (n0 % 4) * K : (n0 % 4 + count) * K]
+            )
+
+        spent = ["deep_raw", "g0a", "deep_grouped", "gd01", "g1b", "gd23", "g2a", "g2b"]
         load_deep()
+        load_scales(es, early_scales)
+        load_ge(0, 1, 2, "g0a")
+        load_ew(0, 2)
         load_gd(0, 2, "gd01")
-        load_ge(0, 1, 2)
-        load_scales(es, early_scales, nc.scalar)
-        load_us(0, nc.scalar)
-        constants()
-        zero(us[1])
-        load_ge(0, 3, 2)
-        load_ew(0, 4)
-        load_ge(1, 1, 2)
-        load_ge(1, 3, 2)
+        load_ew(2, 2)
+        load_ge(0, 3, 1, "g03")
+        load_ge(0, 4, 1, "g04")
+        load_ge(1, 1, 1, "g11")
+        load_ge(1, 2, 1, "g12")
+        load_ge(1, 3, 2, "g1b")
         load_gd(2, 2, "gd23")
-        load_ge(2, 1, 2)
-        load_ge(2, 3, 2)
-        load_ge(3, 1, 2)
-        load_uw(0, 2, "uw0")
-        load_uw(2, 2, "uw2")
-        load_ge(3, 3, 2)
-        load_uw(4, 4, "uw4")
-        begin(0)
-        begin(1)
+        load_ge(2, 1, 2, "g2a")
+        load_ge(2, 3, 2, "g2b")
+        load_uw(0, 2)
+        constants()
+        begin(0, "means0")
+        begin(1, "means1")
         group_deep(0, "V")
         group_deep(1, "V")
-        quantize_deep(0)
-        quantize_deep(1)
-        mean(0, 0, "V")
-        mean(1, 0, "V")
-        quantize_means(0, 0, 1)
-        quantize_means(1, 0, 1)
         mean(0, 1, "A")
         mean(0, 2, "S")
-        stage1(0, (0,))
-        quantize_means(0, 1, 2)
-        mean(0, 3, "V")
+        quantize_deep(0)
+        quantize_deep(1)
+        quantize_means(0, 1)
+        quantize_means(0, 2)
+        stage1(0, 1, 2)
+        mean(0, 0, "S")
+        mean(1, 0, "S")
+        quantize_means(0, 0)
+        mean(0, 3, "S")
+        quantize_means(1, 0)
+        stage1(0, 0)
         mean(0, 4, "S")
-        quantize_means(0, 3, 2)
-        stage1(1, (0,), halves=(0,))
-        stage1(0, (1, 2))
-        stage1(0, (3, 4))
-        relu(0, "SV")
+        quantize_means(0, 3)
+        stage1(1, 0)
         mean(1, 1, "S")
-        mean(1, 2, "V")
-        turn_cam(0, "S")
-        quantize_means(1, 1, 2)
+        quantize_means(0, 4)
+        stage1(0, 3)
+        stage1(0, 4)
+        quantize_means(1, 1)
+        relu(0, "SV")
+        mean(1, 2, "S")
+        stage1(1, 1)
+        quantize_means(1, 2)
+        turn_cam(0, "V")
+        mean(1, 3, "S")
+        stage1(1, 2)
         quantize_cam(0)
-        stage1(1, (0,), halves=(1,))
-        mean(1, 3, "V")
         mean(1, 4, "S")
-        quantize_means(1, 3, 1)
-        quantize_means(1, 4, 1)
-        stage1(1, (1, 2))
-        stage1(1, (3,))
-        stage1(1, (4,))
-        relu(1, "SV")
-        begin(2)
-        begin(3)
+        quantize_means(1, 3)
+        begin(2, "means2")
+        begin(3, "means0")
+        stage1(1, 3)
+        quantize_means(1, 4)
         mean(2, 0, "S")
-        mean(3, 0, "V")
-        quantize_means(2, 0, 1)
-        quantize_means(3, 0, 1)
+        stage1(1, 4)
+        relu(1, "SV")
+        quantize_means(2, 0)
+        mean(3, 0, "S")
         mean(2, 1, "S")
-        mean(2, 2, "V")
-        turn_cam(1, "S")
-        quantize_means(2, 1, 2)
+        quantize_means(3, 0)
+        load_us(0, 4)
+        turn_cam(1, "S", "held")
+        mean(2, 2, "S")
+        quantize_means(2, 1)
+        stage1(2, 0)
         quantize_cam(1)
-        stage1(2, (0,))
-        mean(2, 3, "V")
-        mean(2, 4, "S")
-        load_us(1, nc.scalar)
-        quantize_means(2, 3, 1)
-        quantize_means(2, 4, 1)
-        stage1(2, (1, 2))
-        add_pairs(3, 1)
-        add_pairs(3, 2)
-        stage1(2, (3,))
-        stage1(2, (4,))
-        relu(2, "SS")
+        load_ge(3, 1, 2, "held")
+        load_uw(2, 2)
+        load_ge(3, 3, 2, "g3b")
+        stage1(3, 0)
+        quantize_means(2, 2)
+        mean(2, 3, "S")
+        mean(2, 4, "V")
+        stage1(2, 1, 2)
+        quantize_means(2, 3)
+        quantize_means(2, 4)
+        stage1(2, 3)
+        stage1(2, 4)
+        relu(2, "SV")
         stage2(0, (0, 1), "SS")
+        store(0, 0, 2)
+        load_uw(4, 4)
+        add_pairs(3, 1)
         turn_cam(2, "S")
+        load_us(4, 4)
+        add_pairs(3, 2)
+        stage2(1, (0, 1), "SS")
+        store(1, 0, 2)
+        quantize_cam(2)
         add_halves(3, 1)
         add_halves(3, 2)
-        quantize_cam(2)
-        stage2(1, (0, 1), "SS", width=2)
-        turn_sums("V", (3, 1), (3, 2))
-        stage2(2, (0, 1), "SS", width=2)
-        quantize_means(3, 1, 2)
-        stage1(3, (0,))
         stage2(0, (2, 3), "SS")
+        store(0, 2, 2)
         add_pairs(3, 3)
-        stage1(3, (1, 2))
+        stage2(1, (2, 3), "SS")
+        store(1, 2, 2)
+        stage2(2, (0, 1), "SS")
+        turn_sums("S", (3, 1), (3, 2))
+        stage2(2, (2, 3), "SS")
+        store(2, 0, 4)
+        quantize_means(3, 1, 2)
         add_pairs(3, 4)
-        stage2(1, (2, 3), "SS", width=2)
         add_halves(3, 3)
         add_halves(3, 4)
-        stage2(2, (2, 3), "SS", width=2)
-        stage2(0, (4, 5), "SV")
-        turn_sums("S", (3, 3), (3, 4))
-        stage2(0, (6, 7), "VS")
+        stage2(0, (4, 5), "SS")
+        store(0, 4, 2)
+        stage1(3, 1, 2)
+        stage2(0, (6, 7), "SS")
+        store(0, 6, 2)
+        turn_sums("V", (3, 3), (3, 4))
+        stage2(1, (4, 5), "SS")
+        store(1, 4, 2)
         quantize_means(3, 3, 2)
-        stage2(1, (4, 5), "VS", width=2)
-        stage1(3, (3, 4))
+        stage2(1, (6,), "V")
+        stage1(3, 3, 4)
         relu(3, "SV")
-        stage2(1, (6, 7), "SV", width=2)
-        turn_cam(3, "S")
-        stage2(2, (4, 5), "VS", width=2)
+        stage2(1, (7,), "S")
+        store(1, 6, 2)
+        stage2(2, (4,), "V")
+        turn_cam(3, "V")
+        stage2(2, (5, 6), "SS")
+        store(2, 4, 2)
         quantize_cam(3)
-        stage2(2, (6, 7), "VS", width=2)
-        stage2(3, range(8), "VS", width=2)
+        stage2(2, (7,), "V")
+        store(2, 6, 2)
+        stage2(3, (0, 1), "SV")
+        store(3, 0, 2)
+        stage2(3, (2, 3), "SV")
+        store(3, 2, 2)
+        stage2(3, (4, 5), "SV")
+        store(3, 4, 2)
+        stage2(3, (6,), "S")
+        store(3, 6, 1)
+        stage2(3, (7,), "V")
+        store(3, 7, 1)

@@ -277,11 +277,12 @@ def tile_two_layer_gradcam_s3_kernel(
         spent = ["deep_raw", "g0a", "deep_grouped", "gd01", "g1b", "gd23", "g2a", "g2b"]
         load_deep()
         load_scales(es, early_scales)
-        load_ge(0, 1, 2, "g0a")
+        load_ge(0, 1, 1, "g01")
         load_ew(0, 2)
+        load_ge(0, 2, 1, "g0a")
         load_gd(0, 2, "gd01")
-        load_ew(2, 2)
         load_ge(0, 3, 1, "g03")
+        load_ew(2, 2)
         load_ge(0, 4, 1, "g04")
         load_ge(1, 1, 1, "g11")
         load_ge(1, 2, 1, "g12")
@@ -296,24 +297,25 @@ def tile_two_layer_gradcam_s3_kernel(
         group_deep(0, "V")
         group_deep(1, "V")
         mean(0, 1, "A")
-        mean(0, 2, "S")
+        quantize_means(0, 1)
         quantize_deep(0)
         quantize_deep(1)
-        quantize_means(0, 1)
-        quantize_means(0, 2)
-        stage1(0, 1, 2)
+        stage1(0, 1)
+        mean(0, 2, "S")
         mean(0, 0, "S")
+        quantize_means(0, 2)
         mean(1, 0, "S")
         quantize_means(0, 0)
         mean(0, 3, "S")
         quantize_means(1, 0)
+        stage1(0, 2)
         stage1(0, 0)
-        mean(0, 4, "S")
         quantize_means(0, 3)
         stage1(1, 0)
+        mean(0, 4, "S")
+        stage1(0, 3)
         mean(1, 1, "S")
         quantize_means(0, 4)
-        stage1(0, 3)
         stage1(0, 4)
         quantize_means(1, 1)
         relu(0, "SV")
@@ -346,6 +348,7 @@ def tile_two_layer_gradcam_s3_kernel(
         load_ge(3, 1, 2, "held")
         load_uw(2, 2)
         load_ge(3, 3, 2, "g3b")
+        load_uw(4, 4)
         stage1(3, 0)
         quantize_means(2, 2)
         mean(2, 3, "S")
@@ -355,13 +358,12 @@ def tile_two_layer_gradcam_s3_kernel(
         quantize_means(2, 4)
         stage1(2, 3)
         stage1(2, 4)
+        load_us(4, 4)
         relu(2, "SV")
         stage2(0, (0, 1), "SS")
         store(0, 0, 2)
-        load_uw(4, 4)
         add_pairs(3, 1)
         turn_cam(2, "S")
-        load_us(4, 4)
         add_pairs(3, 2)
         stage2(1, (0, 1), "SS")
         store(1, 0, 2)

@@ -142,12 +142,16 @@ def tile_two_layer_gradcam_s3_kernel(
                 rows = slice(32 * l, 32 * l + 32)
                 nc.vector.tensor_copy(out=pick[rows, :], in_=ident[rows, rows])
 
-        def begin(b, slot):
+        def begin(b, slot, deep_slot):
             st[b] = {
-                "means": keep.tile([P, UNITS * K], BF16, name=slot, align_bytes=256),
+                "means": keep.tile([P, GE * K], BF16, name=slot, align_bytes=256),
+                "deep_means": keep.tile([P, K], BF16, name=deep_slot, align_bytes=256),
                 "codes": placed(work, [P, UNITS * P], U32, 4, STILL, name="codes", bufs=4),
                 "scales": placed(work, [P, UNITS * P], U8, 1, STILL_SCALE, name="scales", bufs=4),
             }
+
+        def means_of(b, u0, n=1):
+            return st[b]["deep_means"][:] if u0 == 0 else st[b]["means"][:, (u0 - 1) * K : (u0 - 1 + n) * K]
 
         def mean(b, u, on):
             acc = bank("mean")
@@ -156,7 +160,7 @@ def tile_two_layer_gradcam_s3_kernel(
                     nc.tensor.matmul(
                         acc[:, t * P + 32 * j : t * P + 32 * j + 32], lhsT=grad[b, u][:, j, t:K:4], rhs=pick[:], start=True, stop=True
                     )
-            dst = st[b]["means"][:, u * K : (u + 1) * K].rearrange("p (i j t) -> p i j t", j=4, t=4)
+            dst = means_of(b, u).rearrange("p (i j t) -> p i j t", j=4, t=4)
             src = acc[:].rearrange("p (t j i) -> p i j t", t=4, j=4)
             engine_copy(on)(out=dst, in_=src)
             release("mean")
@@ -180,7 +184,7 @@ def tile_two_layer_gradcam_s3_kernel(
                     nc.tensor.transpose(turned[:, (2 * n + v) * P : (2 * n + v + 1) * P], words[:, v * P : (v + 1) * P], ident[:])
             for n, (b, u) in enumerate(units):
                 engine_copy(on)(
-                    out=st[b]["means"][:, u * K : (u + 1) * K].bitcast(F32).rearrange("p (m v) -> p m v", v=2),
+                    out=means_of(b, u).bitcast(F32).rearrange("p (m v) -> p m v", v=2),
                     in_=turned[:, 2 * n * P : 2 * (n + 1) * P].rearrange("p (v m) -> p m v", v=2),
                 )
             release("sums")
@@ -189,7 +193,7 @@ def tile_two_layer_gradcam_s3_kernel(
             nc.vector.quantize_mx(
                 out=st[b]["codes"][:, u0 * P : (u0 + n) * P].bitcast(FP8X4),
                 scales=st[b]["scales"][:, u0 * P : (u0 + n) * P],
-                in_=st[b]["means"][:, u0 * K : (u0 + n) * K],
+                in_=means_of(b, u0, n),
             )
 
         def stage1(b, *units, halves=range(GS)):
@@ -269,90 +273,82 @@ def tile_two_layer_gradcam_s3_kernel(
                 engine_copy(engine)(out=staged[b, n // 4][:, (n % 4) * K : (n % 4 + 1) * K], in_=acc[:])
                 release("strip")
 
-        def store(b, n0, count):
-            nc.sync.dma_start(
+        def store(b, n0, count, queue=nc.sync):
+            queue.dma_start(
                 out=out_view[b][:, n0 * K : (n0 + count) * K], in_=staged[b, n0 // 4][:, (n0 % 4) * K : (n0 % 4 + count) * K]
             )
 
-        spent = ["deep_raw", "g0a", "deep_grouped", "gd01", "g1b", "gd23", "g2a", "g2b"]
+        spent = ["deep_raw", "g0a", "deep_grouped", "gd01", "g0b", "g1a", "g1b", "gd23"]
         load_deep()
         load_scales(es, early_scales)
-        load_ge(0, 1, 1, "g01")
-        load_ew(0, 2)
-        load_ge(0, 2, 1, "g0a")
+        load_ge(0, 1, 2, "g0a")
         load_gd(0, 2, "gd01")
-        load_ge(0, 3, 1, "g03")
-        load_ew(2, 2)
-        load_ge(0, 4, 1, "g04")
-        load_ge(1, 1, 1, "g11")
-        load_ge(1, 2, 1, "g12")
+        load_ew(0, 4)
+        load_ge(0, 3, 2, "g0b")
+        load_ge(1, 1, 2, "g1a")
         load_ge(1, 3, 2, "g1b")
         load_gd(2, 2, "gd23")
         load_ge(2, 1, 2, "g2a")
         load_ge(2, 3, 2, "g2b")
-        load_uw(0, 2)
+        load_uw(0, 4)
         constants()
-        begin(0, "means0")
-        begin(1, "means1")
+        begin(0, "means0", "dm0")
+        begin(1, "means1", "dm1")
         group_deep(0, "V")
         group_deep(1, "V")
         mean(0, 1, "A")
-        quantize_means(0, 1)
+        mean(0, 2, "S")
         quantize_deep(0)
         quantize_deep(1)
-        stage1(0, 1)
-        mean(0, 2, "S")
-        mean(0, 0, "S")
-        quantize_means(0, 2)
+        quantize_means(0, 1, 2)
+        mean(0, 0, "V")
         mean(1, 0, "S")
         quantize_means(0, 0)
-        mean(0, 3, "S")
         quantize_means(1, 0)
-        stage1(0, 2)
         stage1(0, 0)
+        stage1(0, 1, 2)
+        mean(0, 3, "V")
+        mean(0, 4, "S")
         quantize_means(0, 3)
         stage1(1, 0)
-        mean(0, 4, "S")
+        quantize_means(0, 4)
         stage1(0, 3)
         mean(1, 1, "S")
-        quantize_means(0, 4)
         stage1(0, 4)
-        quantize_means(1, 1)
         relu(0, "SV")
         mean(1, 2, "S")
-        stage1(1, 1)
+        quantize_means(1, 1)
+        mean(1, 3, "V")
+        turn_cam(0, "S")
         quantize_means(1, 2)
-        turn_cam(0, "V")
-        mean(1, 3, "S")
+        stage1(1, 1)
+        mean(1, 4, "V")
+        quantize_means(1, 3)
         stage1(1, 2)
         quantize_cam(0)
-        mean(1, 4, "S")
-        quantize_means(1, 3)
-        begin(2, "means2")
-        begin(3, "means0")
-        stage1(1, 3)
         quantize_means(1, 4)
-        mean(2, 0, "S")
-        stage1(1, 4)
-        relu(1, "SV")
-        quantize_means(2, 0)
-        mean(3, 0, "S")
-        mean(2, 1, "S")
-        quantize_means(3, 0)
+        begin(2, "means0", "dm0")
+        begin(3, "means1", "held")
+        mean(2, 0, "V")
         load_us(0, 4)
-        turn_cam(1, "S", "held")
-        mean(2, 2, "S")
-        quantize_means(2, 1)
-        stage1(2, 0)
-        quantize_cam(1)
+        mean(3, 0, "S")
+        stage1(1, 3, 4)
+        quantize_means(2, 0)
+        quantize_means(3, 0)
         load_ge(3, 1, 2, "held")
-        load_uw(2, 2)
         load_ge(3, 3, 2, "g3b")
         load_uw(4, 4)
+        relu(1, "SV")
+        mean(2, 1, "V")
+        mean(2, 2, "S")
+        turn_cam(1, "S")
+        quantize_means(2, 1)
+        stage1(2, 0)
         stage1(3, 0)
         quantize_means(2, 2)
-        mean(2, 3, "S")
-        mean(2, 4, "V")
+        quantize_cam(1)
+        mean(2, 3, "V")
+        mean(2, 4, "S")
         stage1(2, 1, 2)
         quantize_means(2, 3)
         quantize_means(2, 4)
@@ -361,20 +357,18 @@ def tile_two_layer_gradcam_s3_kernel(
         load_us(4, 4)
         relu(2, "SV")
         stage2(0, (0, 1), "SS")
-        store(0, 0, 2)
         add_pairs(3, 1)
         turn_cam(2, "S")
         add_pairs(3, 2)
         stage2(1, (0, 1), "SS")
-        store(1, 0, 2)
         quantize_cam(2)
         add_halves(3, 1)
         add_halves(3, 2)
         stage2(0, (2, 3), "SS")
-        store(0, 2, 2)
+        store(0, 0, 4)
         add_pairs(3, 3)
         stage2(1, (2, 3), "SS")
-        store(1, 2, 2)
+        store(1, 0, 4)
         stage2(2, (0, 1), "SS")
         turn_sums("S", (3, 1), (3, 2))
         stage2(2, (2, 3), "SS")
@@ -384,10 +378,9 @@ def tile_two_layer_gradcam_s3_kernel(
         add_halves(3, 3)
         add_halves(3, 4)
         stage2(0, (4, 5), "SS")
-        store(0, 4, 2)
         stage1(3, 1, 2)
         stage2(0, (6, 7), "SS")
-        store(0, 6, 2)
+        store(0, 4, 4)
         turn_sums("V", (3, 3), (3, 4))
         stage2(1, (4, 5), "SS")
         store(1, 4, 2)
@@ -410,7 +403,5 @@ def tile_two_layer_gradcam_s3_kernel(
         store(3, 2, 2)
         stage2(3, (4, 5), "SV")
         store(3, 4, 2)
-        stage2(3, (6,), "S")
-        store(3, 6, 1)
-        stage2(3, (7,), "V")
-        store(3, 7, 1)
+        stage2(3, (6, 7), "SV")
+        store(3, 6, 2)

@@ -281,127 +281,115 @@ def tile_two_layer_gradcam_s3_kernel(
         spent = ["deep_raw", "g0a", "deep_grouped", "gd01", "g0b", "g1a", "g1b", "gd23"]
         load_deep()
         load_scales(es, early_scales)
-        load_ge(0, 1, 2, "g0a")
         load_gd(0, 2, "gd01")
-        load_ew(0, 4)
+        load_ge(0, 1, 2, "g0a")
         load_ge(0, 3, 2, "g0b")
+        load_ew(0, 4)
         load_ge(1, 1, 2, "g1a")
         load_ge(1, 3, 2, "g1b")
         load_gd(2, 2, "gd23")
         load_ge(2, 1, 2, "g2a")
         load_ge(2, 3, 2, "g2b")
-        load_uw(0, 4)
+        load_ge(3, 1, 2, "g3a")
+        load_uw(0, 2)
+        load_uw(2, 2)
         constants()
         begin(0, "means0", "dm0")
         begin(1, "means1", "dm1")
         group_deep(0, "V")
         group_deep(1, "V")
-        mean(0, 1, "A")
-        mean(0, 2, "S")
+        mean(0, 0, "A")
+        mean(1, 0, "S")
         quantize_deep(0)
         quantize_deep(1)
-        quantize_means(0, 1, 2)
-        mean(0, 0, "V")
-        mean(1, 0, "S")
         quantize_means(0, 0)
         quantize_means(1, 0)
+        mean(0, 1, "V")
+        mean(0, 2, "S")
         stage1(0, 0)
-        stage1(0, 1, 2)
+        quantize_means(0, 1, 2)
         mean(0, 3, "V")
         mean(0, 4, "S")
         quantize_means(0, 3)
         stage1(1, 0)
         quantize_means(0, 4)
-        stage1(0, 3)
-        mean(1, 1, "S")
-        stage1(0, 4)
+        stage1(0, 1, 2)
+        stage1(0, 3, 4)
         relu(0, "SV")
+        mean(1, 1, "V")
         mean(1, 2, "S")
-        quantize_means(1, 1)
-        mean(1, 3, "V")
         turn_cam(0, "S")
+        quantize_means(1, 1)
         quantize_means(1, 2)
-        stage1(1, 1)
-        mean(1, 4, "V")
-        quantize_means(1, 3)
-        stage1(1, 2)
+        mean(1, 3, "V")
+        mean(1, 4, "S")
         quantize_cam(0)
+        quantize_means(1, 3)
+        stage1(1, 1, 2)
         quantize_means(1, 4)
-        begin(2, "means0", "dm0")
-        begin(3, "means1", "held")
-        mean(2, 0, "V")
-        load_us(0, 4)
-        mean(3, 0, "S")
         stage1(1, 3, 4)
-        quantize_means(2, 0)
-        quantize_means(3, 0)
-        load_ge(3, 1, 2, "held")
-        load_ge(3, 3, 2, "g3b")
-        load_uw(4, 4)
+        begin(2, "means0", "dm0")
+        begin(3, "means1", "dm1")
         relu(1, "SV")
+        mean(2, 0, "V")
+        mean(3, 0, "S")
+        quantize_means(2, 0)
         mean(2, 1, "V")
+        quantize_means(3, 0)
+        load_us(0, 4)
         mean(2, 2, "S")
-        turn_cam(1, "S")
+        turn_cam(1, "S", "held")
         quantize_means(2, 1)
-        stage1(2, 0)
-        stage1(3, 0)
         quantize_means(2, 2)
-        quantize_cam(1)
         mean(2, 3, "V")
         mean(2, 4, "S")
-        stage1(2, 1, 2)
+        quantize_cam(1)
+        load_ge(3, 3, 2, "held")
+        load_uw(4, 4)
         quantize_means(2, 3)
+        stage1(2, 0)
+        stage1(3, 0)
         quantize_means(2, 4)
-        stage1(2, 3)
-        stage1(2, 4)
-        load_us(4, 4)
-        relu(2, "SV")
-        stage2(0, (0, 1), "SS")
+        stage1(2, 1, 2, 3, 4)
         add_pairs(3, 1)
-        turn_cam(2, "S")
         add_pairs(3, 2)
-        stage2(1, (0, 1), "SS")
-        quantize_cam(2)
+        relu(2, "SS")
+        load_us(4, 4)
         add_halves(3, 1)
         add_halves(3, 2)
+        stage2(0, (0, 1), "SS")
+        turn_cam(2, "S")
+        stage2(1, (0, 1), "VS")
+        quantize_cam(2)
+        add_pairs(3, 3)
+        add_pairs(3, 4)
         stage2(0, (2, 3), "SS")
         store(0, 0, 4)
-        add_pairs(3, 3)
         stage2(1, (2, 3), "SS")
         store(1, 0, 4)
-        stage2(2, (0, 1), "SS")
-        turn_sums("S", (3, 1), (3, 2))
-        stage2(2, (2, 3), "SS")
-        store(2, 0, 4)
-        quantize_means(3, 1, 2)
-        add_pairs(3, 4)
         add_halves(3, 3)
         add_halves(3, 4)
-        stage2(0, (4, 5), "SS")
-        stage1(3, 1, 2)
-        stage2(0, (6, 7), "SS")
-        store(0, 4, 4)
-        turn_sums("V", (3, 3), (3, 4))
-        stage2(1, (4, 5), "SS")
-        store(1, 4, 2)
+        stage2(2, (0, 1, 2, 3), "SSSS")
+        store(2, 0, 4)
+        stage2(0, (4, 5), "SV")
+        store(0, 4, 2)
+        turn_sums("V", (3, 1), (3, 2))
+        turn_sums("S", (3, 3), (3, 4))
+        stage2(0, (6,), "S")
+        quantize_means(3, 1, 2)
         quantize_means(3, 3, 2)
-        stage2(1, (6,), "V")
-        stage1(3, 3, 4)
+        stage2(0, (7,), "V")
+        store(0, 6, 2)
+        stage2(1, (4, 5), "SV")
+        store(1, 4, 2)
+        stage1(3, 1, 2, 3, 4)
         relu(3, "SV")
-        stage2(1, (7,), "S")
+        stage2(1, (6, 7), "SV")
         store(1, 6, 2)
-        stage2(2, (4,), "V")
-        turn_cam(3, "V")
-        stage2(2, (5, 6), "SS")
+        turn_cam(3, "S")
+        stage2(2, (4, 5), "VS")
         store(2, 4, 2)
         quantize_cam(3)
-        stage2(2, (7,), "V")
-        store(2, 6, 2)
-        stage2(3, (0, 1), "SV")
-        store(3, 0, 2)
-        stage2(3, (2, 3), "SV")
-        store(3, 2, 2)
-        stage2(3, (4, 5), "SV")
-        store(3, 4, 2)
-        stage2(3, (6, 7), "SV")
-        store(3, 6, 2)
+        for b, n in [(2, 6), (3, 0), (3, 2), (3, 4), (3, 6)]:
+            stage2(b, (n, n + 1), "VS")
+            store(b, n, 2)

@@ -278,12 +278,11 @@ def tile_two_layer_gradcam_s3_kernel(
                 out=out_view[b][:, n0 * K : (n0 + count) * K], in_=staged[b, n0 // 4][:, (n0 % 4) * K : (n0 % 4 + count) * K]
             )
 
-        spent = ["deep_raw", "g0a", "deep_grouped", "gd01", "g0b", "g1a", "g1b", "gd23"]
+        spent = ["deep_raw", "g0", "deep_grouped", "gd01", "g2b", "g1a", "g1b", "gd23"]
         load_deep()
         load_scales(es, early_scales)
         load_gd(0, 2, "gd01")
-        load_ge(0, 1, 2, "g0a")
-        load_ge(0, 3, 2, "g0b")
+        load_ge(0, 1, 4, "g0")
         load_ew(0, 4)
         load_ge(1, 1, 2, "g1a")
         load_ge(1, 3, 2, "g1b")
@@ -304,16 +303,17 @@ def tile_two_layer_gradcam_s3_kernel(
         quantize_deep(1)
         quantize_means(0, 0)
         quantize_means(1, 0)
+        stage1(0, 0)
+        stage1(1, 0)
         mean(0, 1, "V")
         mean(0, 2, "S")
-        stage1(0, 0)
-        quantize_means(0, 1, 2)
+        quantize_means(0, 1)
         mean(0, 3, "V")
+        quantize_means(0, 2)
         mean(0, 4, "S")
         quantize_means(0, 3)
-        stage1(1, 0)
-        quantize_means(0, 4)
         stage1(0, 1, 2)
+        quantize_means(0, 4)
         stage1(0, 3, 4)
         relu(0, "SV")
         mean(1, 1, "V")
@@ -372,14 +372,13 @@ def tile_two_layer_gradcam_s3_kernel(
         stage2(2, (0, 1, 2, 3), "SSSS")
         store(2, 0, 4)
         stage2(0, (4, 5), "SV")
-        store(0, 4, 2)
         turn_sums("V", (3, 1), (3, 2))
         turn_sums("S", (3, 3), (3, 4))
         stage2(0, (6,), "S")
         quantize_means(3, 1, 2)
         quantize_means(3, 3, 2)
         stage2(0, (7,), "V")
-        store(0, 6, 2)
+        store(0, 4, 4)
         stage2(1, (4, 5), "SV")
         store(1, 4, 2)
         stage1(3, 1, 2, 3, 4)
@@ -387,9 +386,11 @@ def tile_two_layer_gradcam_s3_kernel(
         stage2(1, (6, 7), "SV")
         store(1, 6, 2)
         turn_cam(3, "S")
-        stage2(2, (4, 5), "VS")
-        store(2, 4, 2)
+        stage2(2, (4,), "V")
+        store(2, 4, 1)
+        stage2(2, (5,), "S")
+        store(2, 5, 1)
         quantize_cam(3)
-        for b, n in [(2, 6), (3, 0), (3, 2), (3, 4), (3, 6)]:
-            stage2(b, (n, n + 1), "VS")
-            store(b, n, 2)
+        for b, n in [(2, 6), (2, 7)] + [(3, n) for n in range(8)]:
+            stage2(b, (n,), "VS"[n % 2])
+            store(b, n, 1)

@@ -123,7 +123,7 @@ def tile_two_layer_gradcam_s3_kernel(
                 in_=deep_grouped[:, h * K * 4 : (h + 1) * K * 4],
             )
 
-        st, pairs, summed, staged = {}, {}, {}, {}
+        st, pairs, summed, sums, staged = {}, {}, {}, {}, {}
 
         free = list(range(8))
         held = {}
@@ -171,23 +171,26 @@ def tile_two_layer_gradcam_s3_kernel(
 
         def add_halves(b, u):
             summed[b, u] = work.tile([P, K], BF16, name="summed", bufs=4, align_bytes=256)
-            halves = [pairs[b, u][:, h, :].rearrange("q (p v e) -> q v p e", v=2, e=2) for h in range(2)]
+            halves = [pairs[b, u][:, h, :].rearrange("q (p v e) -> q p v e", v=2, e=2) for h in range(2)]
             nc.vector.tensor_tensor(
-                out=summed[b, u][:].rearrange("q (v p e) -> q v p e", v=2, e=2), in0=halves[0], in1=halves[1], op=ADD
+                out=summed[b, u][:].rearrange("q (v p e) -> q p v e", v=2, e=2), in0=halves[0], in1=halves[1], op=ADD
             )
 
-        def turn_sums(on, *units):
-            turned = bank("sums")
+        def turn_sums(*units):
+            turned = sums[units] = bank(units)
             for n, (b, u) in enumerate(units):
                 words = summed[b, u][:].bitcast(F32)
                 for v in range(2):
                     nc.tensor.transpose(turned[:, (2 * n + v) * P : (2 * n + v + 1) * P], words[:, v * P : (v + 1) * P], ident[:])
+
+        def empty_sums(on, *units):
+            turned = sums[units]
             for n, (b, u) in enumerate(units):
                 engine_copy(on)(
                     out=means_of(b, u).bitcast(F32).rearrange("p (m v) -> p m v", v=2),
                     in_=turned[:, 2 * n * P : 2 * (n + 1) * P].rearrange("p (v m) -> p m v", v=2),
                 )
-            release("sums")
+            release(units)
 
         def quantize_means(b, u0, n=1):
             nc.vector.quantize_mx(
@@ -278,7 +281,7 @@ def tile_two_layer_gradcam_s3_kernel(
                 out=out_view[b][:, n0 * K : (n0 + count) * K], in_=staged[b, n0 // 4][:, (n0 % 4) * K : (n0 % 4 + count) * K]
             )
 
-        spent = ["deep_raw", "g0", "deep_grouped", "gd01", "g2b", "g1a", "g1b", "gd23"]
+        spent = ["deep_raw", "g0", "deep_grouped", "gd01", "g2b", "g1a", "g1b", "g2a"]
         load_deep()
         load_scales(es, early_scales)
         load_gd(0, 2, "gd01")
@@ -286,12 +289,12 @@ def tile_two_layer_gradcam_s3_kernel(
         load_ew(0, 4)
         load_ge(1, 1, 2, "g1a")
         load_ge(1, 3, 2, "g1b")
-        load_gd(2, 2, "gd23")
+        load_gd(2, 1, "gd2")
         load_ge(2, 1, 2, "g2a")
         load_ge(2, 3, 2, "g2b")
-        load_ge(3, 1, 2, "g3a")
+        load_gd(3, 1, "gd3")
         load_uw(0, 2)
-        load_uw(2, 2)
+        load_ge(3, 1, 2, "g3a")
         constants()
         begin(0, "means0", "dm0")
         begin(1, "means1", "dm1")
@@ -332,35 +335,36 @@ def tile_two_layer_gradcam_s3_kernel(
         begin(3, "means1", "dm1")
         relu(1, "SV")
         mean(2, 0, "V")
-        mean(3, 0, "S")
+        mean(2, 1, "S")
         quantize_means(2, 0)
-        mean(2, 1, "V")
-        quantize_means(3, 0)
-        load_us(0, 4)
-        mean(2, 2, "S")
-        turn_cam(1, "S", "held")
+        mean(2, 2, "V")
         quantize_means(2, 1)
+        load_us(0, 4)
+        turn_cam(1, "S", "held")
         quantize_means(2, 2)
         mean(2, 3, "V")
         mean(2, 4, "S")
         quantize_cam(1)
-        load_ge(3, 3, 2, "held")
-        load_uw(4, 4)
+        load_uw(2, 2, "held")
+        load_ge(3, 3, 2, "g3b")
+        load_uw(4, 2)
+        load_uw(6, 2)
         quantize_means(2, 3)
+        mean(3, 0, "V")
         stage1(2, 0)
-        stage1(3, 0)
         quantize_means(2, 4)
         stage1(2, 1, 2, 3, 4)
+        quantize_means(3, 0)
+        relu(2, "SV")
         add_pairs(3, 1)
         add_pairs(3, 2)
-        relu(2, "SS")
-        load_us(4, 4)
-        add_halves(3, 1)
-        add_halves(3, 2)
         stage2(0, (0, 1), "SS")
+        load_us(4, 4)
         turn_cam(2, "S")
-        stage2(1, (0, 1), "VS")
+        add_halves(3, 1)
         quantize_cam(2)
+        add_halves(3, 2)
+        stage2(1, (0, 1), "SS")
         add_pairs(3, 3)
         add_pairs(3, 4)
         stage2(0, (2, 3), "SS")
@@ -371,17 +375,20 @@ def tile_two_layer_gradcam_s3_kernel(
         add_halves(3, 4)
         stage2(2, (0, 1, 2, 3), "SSSS")
         store(2, 0, 4)
-        stage2(0, (4, 5), "SV")
-        turn_sums("V", (3, 1), (3, 2))
-        turn_sums("S", (3, 3), (3, 4))
-        stage2(0, (6,), "S")
-        quantize_means(3, 1, 2)
-        quantize_means(3, 3, 2)
-        stage2(0, (7,), "V")
-        store(0, 4, 4)
-        stage2(1, (4, 5), "SV")
+        stage2(0, (4, 5), "SS")
+        stage2(1, (4, 5), "SS")
         store(1, 4, 2)
-        stage1(3, 1, 2, 3, 4)
+        turn_sums((3, 1), (3, 2))
+        turn_sums((3, 3), (3, 4))
+        empty_sums("V", (3, 1), (3, 2))
+        quantize_means(3, 1, 2)
+        empty_sums("V", (3, 3), (3, 4))
+        quantize_means(3, 3, 2)
+        stage2(0, (6, 7), "SS")
+        store(0, 4, 4)
+        stage1(3, 0)
+        stage1(3, 1, 2)
+        stage1(3, 3, 4)
         relu(3, "SV")
         stage2(1, (6, 7), "SV")
         store(1, 6, 2)

@@ -23,9 +23,10 @@ BANDS = M // P
 GE = CE // K
 GS = S // K
 UNITS = 1 + GE
+STRIPS = NPIX // K
 MOVING, MOVING_SCALE, STILL, STILL_SCALE = 0, 128, 64, 192
 FLOPS = 2 * M * (CD + CE) * S + 2 * M * S * NPIX
-ON_VECTOR = {(3, 1), (3, 2), (3, 3), (3, 4)}
+ON_VECTOR = {(3, 0), (3, 1), (3, 2), (3, 3), (3, 4)}
 
 
 def tile_two_layer_gradcam_s3_kernel(
@@ -54,24 +55,25 @@ def tile_two_layer_gradcam_s3_kernel(
         deep_grouped = keep.tile([P, S * 4], BF16, name="deep_grouped", align_bytes=256)
         deep_codes = placed(keep, [P, S], U32, 4, MOVING, name="deep_codes")
         deep_scales = placed(keep, [P, S], U8, 1, MOVING_SCALE, name="deep_scales")
-        es = placed(keep, [P, GE, S], U8, 1, MOVING_SCALE, name="es")
-        ew, uw, us, grad = {}, {}, {}, {}
+        early_plane = placed(keep, [P, GE, S], U8, 1, MOVING_SCALE, name="early_plane")
+        early_codes = placed(keep, [P, GE, 2 * S], U8, 1, MOVING, name="early_codes")
+        up_codes, up_plane, grad = {}, {}, {}
 
         ctx.enter_context(tc.manual_schedule())
 
-        def load_gd(b0, n, slot):
-            piece = keep.tile([P, 4, n * CD], BF16, name=slot, align_bytes=256)
-            for b in range(b0, b0 + n):
+        def load_gd(b0, count, slot):
+            piece = keep.tile([P, 4, count * CD], BF16, name=slot, align_bytes=256)
+            for b in range(b0, b0 + count):
                 grad[b, 0] = piece[:, :, (b - b0) * CD : (b - b0 + 1) * CD]
             view = gd_by_target if (b0, 0) in ON_VECTOR else gd_stacked
-            nc.sync.dma_start(out=piece[:], in_=view[:, :, b0 * CD : (b0 + n) * CD])
+            nc.sync.dma_start(out=piece[:], in_=view[:, :, b0 * CD : (b0 + count) * CD])
 
-        def load_ge(b, u0, n, slot):
-            piece = keep.tile([P, 4, n * K], BF16, name=slot, align_bytes=256)
-            for u in range(u0, u0 + n):
+        def load_ge(b, u0, slot):
+            piece = keep.tile([P, 4, 2 * K], BF16, name=slot, align_bytes=256)
+            for u in (u0, u0 + 1):
                 grad[b, u] = piece[:, :, (u - u0) * K : (u - u0 + 1) * K]
             view = ge_by_target if (b, u0) in ON_VECTOR else ge_stacked
-            nc.sync.dma_start(out=piece[:], in_=view[b][:, :, (u0 - 1) * K : (u0 - 1 + n) * K])
+            nc.sync.dma_start(out=piece[:], in_=view[b][:, :, (u0 - 1) * K : (u0 + 1) * K])
 
         def load_scales(plane, rows):
             for r in range(4):
@@ -80,25 +82,22 @@ def tile_two_layer_gradcam_s3_kernel(
                     in_=rows.rearrange("g (q r) n -> r q g n", r=4)[r].bitcast(I32),
                 )
 
-        def load_ew(g0, count):
-            piece = placed(keep, [P, count, 2 * S], U8, 1, MOVING, name="ew%d" % g0)
-            for g in range(g0, g0 + count):
-                ew[g] = piece[:, g - g0, :]
-            nc.sync.dma_start(out=piece[:].bitcast(I32), in_=early_words[g0 : g0 + count].rearrange("g p n -> p g n").bitcast(I32))
+        def load_early():
+            nc.sync.dma_start(out=early_codes.bitcast(I32), in_=early_words.rearrange("g p n -> p g n").bitcast(I32))
 
-        def load_uw(n0, count, slot=None):
-            piece = placed(keep, [P, GS, count * 2 * K], U8, 1, MOVING, name=slot or "uw%d" % n0)
+        def load_up(n0, count):
+            piece = placed(keep, [P, GS, count * 2 * K], U8, 1, MOVING, name="up_codes%d" % n0)
             for n in range(n0, n0 + count):
-                uw[n] = piece[:, :, (n - n0) * 2 * K : (n - n0 + 1) * 2 * K]
+                up_codes[n] = piece[:, :, (n - n0) * 2 * K : (n - n0 + 1) * 2 * K]
             nc.sync.dma_start(
-                out=piece[:].bitcast(I32),
+                out=piece.bitcast(I32),
                 in_=up_words[:, :, n0 * 2 * K : (n0 + count) * 2 * K].rearrange("g p n -> p g n").bitcast(I32),
             )
 
-        def load_us(n0, count):
-            plane = placed(keep, [P, GS, count * K], U8, 1, MOVING_SCALE, name="us%d" % n0)
+        def load_up_scales(n0, count):
+            plane = placed(keep, [P, GS, count * K], U8, 1, MOVING_SCALE, name="up_plane%d" % n0)
             for n in range(n0, n0 + count):
-                us[n] = plane[:, :, (n - n0) * K : (n - n0 + 1) * K]
+                up_plane[n] = plane[:, :, (n - n0) * K : (n - n0 + 1) * K]
             load_scales(plane, up_scales[:, :, n0 * K : (n0 + count) * K])
 
         def load_deep():
@@ -123,7 +122,7 @@ def tile_two_layer_gradcam_s3_kernel(
                 in_=deep_grouped[:, h * K * 4 : (h + 1) * K * 4],
             )
 
-        st, pairs, summed, sums, staged = {}, {}, {}, {}, {}
+        band, pairs, summed, turned_sums, staged = {}, {}, {}, {}, {}
 
         free = list(range(8))
         held = {}
@@ -142,121 +141,115 @@ def tile_two_layer_gradcam_s3_kernel(
                 rows = slice(32 * l, 32 * l + 32)
                 nc.vector.tensor_copy(out=pick[rows, :], in_=ident[rows, rows])
 
-        def begin(b, slot, deep_slot):
-            st[b] = {
-                "means": keep.tile([P, GE * K], BF16, name=slot, align_bytes=256),
-                "deep_means": keep.tile([P, K], BF16, name=deep_slot, align_bytes=256),
-                "codes": placed(work, [P, UNITS * P], U32, 4, STILL, name="codes", bufs=4),
-                "scales": placed(work, [P, UNITS * P], U8, 1, STILL_SCALE, name="scales", bufs=4),
+        def begin(b):
+            band[b] = {
+                "early_sums": work.tile([P, GE * K], BF16, name="early_sums", align_bytes=256),
+                "deep_sums": work.tile([P, K], BF16, name="deep_sums", bufs=BANDS, align_bytes=256),
+                "codes": placed(work, [P, UNITS * P], U32, 4, STILL, name="codes", bufs=BANDS),
+                "scales": placed(work, [P, UNITS * P], U8, 1, STILL_SCALE, name="scales", bufs=BANDS),
+                "passes": [0] * GS,
             }
 
-        def means_of(b, u0, n=1):
-            return st[b]["deep_means"][:] if u0 == 0 else st[b]["means"][:, (u0 - 1) * K : (u0 - 1 + n) * K]
+        def sums_of(b, u0, count=1):
+            return band[b]["deep_sums"][:] if u0 == 0 else band[b]["early_sums"][:, (u0 - 1) * K : (u0 - 1 + count) * K]
 
-        def mean(b, u, on):
-            acc = bank("mean")
+        def sum_on_tensor(b, u, on):
+            acc = bank("sum")
             for t in range(4):
                 for j in range(4):
                     nc.tensor.matmul(
                         acc[:, t * P + 32 * j : t * P + 32 * j + 32], lhsT=grad[b, u][:, j, t:K:4], rhs=pick[:], start=True, stop=True
                     )
-            dst = means_of(b, u).rearrange("p (i j t) -> p i j t", j=4, t=4)
-            src = acc[:].rearrange("p (t j i) -> p i j t", t=4, j=4)
-            engine_copy(on)(out=dst, in_=src)
-            release("mean")
+            engine_copy(on)(
+                out=sums_of(b, u).rearrange("p (i j t) -> p i j t", j=4, t=4),
+                in_=acc[:].rearrange("p (t j i) -> p i j t", t=4, j=4),
+            )
+            release("sum")
 
         def add_pairs(b, u):
             pairs[b, u] = work.tile([P, 2, K], F32, name="pairs", align_bytes=256)
             nc.vector.tensor_tensor(out=pairs[b, u][:], in0=grad[b, u][:, 0:2, :], in1=grad[b, u][:, 2:4, :], op=ADD)
 
         def add_halves(b, u):
-            summed[b, u] = work.tile([P, K], BF16, name="summed", bufs=4, align_bytes=256)
+            summed[b, u] = work.tile([P, K], BF16, name="summed", bufs=UNITS, align_bytes=256)
             halves = [pairs[b, u][:, h, :].rearrange("q (p v e) -> q p v e", v=2, e=2) for h in range(2)]
             nc.vector.tensor_tensor(
                 out=summed[b, u][:].rearrange("q (v p e) -> q p v e", v=2, e=2), in0=halves[0], in1=halves[1], op=ADD
             )
 
-        def turn_sums(*units):
-            turned = sums[units] = bank(units)
-            for n, (b, u) in enumerate(units):
+        def turn_sums(b, *units):
+            turned = turned_sums[b, units] = bank((b, units))
+            for n, u in enumerate(units):
                 words = summed[b, u][:].bitcast(F32)
                 for v in range(2):
                     nc.tensor.transpose(turned[:, (2 * n + v) * P : (2 * n + v + 1) * P], words[:, v * P : (v + 1) * P], ident[:])
 
-        def empty_sums(on, *units):
-            turned = sums[units]
-            for n, (b, u) in enumerate(units):
-                engine_copy(on)(
-                    out=means_of(b, u).bitcast(F32).rearrange("p (m v) -> p m v", v=2),
-                    in_=turned[:, 2 * n * P : 2 * (n + 1) * P].rearrange("p (v m) -> p m v", v=2),
+        def empty_sums(b, *units):
+            turned = turned_sums[b, units]
+            for n, u in enumerate(units):
+                nc.vector.tensor_copy(
+                    out=sums_of(b, u).bitcast(F32).rearrange("p (q v) -> p q v", v=2),
+                    in_=turned[:, 2 * n * P : 2 * (n + 1) * P].rearrange("p (v q) -> p q v", v=2),
                 )
-            release(units)
+            release((b, units))
 
-        def quantize_means(b, u0, n=1):
+        def quantize_sums(b, u0, count=1):
             nc.vector.quantize_mx(
-                out=st[b]["codes"][:, u0 * P : (u0 + n) * P].bitcast(FP8X4),
-                scales=st[b]["scales"][:, u0 * P : (u0 + n) * P],
-                in_=means_of(b, u0, n),
+                out=band[b]["codes"][:, u0 * P : (u0 + count) * P].bitcast(FP8X4),
+                scales=band[b]["scales"][:, u0 * P : (u0 + count) * P],
+                in_=sums_of(b, u0, count),
             )
 
-        def stage1(b, *units, halves=range(GS)):
-            for h in halves:
-                done = st[b].setdefault(("done", h), [])
-                if not done:
-                    st[b]["z", h] = bank((b, h))
-                for u in units:
-                    cols = slice(u * P, (u + 1) * P)
+        def stage1(b, *units):
+            for u in units:
+                for h in range(GS):
+                    done = band[b]["passes"][h]
+                    if done == 0:
+                        band[b]["z", h] = bank((b, h))
                     if u == 0:
                         rhs = deep_codes[:, h * K : (h + 1) * K].bitcast(FP8X4)
                         rhs_scale = deep_scales[:, h * K : (h + 1) * K]
                     else:
-                        rhs = ew[u - 1][:, h * 2 * K : (h + 1) * 2 * K].bitcast(FP4X4)
-                        rhs_scale = es[:, u - 1, h * K : (h + 1) * K]
+                        rhs = early_codes[:, u - 1, h * 2 * K : (h + 1) * 2 * K].bitcast(FP4X4)
+                        rhs_scale = early_plane[:, u - 1, h * K : (h + 1) * K]
                     nc.tensor.matmul_mx(
-                        out=st[b]["z", h][:],
-                        lhsT=st[b]["codes"][:, cols].bitcast(FP8X4),
-                        lhsT_scale=st[b]["scales"][:, cols],
+                        out=band[b]["z", h][:],
+                        lhsT=band[b]["codes"][:, u * P : (u + 1) * P].bitcast(FP8X4),
+                        lhsT_scale=band[b]["scales"][:, u * P : (u + 1) * P],
                         rhs=rhs,
                         rhs_scale=rhs_scale,
-                        start=(len(done) == 0),
-                        stop=(len(done) == UNITS - 1),
+                        start=(done == 0),
+                        stop=(done == UNITS - 1),
                     )
-                    done.append(u)
+                    band[b]["passes"][h] = done + 1
 
-        def relu(b, on, slot=None):
-            if slot:
-                st[b]["cam"] = keep.tile([P, S], BF16, name=slot, align_bytes=256)
-            else:
-                st[b]["cam"] = work.tile([P, S], BF16, name="cam", align_bytes=256)
+        def relu(b, on):
+            band[b]["cam"] = work.tile([P, S], BF16, name="cam", align_bytes=256)
             for h in range(GS):
-                dst = st[b]["cam"][:, h * K : (h + 1) * K].rearrange("m (v q e) -> m v q e", v=2, e=2)
-                src = st[b]["z", h][:].rearrange("m (q v e) -> m v q e", v=2, e=2)
+                dst = band[b]["cam"][:, h * K : (h + 1) * K].rearrange("q (v p e) -> q v p e", v=2, e=2)
+                src = band[b]["z", h][:].rearrange("q (p v e) -> q v p e", v=2, e=2)
                 if on[h] == "S":
                     nc.scalar.activation(out=dst, in_=src, func=RELU, scale=1.0 / L)
                 else:
                     nc.vector.tensor_scalar(out=dst, in0=src, scalar1=0.0, scalar2=1.0 / L, op0=MAX, op1=MULT)
                 release((b, h))
 
-        def turn_cam(b, on, slot=None):
+        def turn_cam(b, on):
             turned = bank("cam")
-            words = st[b]["cam"][:].bitcast(F32)
+            words = band[b]["cam"][:].bitcast(F32)
             for i in range(4):
                 nc.tensor.transpose(turned[:, i * P : (i + 1) * P], words[:, i * P : (i + 1) * P], ident[:])
-            if slot:
-                grouped = keep.tile([P, S], BF16, name=slot, align_bytes=256)
-            else:
-                grouped = work.tile([P, S], BF16, name="grouped", align_bytes=256)
+            band[b]["grouped"] = work.tile([P, S], BF16, name="grouped", align_bytes=256)
             engine_copy(on)(
-                out=grouped[:].bitcast(F32).rearrange("p (g m v) -> p g m v", g=GS, v=2),
-                in_=turned[:].rearrange("p (g v m) -> p g m v", g=GS, v=2),
+                out=band[b]["grouped"][:].bitcast(F32).rearrange("p (g q v) -> p g q v", g=GS, v=2),
+                in_=turned[:].rearrange("p (g v q) -> p g q v", g=GS, v=2),
             )
             release("cam")
-            st[b]["grouped"] = grouped
 
         def quantize_cam(b):
-            st[b]["cam_codes"] = placed(work, [P, GS * P], U32, 4, STILL, name="cam_codes", bufs=4)
-            st[b]["cam_scales"] = placed(work, [P, GS * P], U8, 1, STILL_SCALE, name="cam_scales", bufs=4)
-            nc.vector.quantize_mx(out=st[b]["cam_codes"][:].bitcast(FP8X4), scales=st[b]["cam_scales"][:], in_=st[b]["grouped"][:])
+            band[b]["cam_codes"] = placed(work, [P, GS * P], U32, 4, STILL, name="cam_codes", bufs=BANDS)
+            band[b]["cam_scales"] = placed(work, [P, GS * P], U8, 1, STILL_SCALE, name="cam_scales", bufs=BANDS)
+            nc.vector.quantize_mx(out=band[b]["cam_codes"].bitcast(FP8X4), scales=band[b]["cam_scales"], in_=band[b]["grouped"][:])
 
         def stage2(b, strips, on):
             for n, engine in zip(strips, on):
@@ -264,10 +257,10 @@ def tile_two_layer_gradcam_s3_kernel(
                 for g in range(GS):
                     nc.tensor.matmul_mx(
                         out=acc[:],
-                        lhsT=st[b]["cam_codes"][:, g * P : (g + 1) * P].bitcast(FP8X4),
-                        lhsT_scale=st[b]["cam_scales"][:, g * P : (g + 1) * P],
-                        rhs=uw[n][:, g, :].bitcast(FP4X4),
-                        rhs_scale=us[n][:, g, :],
+                        lhsT=band[b]["cam_codes"][:, g * P : (g + 1) * P].bitcast(FP8X4),
+                        lhsT_scale=band[b]["cam_scales"][:, g * P : (g + 1) * P],
+                        rhs=up_codes[n][:, g, :].bitcast(FP4X4),
+                        rhs_scale=up_plane[n][:, g, :],
                         start=(g == 0),
                         stop=(g == GS - 1),
                     )
@@ -276,119 +269,107 @@ def tile_two_layer_gradcam_s3_kernel(
                 engine_copy(engine)(out=staged[b, n // 4][:, (n % 4) * K : (n % 4 + 1) * K], in_=acc[:])
                 release("strip")
 
-        def store(b, n0, count, queue=nc.sync):
-            queue.dma_start(
+        def store(b, n0, count):
+            nc.sync.dma_start(
                 out=out_view[b][:, n0 * K : (n0 + count) * K], in_=staged[b, n0 // 4][:, (n0 % 4) * K : (n0 % 4 + count) * K]
             )
 
-        spent = ["deep_raw", "g0", "deep_grouped", "gd01", "g2b", "g1a", "g1b", "g2a"]
+        spent = ["g0a", "g0b", "g1a", "g1b", "deep_raw", "deep_grouped", "gd01", "g2a"]
+        load_ge(0, 1, "g0a")
+        load_scales(early_plane, early_scales)
+        load_ge(0, 3, "g0b")
+        load_early()
+        load_ge(1, 1, "g1a")
+        load_ge(1, 3, "g1b")
         load_deep()
-        load_scales(es, early_scales)
         load_gd(0, 2, "gd01")
-        load_ge(0, 1, 4, "g0")
-        load_ew(0, 4)
-        load_ge(1, 1, 2, "g1a")
-        load_ge(1, 3, 2, "g1b")
         load_gd(2, 1, "gd2")
-        load_ge(2, 1, 2, "g2a")
-        load_ge(2, 3, 2, "g2b")
+        load_ge(2, 1, "g2a")
+        load_ge(2, 3, "g2b")
         load_gd(3, 1, "gd3")
-        load_uw(0, 2)
-        load_ge(3, 1, 2, "g3a")
+        load_up(0, 4)
+        load_ge(3, 1, "g3a")
         constants()
-        begin(0, "means0", "dm0")
-        begin(1, "means1", "dm1")
+        for b in (0, 1):
+            begin(b)
+            sum_on_tensor(b, 1, "A")
+            sum_on_tensor(b, 2, "V")
+            quantize_sums(b, 1)
+            sum_on_tensor(b, 3, "S")
+            quantize_sums(b, 2)
+            sum_on_tensor(b, 4, "V")
+            quantize_sums(b, 3)
+            quantize_sums(b, 4)
+            stage1(b, 1, 2, 3, 4)
+        group_deep(1, "S")
         group_deep(0, "V")
-        group_deep(1, "V")
-        mean(0, 0, "A")
-        mean(1, 0, "S")
+        begin(2)
+        sum_on_tensor(0, 0, "S")
         quantize_deep(0)
         quantize_deep(1)
-        quantize_means(0, 0)
-        quantize_means(1, 0)
+        sum_on_tensor(1, 0, "S")
+        quantize_sums(0, 0)
+        quantize_sums(1, 0)
+        sum_on_tensor(2, 0, "V")
         stage1(0, 0)
         stage1(1, 0)
-        mean(0, 1, "V")
-        mean(0, 2, "S")
-        quantize_means(0, 1)
-        mean(0, 3, "V")
-        quantize_means(0, 2)
-        mean(0, 4, "S")
-        quantize_means(0, 3)
-        stage1(0, 1, 2)
-        quantize_means(0, 4)
-        stage1(0, 3, 4)
+        quantize_sums(2, 0)
         relu(0, "SV")
-        mean(1, 1, "V")
-        mean(1, 2, "S")
-        turn_cam(0, "S")
-        quantize_means(1, 1)
-        quantize_means(1, 2)
-        mean(1, 3, "V")
-        mean(1, 4, "S")
-        quantize_cam(0)
-        quantize_means(1, 3)
-        stage1(1, 1, 2)
-        quantize_means(1, 4)
-        stage1(1, 3, 4)
-        begin(2, "means0", "dm0")
-        begin(3, "means1", "dm1")
         relu(1, "SV")
-        mean(2, 0, "V")
-        mean(2, 1, "S")
-        quantize_means(2, 0)
-        mean(2, 2, "V")
-        quantize_means(2, 1)
-        load_us(0, 4)
-        turn_cam(1, "S", "held")
-        quantize_means(2, 2)
-        mean(2, 3, "V")
-        mean(2, 4, "S")
+        load_up_scales(0, 4)
+        sum_on_tensor(2, 1, "S")
+        sum_on_tensor(2, 2, "V")
+        turn_cam(0, "S")
+        quantize_sums(2, 1)
+        turn_cam(1, "V")
+        quantize_sums(2, 2)
+        sum_on_tensor(2, 3, "S")
+        quantize_cam(0)
+        sum_on_tensor(2, 4, "V")
+        load_ge(3, 3, "g2b")
+        load_up(4, 4)
+        begin(3)
+        quantize_sums(2, 3)
         quantize_cam(1)
-        load_uw(2, 2, "held")
-        load_ge(3, 3, 2, "g3b")
-        load_uw(4, 2)
-        load_uw(6, 2)
-        quantize_means(2, 3)
-        mean(3, 0, "V")
-        stage1(2, 0)
-        quantize_means(2, 4)
-        stage1(2, 1, 2, 3, 4)
-        quantize_means(3, 0)
-        relu(2, "SV")
-        add_pairs(3, 1)
-        add_pairs(3, 2)
+        quantize_sums(2, 4)
+        stage1(2, 0, 1, 2, 3, 4)
+        add_pairs(3, 0)
+        relu(2, "SS")
+        add_halves(3, 0)
         stage2(0, (0, 1), "SS")
-        load_us(4, 4)
+        turn_sums(3, 0)
         turn_cam(2, "S")
-        add_halves(3, 1)
+        empty_sums(3, 0)
+        add_pairs(3, 1)
+        quantize_sums(3, 0)
+        load_up_scales(4, 4)
         quantize_cam(2)
-        add_halves(3, 2)
-        stage2(1, (0, 1), "SS")
-        add_pairs(3, 3)
-        add_pairs(3, 4)
+        add_pairs(3, 2)
         stage2(0, (2, 3), "SS")
         store(0, 0, 4)
-        stage2(1, (2, 3), "SS")
+        add_halves(3, 1)
+        add_halves(3, 2)
+        add_pairs(3, 3)
+        add_pairs(3, 4)
+        stage2(1, (0, 1, 2, 3), "SSSS")
         store(1, 0, 4)
         add_halves(3, 3)
         add_halves(3, 4)
         stage2(2, (0, 1, 2, 3), "SSSS")
         store(2, 0, 4)
-        stage2(0, (4, 5), "SS")
+        stage1(3, 0)
+        stage2(0, (4, 5, 6), "SSS")
+        turn_sums(3, 1, 2)
+        turn_sums(3, 3, 4)
+        empty_sums(3, 1, 2)
+        quantize_sums(3, 1, 2)
+        empty_sums(3, 3, 4)
+        quantize_sums(3, 3, 2)
+        stage2(0, (7,), "S")
+        store(0, 4, 4)
         stage2(1, (4, 5), "SS")
         store(1, 4, 2)
-        turn_sums((3, 1), (3, 2))
-        turn_sums((3, 3), (3, 4))
-        empty_sums("V", (3, 1), (3, 2))
-        quantize_means(3, 1, 2)
-        empty_sums("V", (3, 3), (3, 4))
-        quantize_means(3, 3, 2)
-        stage2(0, (6, 7), "SS")
-        store(0, 4, 4)
-        stage1(3, 0)
-        stage1(3, 1, 2)
-        stage1(3, 3, 4)
+        stage1(3, 1, 2, 3, 4)
         relu(3, "SV")
         stage2(1, (6, 7), "SV")
         store(1, 6, 2)
@@ -398,6 +379,6 @@ def tile_two_layer_gradcam_s3_kernel(
         stage2(2, (5,), "S")
         store(2, 5, 1)
         quantize_cam(3)
-        for b, n in [(2, 6), (2, 7)] + [(3, n) for n in range(8)]:
+        for b, n in [(2, 6), (2, 7)] + [(3, n) for n in range(STRIPS)]:
             stage2(b, (n,), "VS"[n % 2])
             store(b, n, 1)

@@ -51,6 +51,7 @@ def tile_two_layer_gradcam_s3_kernel(
 
         ident = keep.tile([P, P], F32, align_bytes=256)
         pick = keep.tile([P, 32], BF16, align_bytes=256)
+        pick_pair = keep.tile([P, 2, 64], BF16, align_bytes=256)
         deep_raw = keep.tile([P, 4, S], BF16, name="deep_raw", align_bytes=256)
         deep_grouped = keep.tile([P, S * 4], BF16, name="deep_grouped", align_bytes=256)
         deep_codes = placed(keep, [P, S], U32, 4, MOVING, name="deep_codes")
@@ -127,19 +128,22 @@ def tile_two_layer_gradcam_s3_kernel(
         free = list(range(8))
         held = {}
 
-        def bank(owner):
+        def bank(owner, dtype=F32):
             held[owner] = free[0]
             free.remove(held[owner])
-            return psum.tile([P, K], F32, name="bank%d" % held[owner])
+            return psum.tile([P, K], dtype, name="bank%d" % held[owner])
 
         def release(owner):
             free.append(held[owner])
 
         def constants():
             make_identity(nc, ident[:])
+            nc.vector.memset(pick_pair[:], 0.0)
             for l in range(L):
                 rows = slice(32 * l, 32 * l + 32)
                 nc.vector.tensor_copy(out=pick[rows, :], in_=ident[rows, rows])
+            for e in range(2):
+                nc.vector.tensor_copy(out=pick_pair[:, e, e:64:2], in_=pick[:])
 
         def begin(b):
             band[b] = {
@@ -154,16 +158,28 @@ def tile_two_layer_gradcam_s3_kernel(
             return band[b]["deep_sums"][:] if u0 == 0 else band[b]["early_sums"][:, (u0 - 1) * K : (u0 - 1 + count) * K]
 
         def sum_on_tensor(b, u, on):
-            acc = bank("sum")
-            for t in range(4):
+            acc = bank("sum", BF16)
+            for v in range(2):
                 for j in range(4):
-                    nc.tensor.matmul(
-                        acc[:, t * P + 32 * j : t * P + 32 * j + 32], lhsT=grad[b, u][:, j, t:K:4], rhs=pick[:], start=True, stop=True
+                    for e in range(2):
+                        nc.tensor.matmul(
+                            acc[:, v * 256 + 64 * j : v * 256 + 64 * j + 64],
+                            lhsT=grad[b, u][:, j, 2 * v + e : K : 4],
+                            rhs=pick_pair[:, e, :],
+                            start=(e == 0),
+                            stop=(e == 1),
+                        )
+            if on == "A":
+                for v in range(2):
+                    copy_by_activation(
+                        out=sums_of(b, u).rearrange("p (i j v e) -> p v i j e", j=4, v=2, e=2)[:, v],
+                        in_=acc[:].rearrange("p (v j i e) -> p v i j e", v=2, j=4, e=2)[:, v],
                     )
-            engine_copy(on)(
-                out=sums_of(b, u).rearrange("p (i j t) -> p i j t", j=4, t=4),
-                in_=acc[:].rearrange("p (t j i) -> p i j t", t=4, j=4),
-            )
+            else:
+                engine_copy(on)(
+                    out=sums_of(b, u).bitcast(F32).rearrange("p (i j v) -> p i j v", j=4, v=2),
+                    in_=acc[:].bitcast(F32).rearrange("p (v j i) -> p i j v", v=2, j=4),
+                )
             release("sum")
 
         def add_pairs(b, u):
@@ -292,7 +308,7 @@ def tile_two_layer_gradcam_s3_kernel(
         constants()
         for b in (0, 1):
             begin(b)
-            sum_on_tensor(b, 1, "A")
+            sum_on_tensor(b, 1, "AS"[b])
             sum_on_tensor(b, 2, "V")
             quantize_sums(b, 1)
             sum_on_tensor(b, 3, "S")

@@ -268,22 +268,24 @@ def tile_two_layer_gradcam_s3_kernel(
             nc.vector.quantize_mx(out=band[b]["cam_codes"].bitcast(FP8X4), scales=band[b]["cam_scales"], in_=band[b]["grouped"][:])
 
         def stage2(b, strips, on):
-            for n, engine in zip(strips, on):
-                acc = bank("strip")
+            for at in range(0, len(strips), 2):
+                acc = {n: bank(("strip", n)) for n in strips[at : at + 2]}
                 for g in range(GS):
-                    nc.tensor.matmul_mx(
-                        out=acc[:],
-                        lhsT=band[b]["cam_codes"][:, g * P : (g + 1) * P].bitcast(FP8X4),
-                        lhsT_scale=band[b]["cam_scales"][:, g * P : (g + 1) * P],
-                        rhs=up_codes[n][:, g, :].bitcast(FP4X4),
-                        rhs_scale=up_plane[n][:, g, :],
-                        start=(g == 0),
-                        stop=(g == GS - 1),
-                    )
-                if n % 4 == 0:
-                    staged[b, n // 4] = keep.tile([P, 4 * K], F32, name=spent.pop(0), align_bytes=256)
-                engine_copy(engine)(out=staged[b, n // 4][:, (n % 4) * K : (n % 4 + 1) * K], in_=acc[:])
-                release("strip")
+                    for n in acc:
+                        nc.tensor.matmul_mx(
+                            out=acc[n][:],
+                            lhsT=band[b]["cam_codes"][:, g * P : (g + 1) * P].bitcast(FP8X4),
+                            lhsT_scale=band[b]["cam_scales"][:, g * P : (g + 1) * P],
+                            rhs=up_codes[n][:, g, :].bitcast(FP4X4),
+                            rhs_scale=up_plane[n][:, g, :],
+                            start=(g == 0),
+                            stop=(g == GS - 1),
+                        )
+                for n, engine in zip(acc, on[at : at + 2]):
+                    if n % 4 == 0:
+                        staged[b, n // 4] = keep.tile([P, 4 * K], F32, name=spent.pop(0), align_bytes=256)
+                    engine_copy(engine)(out=staged[b, n // 4][:, (n % 4) * K : (n % 4 + 1) * K], in_=acc[n][:])
+                    release(("strip", n))
 
         def store(b, n0, count):
             nc.sync.dma_start(

from contextlib import ExitStack

import concourse.mybir as mybir
from concourse.masks import make_identity

F32 = mybir.dt.float32
BF16 = mybir.dt.bfloat16
I32 = mybir.dt.int32
U32 = mybir.dt.uint32
U8 = mybir.dt.uint8
FP8X4 = mybir.dt.float8_e4m3fn_x4
FP4X4 = mybir.dt.float4_e2m1fn_x4
RELU = mybir.ActivationFunctionType.Relu
COPY = mybir.ActivationFunctionType.Copy
ADD = mybir.AluOpType.add
MAX = mybir.AluOpType.max
MULT = mybir.AluOpType.mult

P = 128
L, M, CD, CE, S, NPIX = 4, 512, 512, 2048, 1024, 4096
K = 512
BANDS = M // P
GE = CE // K
GS = S // K
UNITS = 1 + GE
STRIPS = NPIX // K
MOVING, MOVING_SCALE, STILL, STILL_SCALE = 0, 128, 64, 192
FLOPS = 2 * M * (CD + CE) * S + 2 * M * S * NPIX
ON_VECTOR = {(3, 0), (3, 1), (3, 2), (3, 3), (3, 4)}


def tile_two_layer_gradcam_s3_kernel(
    tc, grad_deep, grad_early, deep, early_words, early_scales, up_words, up_scales, out
):
    nc = tc.nc
    gd_stacked = grad_deep.rearrange("l (i j b) k -> (l i) j (b k)", j=4, b=BANDS)
    ge_stacked = grad_early.rearrange("l (i j b) k -> b (l i) j k", j=4, b=BANDS)
    gd_by_target = grad_deep.rearrange("l (q b) k -> q l (b k)", b=BANDS)
    ge_by_target = grad_early.rearrange("l (q b) k -> b q l k", b=BANDS)
    out_view = out.rearrange("(q b) n -> b q n", b=BANDS)

    with ExitStack() as ctx:
        keep = ctx.enter_context(tc.tile_pool(name="keep", bufs=1))
        work = ctx.enter_context(tc.tile_pool(name="work", bufs=2))
        psum = ctx.enter_context(tc.psum_pool(name="psum", bufs=1))

        def placed(pool, shape, dtype, size, at, **kw):
            count = shape[1] if len(shape) == 2 else shape[1] * shape[2]
            flat = pool.tile([P, at // size + count], dtype, align_bytes=256, **kw)[:, at // size :]
            return flat if len(shape) == 2 else flat.rearrange("p (g n) -> p g n", g=shape[1])

        ident = keep.tile([P, P], F32, align_bytes=256)
        pick = keep.tile([P, 32], BF16, align_bytes=256)
        pick_pair = keep.tile([P, 2, 64], BF16, align_bytes=256)
        deep_raw = keep.tile([P, 4, S], BF16, name="deep_raw", align_bytes=256)
        deep_grouped = keep.tile([P, S * 4], BF16, name="deep_grouped", align_bytes=256)
        deep_codes = placed(keep, [P, S], U32, 4, MOVING, name="deep_codes")
        deep_scales = placed(keep, [P, S], U8, 1, MOVING_SCALE, name="deep_scales")
        early_plane = placed(keep, [P, GE, S], U8, 1, MOVING_SCALE, name="early_plane")
        early_codes = placed(keep, [P, GE, 2 * S], U8, 1, MOVING, name="early_codes")
        up_codes, up_plane, grad = {}, {}, {}

        ctx.enter_context(tc.manual_schedule())

        def load_gd(b0, count, slot):
            piece = keep.tile([P, 4, count * CD], BF16, name=slot, align_bytes=256)
            for b in range(b0, b0 + count):
                grad[b, 0] = piece[:, :, (b - b0) * CD : (b - b0 + 1) * CD]
            view = gd_by_target if (b0, 0) in ON_VECTOR else gd_stacked
            nc.sync.dma_start(out=piece[:], in_=view[:, :, b0 * CD : (b0 + count) * CD])

        def load_ge(b, u0, slot):
            piece = keep.tile([P, 4, 2 * K], BF16, name=slot, align_bytes=256)
            for u in (u0, u0 + 1):
                grad[b, u] = piece[:, :, (u - u0) * K : (u - u0 + 1) * K]
            view = ge_by_target if (b, u0) in ON_VECTOR else ge_stacked
            nc.sync.dma_start(out=piece[:], in_=view[b][:, :, (u0 - 1) * K : (u0 + 1) * K])

        def load_scales(plane, rows):
            for r in range(4):
                nc.scalar.dma_start(
                    out=plane[r:P:32, :, :].bitcast(I32),
                    in_=rows.rearrange("g (q r) n -> r q g n", r=4)[r].bitcast(I32),
                )

        def load_early():
            nc.sync.dma_start(out=early_codes.bitcast(I32), in_=early_words.rearrange("g p n -> p g n").bitcast(I32))

        def load_up(n0, count):
            piece = placed(keep, [P, GS, count * 2 * K], U8, 1, MOVING, name="up_codes%d" % n0)
            for n in range(n0, n0 + count):
                up_codes[n] = piece[:, :, (n - n0) * 2 * K : (n - n0 + 1) * 2 * K]
            nc.sync.dma_start(
                out=piece.bitcast(I32),
                in_=up_words[:, :, n0 * 2 * K : (n0 + count) * 2 * K].rearrange("g p n -> p g n").bitcast(I32),
            )

        def load_up_scales(n0, count):
            plane = placed(keep, [P, GS, count * K], U8, 1, MOVING_SCALE, name="up_plane%d" % n0)
            for n in range(n0, n0 + count):
                up_plane[n] = plane[:, :, (n - n0) * K : (n - n0 + 1) * K]
            load_scales(plane, up_scales[:, :, n0 * K : (n0 + count) * K])

        def load_deep():
            nc.sync.dma_start(out=deep_raw[:], in_=deep.rearrange("(p j) w -> p j w", j=4))

        def copy_by_activation(out, in_):
            nc.scalar.activation(out=out, in_=in_, func=COPY)

        def engine_copy(on):
            return {"V": nc.vector.tensor_copy, "S": nc.scalar.copy, "A": copy_by_activation}[on]

        def group_deep(h, on):
            engine_copy(on)(
                out=deep_grouped[:, h * K * 4 : (h + 1) * K * 4].rearrange("p (w j) -> p w j", j=4),
                in_=deep_raw[:, :, h * K : (h + 1) * K].rearrange("p j w -> p w j"),
            )

        def quantize_deep(h):
            nc.vector.quantize_mx(
                out=deep_codes[:, h * K : (h + 1) * K].bitcast(FP8X4),
                scales=deep_scales[:, h * K : (h + 1) * K],
                in_=deep_grouped[:, h * K * 4 : (h + 1) * K * 4],
            )

        band, pairs, summed, turned_sums, staged = {}, {}, {}, {}, {}

        free = list(range(8))
        held = {}

        def bank(owner, dtype=F32):
            held[owner] = free[0]
            free.remove(held[owner])
            return psum.tile([P, K], dtype, name="bank%d" % held[owner])

        def release(owner):
            free.append(held[owner])

        def constants():
            make_identity(nc, ident[:])
            nc.vector.memset(pick_pair[:], 0.0)
            for l in range(L):
                rows = slice(32 * l, 32 * l + 32)
                nc.vector.tensor_copy(out=pick[rows, :], in_=ident[rows, rows])
            for e in range(2):
                nc.vector.tensor_copy(out=pick_pair[:, e, e:64:2], in_=pick[:])

        def begin(b):
            band[b] = {
                "early_sums": work.tile([P, GE * K], BF16, name="early_sums", align_bytes=256),
                "deep_sums": work.tile([P, K], BF16, name="deep_sums", bufs=BANDS, align_bytes=256),
                "codes": placed(work, [P, UNITS * P], U32, 4, STILL, name="codes", bufs=BANDS),
                "scales": placed(work, [P, UNITS * P], U8, 1, STILL_SCALE, name="scales", bufs=BANDS),
                "passes": [0] * GS,
            }

        def sums_of(b, u0, count=1):
            return band[b]["deep_sums"][:] if u0 == 0 else band[b]["early_sums"][:, (u0 - 1) * K : (u0 - 1 + count) * K]

        def sum_on_tensor(b, u, on):
            acc = bank("sum", BF16)
            for v in range(2):
                for j in range(4):
                    for e in range(2):
                        nc.tensor.matmul(
                            acc[:, v * 256 + 64 * j : v * 256 + 64 * j + 64],
                            lhsT=grad[b, u][:, j, 2 * v + e : K : 4],
                            rhs=pick_pair[:, e, :],
                            start=(e == 0),
                            stop=(e == 1),
                        )
            if on == "A":
                for v in range(2):
                    copy_by_activation(
                        out=sums_of(b, u).rearrange("p (i j v e) -> p v i j e", j=4, v=2, e=2)[:, v],
                        in_=acc[:].rearrange("p (v j i e) -> p v i j e", v=2, j=4, e=2)[:, v],
                    )
            else:
                engine_copy(on)(
                    out=sums_of(b, u).bitcast(F32).rearrange("p (i j v) -> p i j v", j=4, v=2),
                    in_=acc[:].bitcast(F32).rearrange("p (v j i) -> p i j v", v=2, j=4),
                )
            release("sum")

        def add_pairs(b, u):
            pairs[b, u] = work.tile([P, 2, K], F32, name="pairs", align_bytes=256)
            nc.vector.tensor_tensor(out=pairs[b, u][:], in0=grad[b, u][:, 0:2, :], in1=grad[b, u][:, 2:4, :], op=ADD)

        def add_halves(b, u):
            summed[b, u] = work.tile([P, K], BF16, name="summed", bufs=UNITS, align_bytes=256)
            halves = [pairs[b, u][:, h, :].rearrange("q (p v e) -> q p v e", v=2, e=2) for h in range(2)]
            nc.vector.tensor_tensor(
                out=summed[b, u][:].rearrange("q (v p e) -> q p v e", v=2, e=2), in0=halves[0], in1=halves[1], op=ADD
            )

        def turn_sums(b, *units):
            turned = turned_sums[b, units] = bank((b, units))
            for n, u in enumerate(units):
                words = summed[b, u][:].bitcast(F32)
                for v in range(2):
                    nc.tensor.transpose(turned[:, (2 * n + v) * P : (2 * n + v + 1) * P], words[:, v * P : (v + 1) * P], ident[:])

        def empty_sums(b, *units):
            turned = turned_sums[b, units]
            for n, u in enumerate(units):
                nc.vector.tensor_copy(
                    out=sums_of(b, u).bitcast(F32).rearrange("p (q v) -> p q v", v=2),
                    in_=turned[:, 2 * n * P : 2 * (n + 1) * P].rearrange("p (v q) -> p q v", v=2),
                )
            release((b, units))

        def quantize_sums(b, u0, count=1):
            nc.vector.quantize_mx(
                out=band[b]["codes"][:, u0 * P : (u0 + count) * P].bitcast(FP8X4),
                scales=band[b]["scales"][:, u0 * P : (u0 + count) * P],
                in_=sums_of(b, u0, count),
            )

        def stage1(b, *units):
            for u in units:
                for h in range(GS):
                    done = band[b]["passes"][h]
                    if done == 0:
                        band[b]["z", h] = bank((b, h))
                    if u == 0:
                        rhs = deep_codes[:, h * K : (h + 1) * K].bitcast(FP8X4)
                        rhs_scale = deep_scales[:, h * K : (h + 1) * K]
                    else:
                        rhs = early_codes[:, u - 1, h * 2 * K : (h + 1) * 2 * K].bitcast(FP4X4)
                        rhs_scale = early_plane[:, u - 1, h * K : (h + 1) * K]
                    nc.tensor.matmul_mx(
                        out=band[b]["z", h][:],
                        lhsT=band[b]["codes"][:, u * P : (u + 1) * P].bitcast(FP8X4),
                        lhsT_scale=band[b]["scales"][:, u * P : (u + 1) * P],
                        rhs=rhs,
                        rhs_scale=rhs_scale,
                        start=(done == 0),
                        stop=(done == UNITS - 1),
                    )
                    band[b]["passes"][h] = done + 1

        def relu(b, on):
            band[b]["cam"] = work.tile([P, S], BF16, name="cam", align_bytes=256)
            for h in range(GS):
                dst = band[b]["cam"][:, h * K : (h + 1) * K].rearrange("q (v p e) -> q v p e", v=2, e=2)
                src = band[b]["z", h][:].rearrange("q (p v e) -> q v p e", v=2, e=2)
                if on[h] == "S":
                    nc.scalar.activation(out=dst, in_=src, func=RELU, scale=1.0 / L)
                else:
                    nc.vector.tensor_scalar(out=dst, in0=src, scalar1=0.0, scalar2=1.0 / L, op0=MAX, op1=MULT)
                release((b, h))

        def turn_cam(b, on):
            turned = bank("cam")
            words = band[b]["cam"][:].bitcast(F32)
            for i in range(4):
                nc.tensor.transpose(turned[:, i * P : (i + 1) * P], words[:, i * P : (i + 1) * P], ident[:])
            band[b]["grouped"] = work.tile([P, S], BF16, name="grouped", align_bytes=256)
            engine_copy(on)(
                out=band[b]["grouped"][:].bitcast(F32).rearrange("p (g q v) -> p g q v", g=GS, v=2),
                in_=turned[:].rearrange("p (g v q) -> p g q v", g=GS, v=2),
            )
            release("cam")

        def quantize_cam(b):
            band[b]["cam_codes"] = placed(work, [P, GS * P], U32, 4, STILL, name="cam_codes", bufs=BANDS)
            band[b]["cam_scales"] = placed(work, [P, GS * P], U8, 1, STILL_SCALE, name="cam_scales", bufs=BANDS)
            nc.vector.quantize_mx(out=band[b]["cam_codes"].bitcast(FP8X4), scales=band[b]["cam_scales"], in_=band[b]["grouped"][:])

        def stage2(b, strips, on):
            for at in range(0, len(strips), 2):
                acc = {n: bank(("strip", n)) for n in strips[at : at + 2]}
                for g in range(GS):
                    for n in acc:
                        nc.tensor.matmul_mx(
                            out=acc[n][:],
                            lhsT=band[b]["cam_codes"][:, g * P : (g + 1) * P].bitcast(FP8X4),
                            lhsT_scale=band[b]["cam_scales"][:, g * P : (g + 1) * P],
                            rhs=up_codes[n][:, g, :].bitcast(FP4X4),
                            rhs_scale=up_plane[n][:, g, :],
                            start=(g == 0),
                            stop=(g == GS - 1),
                        )
                for n, engine in zip(acc, on[at : at + 2]):
                    if n % 4 == 0:
                        staged[b, n // 4] = keep.tile([P, 4 * K], F32, name=spent.pop(0), align_bytes=256)
                    engine_copy(engine)(out=staged[b, n // 4][:, (n % 4) * K : (n % 4 + 1) * K], in_=acc[n][:])
                    release(("strip", n))

        def store(b, n0, count):
            nc.sync.dma_start(
                out=out_view[b][:, n0 * K : (n0 + count) * K], in_=staged[b, n0 // 4][:, (n0 % 4) * K : (n0 % 4 + count) * K]
            )

        spent = ["g0a", "g0b", "g1a", "g1b", "deep_raw", "deep_grouped", "gd01", "g2a"]
        load_ge(0, 1, "g0a")
        load_scales(early_plane, early_scales)
        load_ge(0, 3, "g0b")
        load_early()
        load_ge(1, 1, "g1a")
        load_ge(1, 3, "g1b")
        load_deep()
        load_gd(0, 2, "gd01")
        load_gd(2, 1, "gd2")
        load_ge(2, 1, "g2a")
        load_ge(2, 3, "g2b")
        load_gd(3, 1, "gd3")
        load_up(0, 4)
        load_ge(3, 1, "g3a")
        constants()
        for b in (0, 1):
            begin(b)
            sum_on_tensor(b, 1, "AS"[b])
            sum_on_tensor(b, 2, "V")
            quantize_sums(b, 1)
            sum_on_tensor(b, 3, "S")
            quantize_sums(b, 2)
            sum_on_tensor(b, 4, "V")
            quantize_sums(b, 3)
            quantize_sums(b, 4)
            stage1(b, 1, 2, 3, 4)
        group_deep(1, "S")
        group_deep(0, "V")
        begin(2)
        sum_on_tensor(0, 0, "S")
        quantize_deep(0)
        quantize_deep(1)
        sum_on_tensor(1, 0, "S")
        quantize_sums(0, 0)
        quantize_sums(1, 0)
        sum_on_tensor(2, 0, "V")
        stage1(0, 0)
        stage1(1, 0)
        quantize_sums(2, 0)
        relu(0, "SV")
        relu(1, "SV")
        load_up_scales(0, 4)
        sum_on_tensor(2, 1, "S")
        sum_on_tensor(2, 2, "V")
        turn_cam(0, "S")
        quantize_sums(2, 1)
        turn_cam(1, "V")
        quantize_sums(2, 2)
        sum_on_tensor(2, 3, "S")
        quantize_cam(0)
        sum_on_tensor(2, 4, "V")
        load_ge(3, 3, "g2b")
        load_up(4, 4)
        begin(3)
        quantize_sums(2, 3)
        quantize_cam(1)
        quantize_sums(2, 4)
        stage1(2, 0, 1, 2, 3, 4)
        add_pairs(3, 0)
        relu(2, "SS")
        add_halves(3, 0)
        stage2(0, (0, 1), "SS")
        turn_sums(3, 0)
        turn_cam(2, "S")
        empty_sums(3, 0)
        add_pairs(3, 1)
        quantize_sums(3, 0)
        load_up_scales(4, 4)
        quantize_cam(2)
        add_pairs(3, 2)
        stage2(0, (2, 3), "SS")
        store(0, 0, 4)
        add_halves(3, 1)
        add_halves(3, 2)
        add_pairs(3, 3)
        add_pairs(3, 4)
        stage2(1, (0, 1, 2, 3), "SSSS")
        store(1, 0, 4)
        add_halves(3, 3)
        add_halves(3, 4)
        stage2(2, (0, 1, 2, 3), "SSSS")
        store(2, 0, 4)
        stage1(3, 0)
        stage2(0, (4, 5, 6), "SSS")
        turn_sums(3, 1, 2)
        turn_sums(3, 3, 4)
        empty_sums(3, 1, 2)
        quantize_sums(3, 1, 2)
        empty_sums(3, 3, 4)
        quantize_sums(3, 3, 2)
        stage2(0, (7,), "S")
        store(0, 4, 4)
        stage2(1, (4, 5), "SS")
        store(1, 4, 2)
        stage1(3, 1, 2, 3, 4)
        relu(3, "SV")
        stage2(1, (6, 7), "SV")
        store(1, 6, 2)
        turn_cam(3, "S")
        stage2(2, (4,), "V")
        store(2, 4, 1)
        stage2(2, (5,), "S")
        store(2, 5, 1)
        quantize_cam(3)
        for b, n in [(2, 6), (2, 7)] + [(3, n) for n in range(STRIPS)]:
            stage2(b, (n,), "VS"[n % 2])
            store(b, n, 1)
